import numpy as np
import ml_dtypes


def mxq(x, axis, fmt="e4m3"):
    dtype, down = {"e4m3": (ml_dtypes.float8_e4m3fn, 7), "e5m2": (ml_dtypes.float8_e5m2, 14)}[fmt]
    v = np.moveaxis(np.asarray(x, np.float32).astype(ml_dtypes.bfloat16).astype(np.float64), axis, -1)
    blocks = v.reshape(v.shape[:-1] + (-1, 32))
    amax = np.abs(blocks).max(-1, keepdims=True)
    byte = np.maximum(np.where(amax > 0, np.frexp(amax)[1] - 1 + 127, 0) - down, 1)
    scale = np.exp2(byte - 127.0)
    codes = (blocks / scale).astype(np.float32).astype(dtype).astype(np.float64)
    return np.moveaxis((codes * scale).reshape(v.shape), -1, axis)


WIDE = False


def mx_kscale(k):
    if not WIDE:
        return np.ones(k)
    levels = np.array([10, -10, 5, -5, 0])
    if k % 512:
        return np.exp2(np.random.permutation(np.resize(levels, k // 32))).repeat(32)
    a = np.empty((k // 512, 16))
    for p in range(k // 512):
        a[p, :8] = np.random.permutation(np.resize(levels, 8))
        for g in range(8):
            far = levels[np.abs(levels - a[p, g]) >= 10]
            a[p, g + 8] = far[np.random.randint(len(far))]
    return np.exp2(a.ravel()).repeat(32)


def f64(x):
    return np.asarray(x).astype(np.float64)


def striped(idx):
    return np.tile(idx.reshape(-1, 16).T, (8, 1)).astype(np.uint16)


def unstriped(offs):
    return offs[:16].T.reshape(-1).astype(np.int64)


E2M1 = np.array([0.0, 0.5, 1.0, 1.5, 2.0, 3.0, 4.0, 6.0, -0.0, -0.5, -1.0, -1.5, -2.0, -3.0, -4.0, -6.0])


def pack_weight(w, fmt):
    k, n = w.shape
    w = f64(np.asarray(w, np.float32).astype(ml_dtypes.bfloat16)).reshape(k // 32, 32, n)
    amax = np.abs(w).max(1)
    if fmt == "e4m3":
        byte = np.frexp(amax)[1] - 1 + 127 - 7
    else:
        mant, ex = np.frexp(amax / 6.0)
        byte = np.where(mant > 0.5, ex, ex - 1) + 127
    byte = np.clip(np.where(amax > 0, byte, 1), 1, 254)
    scaled = (w * np.exp2(127.0 - byte)[:, None, :]).reshape(k, n).astype(np.float32)
    by_word = np.ascontiguousarray(scaled.reshape(k // 512, 128, 4, n).transpose(0, 1, 3, 2))
    if fmt == "e4m3":
        words = by_word.astype(ml_dtypes.float8_e4m3fn).view(np.uint8)
    else:
        c = by_word.astype(ml_dtypes.float4_e2m1fn).view(np.uint8) & 0xF
        words = (c[..., 0::2] | (c[..., 1::2] << 4)).reshape(k // 512, 128, 2 * n)
    return np.ascontiguousarray(words), np.ascontiguousarray(byte.astype(np.uint8).reshape(k // 512, 16, n))


def unpack_weight(words, scales, fmt):
    g, _, n = scales.shape
    words = np.ascontiguousarray(words).reshape(g, 128, n, -1)
    if fmt == "e4m3":
        vals = words.view(ml_dtypes.float8_e4m3fn).astype(np.float64)
    else:
        nib = np.empty((g, 128, n, 4), np.uint8)
        nib[..., 0::2] = words & 0xF
        nib[..., 1::2] = words >> 4
        vals = E2M1[nib]
    vals = vals * np.repeat(np.exp2(scales.astype(np.float64) - 127.0), 8, axis=1)[..., None]
    return vals.transpose(0, 1, 3, 2).reshape(g * 512, n)


def gelu(v):
    return 0.5 * v * (1.0 + np.tanh(np.sqrt(2.0 / np.pi) * (v + 0.044715 * v**3)))


K, T, S, T2, S2, N = 1024, 4096, 1024, 2048, 512, 512

def setup_inputs():
    n = np.random.standard_normal
    s = mx_kscale(K)[:, None]
    u = mx_kscale(S)[:, None]
    tab_words, tab_scales = pack_weight(n((K, T)) * s / np.sqrt(K), "e4m3")
    tab2_words, tab2_scales = pack_weight(n((K, T2)) / s, "e4m3")
    wv_words, wv_scales = pack_weight(1.5 * n((S, N)) / np.sqrt(S) / u, "e2m1")
    return {
        "tab_words": tab_words, "tab_scales": tab_scales,
        "offs": striped(np.random.permutation(T)[:S]),
        "tab2_words": tab2_words, "tab2_scales": tab2_scales,
        "offs2": striped(np.random.permutation(T2)[:S2]),
        "rw": (np.exp(0.3 * n(S)) * u[:, 0]).astype(np.float32),
        "wv_words": wv_words, "wv_scales": wv_scales,
        "wg": (1.5 * n((S, N)) / np.sqrt(S) / u).astype(np.float32),
        "bg": (0.5 * n(N)).astype(np.float32),
    }

def reference(tab_words, tab_scales, offs, tab2_words, tab2_scales, offs2, rw, wv_words, wv_scales, wg, bg):
    v = unpack_weight(tab_words, tab_scales, "e4m3")[:, unstriped(offs)]
    v2 = unpack_weight(tab2_words, tab2_scales, "e4m3")[:, unstriped(offs2)]
    a = v.T @ v2
    h = np.tanh(a) * f64(rw)[:, None]
    hq = mxq(h, 0, "e4m3")
    wv = unpack_weight(wv_words, wv_scales, "e2m1")
    p = wv.T @ hq
    g = mxq(f64(wg), 0, "e4m3").T @ hq
    return p * (1.0 / (1.0 + np.exp(-(g + f64(bg)[:, None]))))

@@ -1,0 +1,215 @@
+from contextlib import ExitStack
+
+import concourse.mybir as mybir
+
+K, T, S, T2, S2, N = 1024, 4096, 1024, 2048, 512, 512
+FLOPS = 2 * K * S * S2 + 4 * S * N * S2
+
+F32 = mybir.dt.float32
+BF16 = mybir.dt.bfloat16
+I32 = mybir.dt.int32
+U32 = mybir.dt.uint32
+U16 = mybir.dt.uint16
+U8 = mybir.dt.uint8
+FP8X4 = mybir.dt.float8_e4m3fn_x4
+FP4X4 = mybir.dt.float4_e2m1fn_x4
+ACT = mybir.ActivationFunctionType
+ALU = mybir.AluOpType
+
+P = 128
+PACK = 4
+PASS = P * PACK
+KP = K // PASS
+SP = S // PASS
+JC = 128
+NJ = S2 // JC
+NT = N // P
+
+
+def tile_list_residue_pocket_gate_kernel(
+    tc, tab_words, tab_scales, offs, tab2_words, tab2_scales, offs2, rw, wv_words, wv_scales, wg, bg, out
+):
+    nc = tc.nc
+    with ExitStack() as ctx:
+        keep = ctx.enter_context(tc.tile_pool(name="keep", bufs=1))
+        ring = ctx.enter_context(tc.tile_pool(name="ring", bufs=4))
+        psum = ctx.enter_context(tc.psum_pool(name="psum", bufs=1))
+
+        idx = keep.tile([P, S // 16], U16, name="idx")
+        idx2 = keep.tile([P, S2 // 16], U16, name="idx2")
+        sc = keep.tile([P, T // 4], I32, name="sc", align_bytes=64)
+        sc2 = keep.tile([P, T2 // 4], I32, name="sc2", align_bytes=64)
+        planes = [keep.tile([P, (S + S2) // 4], I32, name=f"plane{a}", align_bytes=64) for a in range(KP)]
+        wvs = keep.tile([P, SP, N // 4], I32, name="wvs", align_bytes=64)
+        words = [keep.tile([P, T], I32, name=f"words{a}", align_bytes=64) for a in range(KP)]
+        words2 = [keep.tile([P, T2], I32, name=f"words2{a}", align_bytes=64) for a in range(KP)]
+
+        nc.vector.memset(sc[:], 0)
+        nc.vector.memset(sc2[:], 0)
+        nc.vector.memset(wvs[:], 0)
+        for a in range(KP):
+            nc.vector.memset(planes[a][:], 0)
+
+        nc.scalar.dma_start(sc[0:P:4, :], tab_scales.rearrange("a q t -> (a q) t").bitcast(I32))
+        nc.scalar.dma_start(sc2[0:P:4, :], tab2_scales.rearrange("a q t -> (a q) t").bitcast(I32))
+        rw_t = keep.tile([P, SP, PACK], F32, name="rw_t")
+        bg_t = keep.tile([P, NT], F32, name="bg_t")
+        with nc.allow_non_contiguous_dma(reason="small per-partition vectors"):
+            nc.scalar.dma_start(rw_t[:], rw.rearrange("(b p t) -> p b t", b=SP, t=PACK))
+            nc.scalar.dma_start(bg_t[:], bg.rearrange("(c p) -> p c", p=P))
+        nc.sync.dma_start(idx[:], offs)
+        nc.sync.dma_start(idx2[:], offs2)
+        for a in range(KP):
+            if a == 0:
+                nc.sync.dma_start(words2[a][:], tab2_words[a].rearrange("p n t -> p (n t)").bitcast(I32))
+                nc.sync.dma_start(words[a][:], tab_words[a].rearrange("p n t -> p (n t)").bitcast(I32))
+            else:
+                nc.sync.dma_start(words[a][:], tab_words[a].rearrange("p n t -> p (n t)").bitcast(I32))
+                nc.sync.dma_start(words2[a][:], tab2_words[a].rearrange("p n t -> p (n t)").bitcast(I32))
+        wg_raw = [keep.tile([P, PACK, N], F32, name=f"wg_raw{b}") for b in range(SP)]
+        wvw = keep.tile([P, SP, 2 * N], U8, name="wvw", align_bytes=64)
+        nc.sync.dma_start(wg_raw[0][:], wg[0:PASS, :].rearrange("(p t) n -> p t n", t=PACK))
+        nc.sync.dma_start(wvw[:].bitcast(I32), wv_words.rearrange("b p n -> p b n").bitcast(I32))
+        nc.sync.dma_start(wg_raw[1][:], wg[PASS : 2 * PASS, :].rearrange("(p t) n -> p t n", t=PACK))
+
+        for r in range(4):
+            nc.gpsimd.dma_start(wvs[r:P:32, :, :], wv_scales[:, r:16:4, :].rearrange("b q n -> q b n").bitcast(I32))
+        rw_h = keep.tile([P, SP, PACK], F32, name="rw_h")
+        bg_h = keep.tile([P, NT], F32, name="bg_h")
+        nc.scalar.activation(rw_h[:], rw_t[:], ACT.Copy, scale=0.5)
+        nc.scalar.activation(bg_h[:], bg_t[:], ACT.Copy, scale=0.5)
+
+        gs = keep.tile([P, S], U8, name="gs", align_bytes=64)
+        gs2 = keep.tile([P, S2], U8, name="gs2", align_bytes=64)
+        stage = keep.tile([P, S + S2], U8, name="stage", align_bytes=64)
+        nc.vector.tensor_copy(gs[:], sc[:].bitcast(U8).indirect(idx[:]))
+        nc.vector.tensor_copy(gs2[:], sc2[:].bitcast(U8).indirect(idx2[:]))
+        nc.vector.tensor_copy(
+            stage[:, 0:S].rearrange("p (b t m) -> p b t m", b=SP, t=PACK),
+            gs[:].rearrange("p (b m t) -> p b t m", b=SP, t=PACK),
+        )
+        nc.vector.tensor_copy(stage[:, S : S + S2], gs2[:])
+        stage32 = stage[:].bitcast(I32)
+        for a in range(KP):
+            for r in range(4):
+                nc.gpsimd.dma_start(planes[a][4 * a + r : P : 32, :], stage32[64 * a + 4 * r : 64 * a + 64 : 16, :])
+
+        gw = [[keep.tile([P, PASS], U32, name=f"gw{a}{b}", tag=f"gw{a}{b}", align_bytes=64) for b in range(SP)] for a in range(KP)]
+        gw2 = [[keep.tile([P, S2 // 2], U32, name=f"gw2{a}{h}", align_bytes=64) for h in range(2)] for a in range(KP)]
+
+        def gather_tab(a, b):
+            nc.vector.tensor_copy(
+                gw[a][b][:].rearrange("p (t m) -> p m t", t=PACK),
+                words[a][:].bitcast(U32).indirect(idx[:, 32 * b : 32 * (b + 1)]),
+            )
+
+        def gather_tab2(a, h):
+            nc.vector.tensor_copy(gw2[a][h][:], words2[a][:].bitcast(U32).indirect(idx2[:, 16 * h : 16 * (h + 1)]))
+
+        banks = [[psum.tile([P, PACK, JC], F32, name=f"score{b}{c}", tag=f"bank{b * NJ + c}") for c in range(NJ)] for b in range(SP)]
+
+        def score_pass(a, b, c):
+            plane = planes[a][:].bitcast(U8)
+            for t in range(PACK):
+                col = b * PASS + t * P
+                nc.tensor.matmul_mx(
+                    out=banks[b][c][:, t, :],
+                    lhsT=gw[a][b][:, t * P : (t + 1) * P].bitcast(FP8X4),
+                    lhsT_scale=plane[4 * a : P, col : col + P],
+                    rhs=gw2[a][c // 2][:, (c % 2) * JC : (c % 2 + 1) * JC].bitcast(FP8X4),
+                    rhs_scale=plane[4 * a : P, S + c * JC : S + (c + 1) * JC],
+                    start=(a == 0 and t == 0),
+                    stop=(a == KP - 1 and t == PACK - 1),
+                )
+
+        for h in range(2):
+            gather_tab2(0, h)
+        for b in range(SP):
+            gather_tab(0, b)
+        for b in range(SP):
+            for c in range(NJ):
+                score_pass(0, b, c)
+        for b in range(SP):
+            gather_tab(1, b)
+        for h in range(2):
+            gather_tab2(1, h)
+        for b in range(SP):
+            for c in range(NJ):
+                score_pass(1, b, c)
+
+        h16 = [keep.tile([P, S2, PACK], BF16, name=f"h16{b}", align_bytes=64) for b in range(SP)]
+        hq = [keep.tile([P, S2], U32, name=f"hq{b}", align_bytes=64) for b in range(SP)]
+        hs = [keep.tile([P, S2], U8, name=f"hs{b}", align_bytes=64) for b in range(SP)]
+        wg16 = [keep.tile([P, N, PACK], BF16, name=f"wg16{b}", tag=f"gw1{b}", align_bytes=64) for b in range(SP)]
+        wq = [keep.tile([P, N], U32, name=f"wq{b}", align_bytes=64) for b in range(SP)]
+        ws = [keep.tile([P, N], U8, name=f"ws{b}", align_bytes=64) for b in range(SP)]
+
+        def bound(b, c):
+            th = ring.tile([P, JC, PACK], F32, name="th")
+            nc.scalar.activation(th[:], banks[b][c][:].rearrange("p t j -> p j t"), ACT.Tanh)
+            nc.vector.tensor_tensor(
+                h16[b][:, c * JC : (c + 1) * JC, :],
+                th[:],
+                rw_h[:, b, :].unsqueeze(1).to_broadcast([P, JC, PACK]),
+                ALU.mult,
+            )
+
+        def quant(codes, scales, src):
+            nc.vector.quantize_mx(out=codes[:].bitcast(FP8X4), scales=scales[:], in_=src[:].rearrange("p n t -> p (n t)"))
+
+        def wg_views(b):
+            return (
+                wg16[b][:].rearrange("p (c i) t -> p c t i", i=4),
+                wg_raw[b][:].rearrange("p t (c i) -> p c t i", i=4),
+            )
+
+        for c in range(NJ):
+            bound(0, c)
+        nc.vector.tensor_copy(*wg_views(0))
+        quant(hq[0], hs[0], h16[0])
+        bound(1, 0)
+        quant(wq[0], ws[0], wg16[0])
+        for c in range(1, NJ):
+            bound(1, c)
+        nc.scalar.copy(*wg_views(1))
+
+        pb = [psum.tile([P, S2], F32, name=f"feat{n}", tag=f"bank{n}") for n in range(NT)]
+        gb = [psum.tile([P, S2], F32, name=f"gate{n}", tag=f"bank{NT + n}") for n in range(NT)]
+        wvs8 = wvs[:].bitcast(U8)
+
+        def feat_pass(b, n):
+            nc.tensor.matmul_mx(
+                out=pb[n][:],
+                lhsT=wvw[:, b, 2 * P * n : 2 * P * (n + 1)].bitcast(FP4X4),
+                lhsT_scale=wvs8[:, b, P * n : P * (n + 1)],
+                rhs=hq[b][:].bitcast(FP8X4),
+                rhs_scale=hs[b][:],
+                start=(b == 0),
+                stop=(b == SP - 1),
+            )
+
+        def gate_pass(b, n):
+            nc.tensor.matmul_mx(
+                out=gb[n][:],
+                lhsT=wq[b][:, P * n : P * (n + 1)].bitcast(FP8X4),
+                lhsT_scale=ws[b][:, P * n : P * (n + 1)],
+                rhs=hq[b][:].bitcast(FP8X4),
+                rhs_scale=hs[b][:],
+                start=(b == 0),
+                stop=(b == SP - 1),
+            )
+
+        for n in range(NT):
+            feat_pass(0, n)
+        for n in range(NT):
+            gate_pass(0, n)
+        quant(wq[1], ws[1], wg16[1])
+        quant(hq[1], hs[1], h16[1])
+        for n in range(NT):
+            gate_pass(1, n)
+            feat_pass(1, n)
+            th2 = ring.tile([P, S2], F32, name="th2")
+            nc.scalar.activation(th2[:], gb[n][:], ACT.Tanh, bias=bg_h[:, n : n + 1])
+            res = ring.tile([P, S2], F32, name="res")
+            nc.vector.scalar_tensor_tensor(res[:], th2[:], 1.0, pb[n][:], ALU.add, ALU.mult)
+            nc.sync.dma_start(out[n * P : (n + 1) * P, :], res[:])

@@ -32,8 +32,9 @@ def tile_list_residue_pocket_gate_kernel(
     nc = tc.nc
     with ExitStack() as ctx:
         keep = ctx.enter_context(tc.tile_pool(name="keep", bufs=1))
-        ring = ctx.enter_context(tc.tile_pool(name="ring", bufs=4))
+        ring = ctx.enter_context(tc.tile_pool(name="ring", bufs=8))
         psum = ctx.enter_context(tc.psum_pool(name="psum", bufs=1))
+        late = ctx.enter_context(tc.tile_pool(name="late", bufs=1))
 
         idx = keep.tile([P, S // 16], U16, name="idx")
         idx2 = keep.tile([P, S2 // 16], U16, name="idx2")
@@ -41,43 +42,39 @@ def tile_list_residue_pocket_gate_kernel(
         sc2 = keep.tile([P, T2 // 4], I32, name="sc2", align_bytes=64)
         planes = [keep.tile([P, (S + S2) // 4], I32, name=f"plane{a}", align_bytes=64) for a in range(KP)]
         wvs = keep.tile([P, SP, N // 4], I32, name="wvs", align_bytes=64)
-        words = [keep.tile([P, T], I32, name=f"words{a}", align_bytes=64) for a in range(KP)]
-        words2 = [keep.tile([P, T2], I32, name=f"words2{a}", align_bytes=64) for a in range(KP)]
+        words = [
+            late.tile([P, T], I32, name="words0", align_bytes=64, offset=4 * T2 - 64),
+            keep.tile([P, T], I32, name="words1", align_bytes=64),
+        ]
+        words2 = [
+            keep.tile([P, T2], I32, name="words20", align_bytes=64),
+            late.tile([P, T2], I32, name="words21", align_bytes=64, offset=0),
+        ]
 
-        nc.vector.memset(sc[:], 0)
-        nc.vector.memset(sc2[:], 0)
-        nc.vector.memset(wvs[:], 0)
+        nc.vector.memset(sc[0:96, :], 0)
+        nc.gpsimd.memset(sc2[0:96, :], 0)
+        nc.gpsimd.memset(wvs[:], 0)
         for a in range(KP):
-            nc.vector.memset(planes[a][:], 0)
+            nc.gpsimd.memset(planes[a][:], 0)
 
-        nc.scalar.dma_start(sc[0:P:4, :], tab_scales.rearrange("a q t -> (a q) t").bitcast(I32))
-        nc.scalar.dma_start(sc2[0:P:4, :], tab2_scales.rearrange("a q t -> (a q) t").bitcast(I32))
         rw_t = keep.tile([P, SP, PACK], F32, name="rw_t")
-        bg_t = keep.tile([P, NT], F32, name="bg_t")
         with nc.allow_non_contiguous_dma(reason="small per-partition vectors"):
             nc.scalar.dma_start(rw_t[:], rw.rearrange("(b p t) -> p b t", b=SP, t=PACK))
-            nc.scalar.dma_start(bg_t[:], bg.rearrange("(c p) -> p c", p=P))
+        nc.sync.dma_start(sc[96:P, :], tab_scales.rearrange("a q t -> (a q) t").bitcast(I32))
         nc.sync.dma_start(idx[:], offs)
+        nc.sync.dma_start(sc2[96:P, :], tab2_scales.rearrange("a q t -> (a q) t").bitcast(I32))
         nc.sync.dma_start(idx2[:], offs2)
-        for a in range(KP):
-            if a == 0:
-                nc.sync.dma_start(words2[a][:], tab2_words[a].rearrange("p n t -> p (n t)").bitcast(I32))
-                nc.sync.dma_start(words[a][:], tab_words[a].rearrange("p n t -> p (n t)").bitcast(I32))
-            else:
-                nc.sync.dma_start(words[a][:], tab_words[a].rearrange("p n t -> p (n t)").bitcast(I32))
-                nc.sync.dma_start(words2[a][:], tab2_words[a].rearrange("p n t -> p (n t)").bitcast(I32))
-        wg_raw = [keep.tile([P, PACK, N], F32, name=f"wg_raw{b}") for b in range(SP)]
-        wvw = keep.tile([P, SP, 2 * N], U8, name="wvw", align_bytes=64)
-        nc.sync.dma_start(wg_raw[0][:], wg[0:PASS, :].rearrange("(p t) n -> p t n", t=PACK))
-        nc.sync.dma_start(wvw[:].bitcast(I32), wv_words.rearrange("b p n -> p b n").bitcast(I32))
-        nc.sync.dma_start(wg_raw[1][:], wg[PASS : 2 * PASS, :].rearrange("(p t) n -> p t n", t=PACK))
 
+        def load_words(tile, source):
+            nc.sync.dma_start(tile[:], source.rearrange("p n t -> p (n t)").bitcast(I32))
+
+        load_words(words2[0], tab2_words[0])
+        load_words(words[0], tab_words[0])
+        load_words(words[1], tab_words[1])
         for r in range(4):
             nc.gpsimd.dma_start(wvs[r:P:32, :, :], wv_scales[:, r:16:4, :].rearrange("b q n -> q b n").bitcast(I32))
         rw_h = keep.tile([P, SP, PACK], F32, name="rw_h")
-        bg_h = keep.tile([P, NT], F32, name="bg_h")
         nc.scalar.activation(rw_h[:], rw_t[:], ACT.Copy, scale=0.5)
-        nc.scalar.activation(bg_h[:], bg_t[:], ACT.Copy, scale=0.5)
 
         gs = keep.tile([P, S], U8, name="gs", align_bytes=64)
         gs2 = keep.tile([P, S2], U8, name="gs2", align_bytes=64)
@@ -92,7 +89,7 @@ def tile_list_residue_pocket_gate_kernel(
         stage32 = stage[:].bitcast(I32)
         for a in range(KP):
             for r in range(4):
-                nc.gpsimd.dma_start(planes[a][4 * a + r : P : 32, :], stage32[64 * a + 4 * r : 64 * a + 64 : 16, :])
+                nc.scalar.dma_start(planes[a][4 * a + r : P : 32, :], stage32[96 + 16 * a + r : 96 + 16 * a + 16 : 4, :])
 
         gw = [[keep.tile([P, PASS], U32, name=f"gw{a}{b}", tag=f"gw{a}{b}", align_bytes=64) for b in range(SP)] for a in range(KP)]
         gw2 = [[keep.tile([P, S2 // 2], U32, name=f"gw2{a}{h}", align_bytes=64) for h in range(2)] for a in range(KP)]
@@ -106,7 +103,7 @@ def tile_list_residue_pocket_gate_kernel(
         def gather_tab2(a, h):
             nc.vector.tensor_copy(gw2[a][h][:], words2[a][:].bitcast(U32).indirect(idx2[:, 16 * h : 16 * (h + 1)]))
 
-        banks = [[psum.tile([P, PACK, JC], F32, name=f"score{b}{c}", tag=f"bank{b * NJ + c}") for c in range(NJ)] for b in range(SP)]
+        banks = [[psum.tile([P, PACK, JC], F32, name=f"score{b}{c}", tag=f"bank{4 * (c // 2) + 2 * b + c % 2}") for c in range(NJ)] for b in range(SP)]
 
         def score_pass(a, b, c):
             plane = planes[a][:].bitcast(U8)
@@ -126,6 +123,20 @@ def tile_list_residue_pocket_gate_kernel(
             gather_tab2(0, h)
         for b in range(SP):
             gather_tab(0, b)
+        wg_raw = [
+            late.tile([P, PACK, N], F32, name="wg_raw0", align_bytes=64, offset=4 * T2),
+            late.tile([P, PACK, N], F32, name="wg_raw1", align_bytes=64, offset=4 * T2 + 4 * T - 128),
+        ]
+        wvw = late.tile([P, SP, 2 * N], U8, name="wvw", align_bytes=64, offset=4 * T2 + 4 * PACK * N)
+        load_words(words2[1], tab2_words[1])
+        nc.sync.dma_start(wg_raw[0][:], wg[0:PASS, :].rearrange("(p t) n -> p t n", t=PACK))
+        nc.sync.dma_start(wg_raw[1][:], wg[PASS : 2 * PASS, :].rearrange("(p t) n -> p t n", t=PACK))
+        nc.sync.dma_start(wvw[:].bitcast(I32), wv_words.rearrange("b p n -> p b n").bitcast(I32))
+        bg_t = late.tile([P, NT], F32, name="bg_t", align_bytes=64, offset=4 * T2 + 4 * PACK * N + SP * 2 * N)
+        with nc.allow_non_contiguous_dma(reason="one value a partition"):
+            nc.sync.dma_start(bg_t[:], bg.rearrange("(c p) -> p c", p=P))
+        bg_h = keep.tile([P, NT], F32, name="bg_h")
+        nc.gpsimd.tensor_scalar(bg_h[:], bg_t[:], 0.5, 0.0, ALU.mult, ALU.add)
         for b in range(SP):
             for c in range(NJ):
                 score_pass(0, b, c)
@@ -133,9 +144,9 @@ def tile_list_residue_pocket_gate_kernel(
             gather_tab(1, b)
         for h in range(2):
             gather_tab2(1, h)
-        for b in range(SP):
-            for c in range(NJ):
-                score_pass(1, b, c)
+        order = [(b, 2 * h + e) for h in range(2) for b in range(SP) for e in range(2)]
+        for b, c in order:
+            score_pass(1, b, c)
 
         h16 = [keep.tile([P, S2, PACK], BF16, name=f"h16{b}", align_bytes=64) for b in range(SP)]
         hq = [keep.tile([P, S2], U32, name=f"hq{b}", align_bytes=64) for b in range(SP)]
@@ -154,62 +165,109 @@ def tile_list_residue_pocket_gate_kernel(
                 ALU.mult,
             )
 
-        def quant(codes, scales, src):
-            nc.vector.quantize_mx(out=codes[:].bitcast(FP8X4), scales=scales[:], in_=src[:].rearrange("p n t -> p (n t)"))
+        JH = S2 // 2
+        NH = N // 2
 
-        def wg_views(b):
+        def quant(codes, scales, src, lo, hi):
+            nc.vector.quantize_mx(
+                out=codes[:, lo:hi].bitcast(FP8X4),
+                scales=scales[:, lo:hi],
+                in_=src[:, lo:hi, :].rearrange("p n t -> p (n t)"),
+            )
+
+        def quant_h(b, h):
+            quant(hq[b], hs[b], h16[b], h * JH, (h + 1) * JH)
+
+        def quant_wg(b, u):
+            quant(wq[b], ws[b], wg16[b], u * NH, (u + 1) * NH)
+
+        def wg_views(b, u):
             return (
-                wg16[b][:].rearrange("p (c i) t -> p c t i", i=4),
-                wg_raw[b][:].rearrange("p t (c i) -> p c t i", i=4),
+                wg16[b][:, u * NH : (u + 1) * NH, :].rearrange("p (c i) t -> p c t i", i=4),
+                wg_raw[b][:, :, u * NH : (u + 1) * NH].rearrange("p t (c i) -> p c t i", i=4),
             )
 
-        for c in range(NJ):
-            bound(0, c)
-        nc.vector.tensor_copy(*wg_views(0))
-        quant(hq[0], hs[0], h16[0])
-        bound(1, 0)
-        quant(wq[0], ws[0], wg16[0])
-        for c in range(1, NJ):
-            bound(1, c)
-        nc.scalar.copy(*wg_views(1))
-
-        pb = [psum.tile([P, S2], F32, name=f"feat{n}", tag=f"bank{n}") for n in range(NT)]
-        gb = [psum.tile([P, S2], F32, name=f"gate{n}", tag=f"bank{NT + n}") for n in range(NT)]
         wvs8 = wvs[:].bitcast(U8)
+        feat = {}
+        gate = {}
 
-        def feat_pass(b, n):
-            nc.tensor.matmul_mx(
-                out=pb[n][:],
-                lhsT=wvw[:, b, 2 * P * n : 2 * P * (n + 1)].bitcast(FP4X4),
-                lhsT_scale=wvs8[:, b, P * n : P * (n + 1)],
-                rhs=hq[b][:].bitcast(FP8X4),
-                rhs_scale=hs[b][:],
-                start=(b == 0),
-                stop=(b == SP - 1),
+        def feat_pass(b, h, u):
+            if b == 0:
+                feat[h, u] = psum.tile([P, 2, JH], F32, name=f"feat{h}{u}", tag=f"bank{4 * h + u}")
+            for e in range(2):
+                n = 2 * u + e
+                for q in range(2):
+                    cols = slice(h * JH + q * JC, h * JH + (q + 1) * JC)
+                    nc.tensor.matmul_mx(
+                        out=feat[h, u][:, e, q * JC : (q + 1) * JC],
+                        lhsT=wvw[:, b, 2 * P * n : 2 * P * (n + 1)].bitcast(FP4X4),
+                        lhsT_scale=wvs8[:, b, P * n : P * (n + 1)],
+                        rhs=hq[b][:, cols].bitcast(FP8X4),
+                        rhs_scale=hs[b][:, cols],
+                        start=(b == 0 and e == 0 and q == 0),
+                        stop=(b == SP - 1 and e == 1 and q == 1),
+                    )
+
+        def gate_pass(b, h, u):
+            if b == 0:
+                gate[h, u] = psum.tile([P, 2, JH], F32, name=f"gate{h}{u}", tag=f"bank{4 * h + 2 + u}")
+            cols = slice(h * JH, (h + 1) * JH)
+            for e in range(2):
+                n = 2 * u + e
+                nc.tensor.matmul_mx(
+                    out=gate[h, u][:, e, :],
+                    lhsT=wq[b][:, P * n : P * (n + 1)].bitcast(FP8X4),
+                    lhsT_scale=ws[b][:, P * n : P * (n + 1)],
+                    rhs=hq[b][:, cols].bitcast(FP8X4),
+                    rhs_scale=hs[b][:, cols],
+                    start=(b == 0 and e == 0),
+                    stop=(b == SP - 1 and e == 1),
+                )
+
+        def finish(h, u):
+            th2 = ring.tile([P, 2, JH], F32, name="th2", bufs=4)
+            for e in range(2):
+                n = 2 * u + e
+                nc.scalar.activation(th2[:, e, :], gate[h, u][:, e, :], ACT.Tanh, bias=bg_h[:, n : n + 1])
+            res = ring.tile([P, 2, JH], F32, name="res", bufs=4)
+            nc.vector.scalar_tensor_tensor(res[:], th2[:], 1.0, feat[h, u][:], ALU.add, ALU.mult)
+            nc.sync.dma_start(
+                out[u * NH : (u + 1) * NH, h * JH : (h + 1) * JH].rearrange("(e p) j -> p e j", p=P), res[:]
             )
 
-        def gate_pass(b, n):
-            nc.tensor.matmul_mx(
-                out=gb[n][:],
-                lhsT=wq[b][:, P * n : P * (n + 1)].bitcast(FP8X4),
-                lhsT_scale=ws[b][:, P * n : P * (n + 1)],
-                rhs=hq[b][:].bitcast(FP8X4),
-                rhs_scale=hs[b][:],
-                start=(b == 0),
-                stop=(b == SP - 1),
-            )
-
-        for n in range(NT):
-            feat_pass(0, n)
-        for n in range(NT):
-            gate_pass(0, n)
-        quant(wq[1], ws[1], wg16[1])
-        quant(hq[1], hs[1], h16[1])
-        for n in range(NT):
-            gate_pass(1, n)
-            feat_pass(1, n)
-            th2 = ring.tile([P, S2], F32, name="th2")
-            nc.scalar.activation(th2[:], gb[n][:], ACT.Tanh, bias=bg_h[:, n : n + 1])
-            res = ring.tile([P, S2], F32, name="res")
-            nc.vector.scalar_tensor_tensor(res[:], th2[:], 1.0, pb[n][:], ALU.add, ALU.mult)
-            nc.sync.dma_start(out[n * P : (n + 1) * P, :], res[:])
+        bound(0, 0)
+        bound(0, 1)
+        bound(1, 0)
+        quant_h(0, 0)
+        bound(1, 1)
+        bound(0, 2)
+        quant_h(1, 0)
+        nc.vector.tensor_copy(*wg_views(0, 0))
+        bound(0, 3)
+        quant_wg(0, 0)
+        nc.vector.tensor_copy(*wg_views(0, 1))
+        bound(1, 2)
+        quant_h(0, 1)
+        quant_wg(0, 1)
+        bound(1, 3)
+        nc.scalar.copy(*wg_views(1, 0))
+        nc.scalar.copy(*wg_views(1, 1))
+        quant_wg(1, 0)
+        quant_h(1, 1)
+        quant_wg(1, 1)
+        for b in range(SP):
+            for u in range(2):
+                feat_pass(b, 0, u)
+        for u in range(2):
+            gate_pass(0, 0, u)
+        gate_pass(1, 0, 0)
+        finish(0, 0)
+        for u in range(2):
+            feat_pass(0, 1, u)
+            gate_pass(0, 1, u)
+        gate_pass(1, 0, 1)
+        finish(0, 1)
+        for u in range(2):
+            gate_pass(1, 1, u)
+            feat_pass(1, 1, u)
+            finish(1, u)

@@ -41,7 +41,6 @@ def tile_list_residue_pocket_gate_kernel(
         sc = keep.tile([P, T // 4], I32, name="sc", align_bytes=64)
         sc2 = keep.tile([P, T2 // 4], I32, name="sc2", align_bytes=64)
         planes = [keep.tile([P, (S + S2) // 4], I32, name=f"plane{a}", align_bytes=64) for a in range(KP)]
-        wvs = keep.tile([P, SP, N // 4], I32, name="wvs", align_bytes=64)
         words = [
             late.tile([P, T], I32, name="words0", align_bytes=64, offset=4 * T2 - 64),
             keep.tile([P, T], I32, name="words1", align_bytes=64),
@@ -53,7 +52,6 @@ def tile_list_residue_pocket_gate_kernel(
 
         nc.vector.memset(sc[0:96, :], 0)
         nc.gpsimd.memset(sc2[0:96, :], 0)
-        nc.gpsimd.memset(wvs[:], 0)
         for a in range(KP):
             nc.gpsimd.memset(planes[a][:], 0)
 
@@ -68,11 +66,9 @@ def tile_list_residue_pocket_gate_kernel(
         def load_words(tile, source):
             nc.sync.dma_start(tile[:], source.rearrange("p n t -> p (n t)").bitcast(I32))
 
-        load_words(words2[0], tab2_words[0])
         load_words(words[0], tab_words[0])
         load_words(words[1], tab_words[1])
-        for r in range(4):
-            nc.gpsimd.dma_start(wvs[r:P:32, :, :], wv_scales[:, r:16:4, :].rearrange("b q n -> q b n").bitcast(I32))
+        load_words(words2[0], tab2_words[0])
         rw_h = keep.tile([P, SP, PACK], F32, name="rw_h")
         nc.scalar.activation(rw_h[:], rw_t[:], ACT.Copy, scale=0.5)
 
@@ -92,7 +88,7 @@ def tile_list_residue_pocket_gate_kernel(
                 nc.scalar.dma_start(planes[a][4 * a + r : P : 32, :], stage32[96 + 16 * a + r : 96 + 16 * a + 16 : 4, :])
 
         gw = [[keep.tile([P, PASS], U32, name=f"gw{a}{b}", tag=f"gw{a}{b}", align_bytes=64) for b in range(SP)] for a in range(KP)]
-        gw2 = [[keep.tile([P, S2 // 2], U32, name=f"gw2{a}{h}", align_bytes=64) for h in range(2)] for a in range(KP)]
+        gw2 = [[keep.tile([P, S2 // 2], U32, name=f"gw2{a}{h}", tag=f"gw2{a}{h}", align_bytes=64) for h in range(2)] for a in range(KP)]
 
         def gather_tab(a, b):
             nc.vector.tensor_copy(
@@ -103,14 +99,16 @@ def tile_list_residue_pocket_gate_kernel(
         def gather_tab2(a, h):
             nc.vector.tensor_copy(gw2[a][h][:], words2[a][:].bitcast(U32).indirect(idx2[:, 16 * h : 16 * (h + 1)]))
 
-        banks = [[psum.tile([P, PACK, JC], F32, name=f"score{b}{c}", tag=f"bank{4 * (c // 2) + 2 * b + c % 2}") for c in range(NJ)] for b in range(SP)]
+        banks = {}
 
         def score_pass(a, b, c):
+            if a == 0:
+                banks[b, c] = psum.tile([P, PACK, JC], F32, name=f"score{b}{c}", tag=f"bank{2 * b + c % 2}")
             plane = planes[a][:].bitcast(U8)
             for t in range(PACK):
                 col = b * PASS + t * P
                 nc.tensor.matmul_mx(
-                    out=banks[b][c][:, t, :],
+                    out=banks[b, c][:, t, :],
                     lhsT=gw[a][b][:, t * P : (t + 1) * P].bitcast(FP8X4),
                     lhsT_scale=plane[4 * a : P, col : col + P],
                     rhs=gw2[a][c // 2][:, (c % 2) * JC : (c % 2 + 1) * JC].bitcast(FP8X4),
@@ -119,45 +117,65 @@ def tile_list_residue_pocket_gate_kernel(
                     stop=(a == KP - 1 and t == PACK - 1),
                 )
 
-        for h in range(2):
-            gather_tab2(0, h)
+        NH = N // 2
         for b in range(SP):
             gather_tab(0, b)
-        wg_raw = [
-            late.tile([P, PACK, N], F32, name="wg_raw0", align_bytes=64, offset=4 * T2),
-            late.tile([P, PACK, N], F32, name="wg_raw1", align_bytes=64, offset=4 * T2 + 4 * T - 128),
-        ]
-        wvw = late.tile([P, SP, 2 * N], U8, name="wvw", align_bytes=64, offset=4 * T2 + 4 * PACK * N)
+        quarter = 4 * PACK * NH
+        base = 4 * T2
+        places = {(0, 0): base, (1, 0): base + quarter, (0, 1): base + 2 * quarter, (1, 1): base + 4 * T - 128}
+        wg_raw = {
+            key: late.tile([P, PACK, NH], F32, name=f"wg_raw{key[0]}{key[1]}", align_bytes=64, offset=place)
+            for key, place in places.items()
+        }
+        wvw = late.tile([P, SP, 2 * N], U8, name="wvw", align_bytes=64, offset=base + 3 * quarter)
+        wvs = late.tile([P, SP, N // 4], I32, name="wvs", align_bytes=64, offset=base + 3 * quarter + SP * 2 * N)
+        bg_t = late.tile([P, NT], F32, name="bg_t", align_bytes=64, offset=base + 3 * quarter + SP * 3 * N)
+
+        def load_wg(b, u):
+            rows = wg[b * PASS : (b + 1) * PASS, u * NH : (u + 1) * NH]
+            nc.sync.dma_start(wg_raw[b, u][:], rows.rearrange("(p t) n -> p t n", t=PACK))
+
+        nc.vector.memset(wvs[:], 0)
         load_words(words2[1], tab2_words[1])
-        nc.sync.dma_start(wg_raw[0][:], wg[0:PASS, :].rearrange("(p t) n -> p t n", t=PACK))
-        nc.sync.dma_start(wg_raw[1][:], wg[PASS : 2 * PASS, :].rearrange("(p t) n -> p t n", t=PACK))
+        load_wg(0, 0)
+        load_wg(1, 0)
         nc.sync.dma_start(wvw[:].bitcast(I32), wv_words.rearrange("b p n -> p b n").bitcast(I32))
-        bg_t = late.tile([P, NT], F32, name="bg_t", align_bytes=64, offset=4 * T2 + 4 * PACK * N + SP * 2 * N)
+        for r in range(4):
+            nc.sync.dma_start(wvs[r:P:32, :, :], wv_scales[:, r:16:4, :].rearrange("b q n -> q b n").bitcast(I32))
+        load_wg(0, 1)
+        load_wg(1, 1)
         with nc.allow_non_contiguous_dma(reason="one value a partition"):
             nc.sync.dma_start(bg_t[:], bg.rearrange("(c p) -> p c", p=P))
         bg_h = keep.tile([P, NT], F32, name="bg_h")
         nc.gpsimd.tensor_scalar(bg_h[:], bg_t[:], 0.5, 0.0, ALU.mult, ALU.add)
         for b in range(SP):
-            for c in range(NJ):
-                score_pass(0, b, c)
-        for b in range(SP):
             gather_tab(1, b)
-        for h in range(2):
-            gather_tab2(1, h)
-        order = [(b, 2 * h + e) for h in range(2) for b in range(SP) for e in range(2)]
-        for b, c in order:
-            score_pass(1, b, c)
+        for a in range(KP):
+            for h in range(2):
+                gather_tab2(a, h)
+
+        def score(b, c):
+            for a in range(KP):
+                score_pass(a, b, c)
+
+        for b in range(SP):
+            for c in range(2):
+                score(b, c)
 
         h16 = [keep.tile([P, S2, PACK], BF16, name=f"h16{b}", align_bytes=64) for b in range(SP)]
         hq = [keep.tile([P, S2], U32, name=f"hq{b}", align_bytes=64) for b in range(SP)]
         hs = [keep.tile([P, S2], U8, name=f"hs{b}", align_bytes=64) for b in range(SP)]
-        wg16 = [keep.tile([P, N, PACK], BF16, name=f"wg16{b}", tag=f"gw1{b}", align_bytes=64) for b in range(SP)]
+        slots = {(0, 0): "wg16", (1, 0): "gw11", (0, 1): "gw211", (1, 1): "gw01"}
+        wg16 = {
+            key: keep.tile([P, NH, PACK], BF16, name=f"wg16{key[0]}{key[1]}", tag=slot, align_bytes=64)
+            for key, slot in slots.items()
+        }
         wq = [keep.tile([P, N], U32, name=f"wq{b}", align_bytes=64) for b in range(SP)]
         ws = [keep.tile([P, N], U8, name=f"ws{b}", align_bytes=64) for b in range(SP)]
 
         def bound(b, c):
             th = ring.tile([P, JC, PACK], F32, name="th")
-            nc.scalar.activation(th[:], banks[b][c][:].rearrange("p t j -> p j t"), ACT.Tanh)
+            nc.scalar.activation(th[:], banks[b, c][:].rearrange("p t j -> p j t"), ACT.Tanh)
             nc.vector.tensor_tensor(
                 h16[b][:, c * JC : (c + 1) * JC, :],
                 th[:],
@@ -166,25 +184,24 @@ def tile_list_residue_pocket_gate_kernel(
             )
 
         JH = S2 // 2
-        NH = N // 2
 
         def quant(codes, scales, src, lo, hi):
             nc.vector.quantize_mx(
                 out=codes[:, lo:hi].bitcast(FP8X4),
                 scales=scales[:, lo:hi],
-                in_=src[:, lo:hi, :].rearrange("p n t -> p (n t)"),
+                in_=src.rearrange("p n t -> p (n t)"),
             )
 
         def quant_h(b, h):
-            quant(hq[b], hs[b], h16[b], h * JH, (h + 1) * JH)
+            quant(hq[b], hs[b], h16[b][:, h * JH : (h + 1) * JH, :], h * JH, (h + 1) * JH)
 
         def quant_wg(b, u):
-            quant(wq[b], ws[b], wg16[b], u * NH, (u + 1) * NH)
+            quant(wq[b], ws[b], wg16[b, u][:], u * NH, (u + 1) * NH)
 
         def wg_views(b, u):
             return (
-                wg16[b][:, u * NH : (u + 1) * NH, :].rearrange("p (c i) t -> p c t i", i=4),
-                wg_raw[b][:, :, u * NH : (u + 1) * NH].rearrange("p t (c i) -> p c t i", i=4),
+                wg16[b, u][:].rearrange("p (c i) t -> p c t i", i=4),
+                wg_raw[b, u][:].rearrange("p t (c i) -> p c t i", i=4),
             )
 
         wvs8 = wvs[:].bitcast(U8)
@@ -193,7 +210,7 @@ def tile_list_residue_pocket_gate_kernel(
 
         def feat_pass(b, h, u):
             if b == 0:
-                feat[h, u] = psum.tile([P, 2, JH], F32, name=f"feat{h}{u}", tag=f"bank{4 * h + u}")
+                feat[h, u] = psum.tile([P, 2, JH], F32, name=f"feat{h}{u}", tag=f"bank{4 * (1 - h) + u}")
             for e in range(2):
                 n = 2 * u + e
                 for q in range(2):
@@ -210,7 +227,7 @@ def tile_list_residue_pocket_gate_kernel(
 
         def gate_pass(b, h, u):
             if b == 0:
-                gate[h, u] = psum.tile([P, 2, JH], F32, name=f"gate{h}{u}", tag=f"bank{4 * h + 2 + u}")
+                gate[h, u] = psum.tile([P, 2, JH], F32, name=f"gate{h}{u}", tag=f"bank{4 * (1 - h) + 2 + u}")
             cols = slice(h * JH, (h + 1) * JH)
             for e in range(2):
                 n = 2 * u + e
@@ -224,50 +241,59 @@ def tile_list_residue_pocket_gate_kernel(
                     stop=(b == SP - 1 and e == 1),
                 )
 
-        def finish(h, u):
+        def finish(h, u, parts):
             th2 = ring.tile([P, 2, JH], F32, name="th2", bufs=4)
+            res = ring.tile([P, 2, JH], F32, name="res", bufs=4)
+            rows = out[u * NH : (u + 1) * NH, h * JH : (h + 1) * JH].rearrange("(e p) j -> p e j", p=P)
             for e in range(2):
                 n = 2 * u + e
                 nc.scalar.activation(th2[:, e, :], gate[h, u][:, e, :], ACT.Tanh, bias=bg_h[:, n : n + 1])
-            res = ring.tile([P, 2, JH], F32, name="res", bufs=4)
-            nc.vector.scalar_tensor_tensor(res[:], th2[:], 1.0, feat[h, u][:], ALU.add, ALU.mult)
-            nc.sync.dma_start(
-                out[u * NH : (u + 1) * NH, h * JH : (h + 1) * JH].rearrange("(e p) j -> p e j", p=P), res[:]
-            )
+            for part in parts:
+                nc.vector.scalar_tensor_tensor(res[:, part, :], th2[:, part, :], 1.0, feat[h, u][:, part, :], ALU.add, ALU.mult)
+                nc.sync.dma_start(rows[:, part, :], res[:, part, :])
 
+        whole = [slice(0, 2)]
+        halves = [slice(0, 1), slice(1, 2)]
+        nc.vector.tensor_copy(*wg_views(0, 0))
         bound(0, 0)
+        score(0, 2)
+        quant_wg(0, 0)
         bound(0, 1)
+        score(0, 3)
         bound(1, 0)
+        score(1, 2)
         quant_h(0, 0)
         bound(1, 1)
+        score(1, 3)
         bound(0, 2)
         quant_h(1, 0)
-        nc.vector.tensor_copy(*wg_views(0, 0))
         bound(0, 3)
-        quant_wg(0, 0)
-        nc.vector.tensor_copy(*wg_views(0, 1))
         bound(1, 2)
         quant_h(0, 1)
-        quant_wg(0, 1)
         bound(1, 3)
         nc.scalar.copy(*wg_views(1, 0))
+        nc.scalar.copy(*wg_views(0, 1))
         nc.scalar.copy(*wg_views(1, 1))
         quant_wg(1, 0)
         quant_h(1, 1)
+        quant_wg(0, 1)
         quant_wg(1, 1)
         for b in range(SP):
             for u in range(2):
                 feat_pass(b, 0, u)
-        for u in range(2):
-            gate_pass(0, 0, u)
-        gate_pass(1, 0, 0)
-        finish(0, 0)
+        for b in range(SP):
+            gate_pass(b, 0, 0)
+        finish(0, 0, whole)
         for u in range(2):
             feat_pass(0, 1, u)
-            gate_pass(0, 1, u)
+        gate_pass(0, 1, 0)
+        gate_pass(1, 1, 0)
+        feat_pass(1, 1, 0)
+        finish(1, 0, whole)
+        feat_pass(1, 1, 1)
+        for h in range(2):
+            gate_pass(0, h, 1)
         gate_pass(1, 0, 1)
-        finish(0, 1)
-        for u in range(2):
-            gate_pass(1, 1, u)
-            feat_pass(1, 1, u)
-            finish(1, u)
+        finish(0, 1, whole)
+        gate_pass(1, 1, 1)
+        finish(1, 1, halves)

@@ -46,54 +46,55 @@ def tile_list_residue_pocket_gate_kernel(
             keep.tile([P, T], I32, name="words1", align_bytes=64),
         ]
         words2 = [
-            keep.tile([P, T2], I32, name="words20", align_bytes=64),
+            late.tile([P, T2], I32, name="words20", align_bytes=64, offset=8 * T),
             late.tile([P, T2], I32, name="words21", align_bytes=64, offset=0),
         ]
 
-        nc.vector.memset(sc[0:96, :], 0)
-        nc.gpsimd.memset(sc2[0:96, :], 0)
+        nc.vector.memset(sc2[0:96, :], 0)
+        nc.gpsimd.memset(sc[0:96, :], 0)
         for a in range(KP):
             nc.gpsimd.memset(planes[a][:], 0)
 
-        rw_t = keep.tile([P, SP, PACK], F32, name="rw_t")
-        with nc.allow_non_contiguous_dma(reason="small per-partition vectors"):
-            nc.scalar.dma_start(rw_t[:], rw.rearrange("(b p t) -> p b t", b=SP, t=PACK))
-        nc.sync.dma_start(sc[96:P, :], tab_scales.rearrange("a q t -> (a q) t").bitcast(I32))
-        nc.sync.dma_start(idx[:], offs)
         nc.sync.dma_start(sc2[96:P, :], tab2_scales.rearrange("a q t -> (a q) t").bitcast(I32))
         nc.sync.dma_start(idx2[:], offs2)
+        nc.sync.dma_start(sc[96:P, :], tab_scales.rearrange("a q t -> (a q) t").bitcast(I32))
+        nc.sync.dma_start(idx[:], offs)
 
         def load_words(tile, source):
             nc.sync.dma_start(tile[:], source.rearrange("p n t -> p (n t)").bitcast(I32))
 
         load_words(words[0], tab_words[0])
         load_words(words[1], tab_words[1])
-        load_words(words2[0], tab2_words[0])
-        rw_h = keep.tile([P, SP, PACK], F32, name="rw_h")
-        nc.scalar.activation(rw_h[:], rw_t[:], ACT.Copy, scale=0.5)
 
-        gs = keep.tile([P, S], U8, name="gs", align_bytes=64)
+        gs = late.tile([P, S], U8, name="gs", align_bytes=64, offset=8 * T)
         gs2 = keep.tile([P, S2], U8, name="gs2", align_bytes=64)
         stage = keep.tile([P, S + S2], U8, name="stage", align_bytes=64)
-        nc.vector.tensor_copy(gs[:], sc[:].bitcast(U8).indirect(idx[:]))
+        stage32 = stage[:].bitcast(I32)
         nc.vector.tensor_copy(gs2[:], sc2[:].bitcast(U8).indirect(idx2[:]))
+        nc.vector.tensor_copy(gs[:], sc[:].bitcast(U8).indirect(idx[:]))
+        nc.vector.tensor_copy(stage32[:, S // 4 : (S + S2) // 4], gs2[:].bitcast(I32))
         nc.vector.tensor_copy(
             stage[:, 0:S].rearrange("p (b t m) -> p b t m", b=SP, t=PACK),
             gs[:].rearrange("p (b m t) -> p b t m", b=SP, t=PACK),
         )
-        nc.vector.tensor_copy(stage[:, S : S + S2], gs2[:])
-        stage32 = stage[:].bitcast(I32)
         for a in range(KP):
             for r in range(4):
-                nc.scalar.dma_start(planes[a][4 * a + r : P : 32, :], stage32[96 + 16 * a + r : 96 + 16 * a + 16 : 4, :])
+                nc.sync.dma_start(planes[a][4 * a + r : P : 32, :], stage32[96 + 16 * a + r : 96 + 16 * a + 16 : 4, :])
+            if a == 0:
+                load_words(words2[0], tab2_words[0])
 
         gw = [[keep.tile([P, PASS], U32, name=f"gw{a}{b}", tag=f"gw{a}{b}", align_bytes=64) for b in range(SP)] for a in range(KP)]
         gw2 = [[keep.tile([P, S2 // 2], U32, name=f"gw2{a}{h}", tag=f"gw2{a}{h}", align_bytes=64) for h in range(2)] for a in range(KP)]
 
-        def gather_tab(a, b):
+        picked = [keep.tile([P, S], U32, name=f"picked{a}", align_bytes=64) for a in range(KP)]
+
+        def gather_tab(a):
+            nc.vector.tensor_copy(picked[a][:], words[a][:].bitcast(U32).indirect(idx[:]))
+
+        def permute_tab(a, b):
             nc.vector.tensor_copy(
-                gw[a][b][:].rearrange("p (t m) -> p m t", t=PACK),
-                words[a][:].bitcast(U32).indirect(idx[:, 32 * b : 32 * (b + 1)]),
+                gw[a][b][:].bitcast(I32).rearrange("p (t c i) -> p c t i", t=PACK, i=4),
+                picked[a][:, b * PASS : (b + 1) * PASS].bitcast(I32).rearrange("p (c i t) -> p c t i", t=PACK, i=4),
             )
 
         def gather_tab2(a, h):
@@ -118,8 +119,8 @@ def tile_list_residue_pocket_gate_kernel(
                 )
 
         NH = N // 2
-        for b in range(SP):
-            gather_tab(0, b)
+        gather_tab(0)
+        permute_tab(0, 0)
         quarter = 4 * PACK * NH
         base = 4 * T2
         places = {(0, 0): base, (1, 0): base + quarter, (0, 1): base + 2 * quarter, (1, 1): base + 4 * T - 128}
@@ -137,22 +138,29 @@ def tile_list_residue_pocket_gate_kernel(
 
         nc.vector.memset(wvs[:], 0)
         load_words(words2[1], tab2_words[1])
+        rw_t = late.tile([P, SP, PACK], F32, name="rw_t", align_bytes=64, offset=base + 3 * quarter + SP * 3 * N + 64)
+        nc.sync.dma_start(rw_t[:], rw.rearrange("(b p t) -> p b t", b=SP, t=PACK))
+        rw_h = keep.tile([P, SP, PACK], F32, name="rw_h")
+        nc.scalar.activation(rw_h[:], rw_t[:], ACT.Copy, scale=0.5)
         load_wg(0, 0)
         load_wg(1, 0)
         nc.sync.dma_start(wvw[:].bitcast(I32), wv_words.rearrange("b p n -> p b n").bitcast(I32))
         for r in range(4):
             nc.sync.dma_start(wvs[r:P:32, :, :], wv_scales[:, r:16:4, :].rearrange("b q n -> q b n").bitcast(I32))
-        load_wg(0, 1)
-        load_wg(1, 1)
         with nc.allow_non_contiguous_dma(reason="one value a partition"):
             nc.sync.dma_start(bg_t[:], bg.rearrange("(c p) -> p c", p=P))
+        load_wg(0, 1)
+        load_wg(1, 1)
         bg_h = keep.tile([P, NT], F32, name="bg_h")
         nc.gpsimd.tensor_scalar(bg_h[:], bg_t[:], 0.5, 0.0, ALU.mult, ALU.add)
-        for b in range(SP):
-            gather_tab(1, b)
-        for a in range(KP):
-            for h in range(2):
-                gather_tab2(a, h)
+        gather_tab(1)
+        gather_tab2(0, 0)
+        permute_tab(1, 0)
+        gather_tab2(1, 0)
+        permute_tab(0, 1)
+        permute_tab(1, 1)
+        gather_tab2(0, 1)
+        gather_tab2(1, 1)
 
         def score(b, c):
             for a in range(KP):
@@ -198,10 +206,10 @@ def tile_list_residue_pocket_gate_kernel(
         def quant_wg(b, u):
             quant(wq[b], ws[b], wg16[b, u][:], u * NH, (u + 1) * NH)
 
-        def wg_views(b, u):
+        def wg_views(b, u, lo=0, hi=NH):
             return (
-                wg16[b, u][:].rearrange("p (c i) t -> p c t i", i=4),
-                wg_raw[b, u][:].rearrange("p t (c i) -> p c t i", i=4),
+                wg16[b, u][:, lo:hi, :].rearrange("p (c i) t -> p c t i", i=4),
+                wg_raw[b, u][:, :, lo:hi].rearrange("p t (c i) -> p c t i", i=4),
             )
 
         wvs8 = wvs[:].bitcast(U8)
@@ -254,7 +262,7 @@ def tile_list_residue_pocket_gate_kernel(
 
         whole = [slice(0, 2)]
         halves = [slice(0, 1), slice(1, 2)]
-        nc.vector.tensor_copy(*wg_views(0, 0))
+        nc.scalar.copy(*wg_views(0, 0))
         bound(0, 0)
         score(0, 2)
         quant_wg(0, 0)
@@ -273,9 +281,10 @@ def tile_list_residue_pocket_gate_kernel(
         bound(1, 3)
         nc.scalar.copy(*wg_views(1, 0))
         nc.scalar.copy(*wg_views(0, 1))
-        nc.scalar.copy(*wg_views(1, 1))
+        nc.scalar.copy(*wg_views(1, 1, 0, P))
         quant_wg(1, 0)
         quant_h(1, 1)
+        nc.vector.tensor_copy(*wg_views(1, 1, P, NH))
         quant_wg(0, 1)
         quant_wg(1, 1)
         for b in range(SP):

@@ -18,12 +18,28 @@ ALU = mybir.AluOpType
 
 P = 128
 PACK = 4
-PASS = P * PACK
-KP = K // PASS
-SP = S // PASS
-JC = 128
-NJ = S2 // JC
-NT = N // P
+GROUP = P * PACK
+KG = K // GROUP
+IG = S // GROUP
+BLOCKS = 16
+QUAD = 32
+LIST = 16
+JQ = 128
+JH = S2 // 2
+NH = N // 2
+ROWS_AT = P - KG * BLOCKS
+SCORE_BANKS = 3
+ALIGN = 64
+
+WG_BYTES = 4 * PACK * NH
+V_WORDS_AT = 0
+WG_AT = {(0, 0): 0, (1, 0): WG_BYTES, (0, 1): 2 * WG_BYTES, (1, 1): 4 * T - ALIGN}
+WV_WORDS_AT = 3 * WG_BYTES
+WV_SCALES_AT = WV_WORDS_AT + IG * 2 * N
+BG_AT = WV_SCALES_AT + IG * N
+RW_AT = BG_AT + ALIGN
+V2_WORDS_AT = [4 * T + WG_BYTES + a * 4 * T2 for a in range(KG)]
+V_PICKED_SCALES_AT = V2_WORDS_AT[1] - S // 2
 
 
 def tile_list_residue_pocket_gate_kernel(
@@ -34,185 +50,179 @@ def tile_list_residue_pocket_gate_kernel(
         keep = ctx.enter_context(tc.tile_pool(name="keep", bufs=1))
         ring = ctx.enter_context(tc.tile_pool(name="ring", bufs=8))
         psum = ctx.enter_context(tc.psum_pool(name="psum", bufs=1))
-        late = ctx.enter_context(tc.tile_pool(name="late", bufs=1))
+        shared = ctx.enter_context(tc.tile_pool(name="shared", bufs=1))
 
-        idx = keep.tile([P, S // 16], U16, name="idx")
-        idx2 = keep.tile([P, S2 // 16], U16, name="idx2")
-        sc = keep.tile([P, T // 4], I32, name="sc", align_bytes=64)
-        sc2 = keep.tile([P, T2 // 4], I32, name="sc2", align_bytes=64)
-        planes = [keep.tile([P, (S + S2) // 4], I32, name=f"plane{a}", align_bytes=64) for a in range(KP)]
-        words = [
-            late.tile([P, T], I32, name="words0", align_bytes=64, offset=4 * T2 - 64),
-            keep.tile([P, T], I32, name="words1", align_bytes=64),
+        idx = keep.tile([P, S // LIST], U16, name="idx")
+        idx2 = keep.tile([P, S2 // LIST], U16, name="idx2")
+        v_rows = keep.tile([P, T // 4], I32, name="v_rows", align_bytes=ALIGN)
+        v2_rows = keep.tile([P, T2 // 4], I32, name="v2_rows", align_bytes=ALIGN)
+        scales = [keep.tile([P, (S + S2) // 4], I32, name=f"scales{a}", align_bytes=ALIGN) for a in range(KG)]
+        v_words = [
+            shared.tile([P, T], I32, name="v_words0", align_bytes=ALIGN, offset=V_WORDS_AT),
+            keep.tile([P, T], I32, name="v_words1", align_bytes=ALIGN),
         ]
-        words2 = [
-            late.tile([P, T2], I32, name="words20", align_bytes=64, offset=8 * T),
-            late.tile([P, T2], I32, name="words21", align_bytes=64, offset=0),
+        v2_words = [
+            shared.tile([P, T2], I32, name=f"v2_words{a}", align_bytes=ALIGN, offset=V2_WORDS_AT[a]) for a in range(KG)
         ]
 
-        nc.vector.memset(sc2[0:96, :], 0)
-        nc.gpsimd.memset(sc[0:96, :], 0)
-        for a in range(KP):
-            nc.gpsimd.memset(planes[a][:], 0)
+        nc.vector.memset(v2_rows[0:ROWS_AT, :], 0)
+        nc.gpsimd.memset(v_rows[0:ROWS_AT, :], 0)
+        for a in range(KG):
+            nc.gpsimd.memset(scales[a][:], 0)
 
-        nc.sync.dma_start(sc2[96:P, :], tab2_scales.rearrange("a q t -> (a q) t").bitcast(I32))
+        nc.sync.dma_start(v2_rows[ROWS_AT:P, :], tab2_scales.rearrange("a q t -> (a q) t").bitcast(I32))
         nc.sync.dma_start(idx2[:], offs2)
-        nc.sync.dma_start(sc[96:P, :], tab_scales.rearrange("a q t -> (a q) t").bitcast(I32))
+        nc.sync.dma_start(v_rows[ROWS_AT:P, :], tab_scales.rearrange("a q t -> (a q) t").bitcast(I32))
         nc.sync.dma_start(idx[:], offs)
 
         def load_words(tile, source):
             nc.sync.dma_start(tile[:], source.rearrange("p n t -> p (n t)").bitcast(I32))
 
-        load_words(words[0], tab_words[0])
-        load_words(words[1], tab_words[1])
+        for a in range(KG):
+            load_words(v_words[a], tab_words[a])
 
-        gs = late.tile([P, S], U8, name="gs", align_bytes=64, offset=8 * T)
-        gs2 = keep.tile([P, S2], U8, name="gs2", align_bytes=64)
-        stage = keep.tile([P, S + S2], U8, name="stage", align_bytes=64)
-        stage32 = stage[:].bitcast(I32)
-        nc.vector.tensor_copy(gs2[:], sc2[:].bitcast(U8).indirect(idx2[:]))
-        nc.vector.tensor_copy(gs[:], sc[:].bitcast(U8).indirect(idx[:]))
-        nc.vector.tensor_copy(stage32[:, S // 4 : (S + S2) // 4], gs2[:].bitcast(I32))
+        v_picked = shared.tile([P, S], U8, name="v_picked", align_bytes=ALIGN, offset=V_PICKED_SCALES_AT)
+        v2_picked = keep.tile([P, S2], U8, name="v2_picked", align_bytes=ALIGN)
+        staged = keep.tile([P, S + S2], U8, name="staged", align_bytes=ALIGN)
+        staged32 = staged[:].bitcast(I32)
+        nc.vector.tensor_copy(v2_picked[:], v2_rows[:].bitcast(U8).indirect(idx2[:]))
+        nc.vector.tensor_copy(v_picked[:], v_rows[:].bitcast(U8).indirect(idx[:]))
+        nc.vector.tensor_copy(staged32[:, S // 4 : (S + S2) // 4], v2_picked[:].bitcast(I32))
         nc.vector.tensor_copy(
-            stage[:, 0:S].rearrange("p (b t m) -> p b t m", b=SP, t=PACK),
-            gs[:].rearrange("p (b m t) -> p b t m", b=SP, t=PACK),
+            staged[:, 0:S].rearrange("p (b t m) -> p b t m", b=IG, t=PACK),
+            v_picked[:].rearrange("p (b m t) -> p b t m", b=IG, t=PACK),
         )
-        for a in range(KP):
+        for a in range(KG):
+            first = ROWS_AT + BLOCKS * a
             for r in range(4):
-                nc.sync.dma_start(planes[a][4 * a + r : P : 32, :], stage32[96 + 16 * a + r : 96 + 16 * a + 16 : 4, :])
-            if a == 0:
-                load_words(words2[0], tab2_words[0])
+                nc.sync.dma_start(scales[a][4 * a + r : P : QUAD, :], staged32[first + r : first + BLOCKS : 4, :])
+            load_words(v2_words[a], tab2_words[a])
 
-        gw = [[keep.tile([P, PASS], U32, name=f"gw{a}{b}", tag=f"gw{a}{b}", align_bytes=64) for b in range(SP)] for a in range(KP)]
-        gw2 = [[keep.tile([P, S2 // 2], U32, name=f"gw2{a}{h}", tag=f"gw2{a}{h}", align_bytes=64) for h in range(2)] for a in range(KP)]
+        v_codes = [
+            [keep.tile([P, GROUP], U32, name=f"v_codes{a}{b}", tag=f"v_codes{a}{b}", align_bytes=ALIGN) for b in range(IG)]
+            for a in range(KG)
+        ]
+        v2_codes = [
+            [keep.tile([P, JH], U32, name=f"v2_codes{a}{h}", tag=f"v2_codes{a}{h}", align_bytes=ALIGN) for h in range(2)]
+            for a in range(KG)
+        ]
 
-        picked = [keep.tile([P, S], U32, name=f"picked{a}", align_bytes=64) for a in range(KP)]
-
-        def gather_tab(a):
-            nc.vector.tensor_copy(picked[a][:], words[a][:].bitcast(U32).indirect(idx[:]))
-
-        def permute_tab(a, b):
+        def gather_v(a, b):
+            columns = GROUP // LIST
             nc.vector.tensor_copy(
-                gw[a][b][:].bitcast(I32).rearrange("p (t c i) -> p c t i", t=PACK, i=4),
-                picked[a][:, b * PASS : (b + 1) * PASS].bitcast(I32).rearrange("p (c i t) -> p c t i", t=PACK, i=4),
+                v_codes[a][b][:].rearrange("p (t m) -> p m t", t=PACK),
+                v_words[a][:].bitcast(U32).indirect(idx[:, columns * b : columns * (b + 1)]),
             )
 
-        def gather_tab2(a, h):
-            nc.vector.tensor_copy(gw2[a][h][:], words2[a][:].bitcast(U32).indirect(idx2[:, 16 * h : 16 * (h + 1)]))
+        def gather_v2(a, h):
+            columns = JH // LIST
+            nc.vector.tensor_copy(
+                v2_codes[a][h][:], v2_words[a][:].bitcast(U32).indirect(idx2[:, columns * h : columns * (h + 1)])
+            )
 
-        banks = {}
+        for b in range(IG):
+            gather_v(0, b)
 
-        def score_pass(a, b, c):
-            if a == 0:
-                banks[b, c] = psum.tile([P, PACK, JC], F32, name=f"score{b}{c}", tag=f"bank{2 * b + c % 2}")
-            plane = planes[a][:].bitcast(U8)
-            for t in range(PACK):
-                col = b * PASS + t * P
-                nc.tensor.matmul_mx(
-                    out=banks[b, c][:, t, :],
-                    lhsT=gw[a][b][:, t * P : (t + 1) * P].bitcast(FP8X4),
-                    lhsT_scale=plane[4 * a : P, col : col + P],
-                    rhs=gw2[a][c // 2][:, (c % 2) * JC : (c % 2 + 1) * JC].bitcast(FP8X4),
-                    rhs_scale=plane[4 * a : P, S + c * JC : S + (c + 1) * JC],
-                    start=(a == 0 and t == 0),
-                    stop=(a == KP - 1 and t == PACK - 1),
-                )
-
-        NH = N // 2
-        gather_tab(0)
-        permute_tab(0, 0)
-        quarter = 4 * PACK * NH
-        base = 4 * T2
-        places = {(0, 0): base, (1, 0): base + quarter, (0, 1): base + 2 * quarter, (1, 1): base + 4 * T - 128}
         wg_raw = {
-            key: late.tile([P, PACK, NH], F32, name=f"wg_raw{key[0]}{key[1]}", align_bytes=64, offset=place)
-            for key, place in places.items()
+            (b, u): shared.tile([P, PACK, NH], F32, name=f"wg_raw{b}{u}", align_bytes=ALIGN, offset=place)
+            for (b, u), place in WG_AT.items()
         }
-        wvw = late.tile([P, SP, 2 * N], U8, name="wvw", align_bytes=64, offset=base + 3 * quarter)
-        wvs = late.tile([P, SP, N // 4], I32, name="wvs", align_bytes=64, offset=base + 3 * quarter + SP * 2 * N)
-        bg_t = late.tile([P, NT], F32, name="bg_t", align_bytes=64, offset=base + 3 * quarter + SP * 3 * N)
+        wv_codes = shared.tile([P, IG, 2 * N], U8, name="wv_codes", align_bytes=ALIGN, offset=WV_WORDS_AT)
+        wv_rows = shared.tile([P, IG, N // 4], I32, name="wv_rows", align_bytes=ALIGN, offset=WV_SCALES_AT)
+        bg_raw = shared.tile([P, N // P], F32, name="bg_raw", align_bytes=ALIGN, offset=BG_AT)
+        rw_col = shared.tile([P, IG, PACK], F32, name="rw_col", align_bytes=ALIGN, offset=RW_AT)
 
         def load_wg(b, u):
-            rows = wg[b * PASS : (b + 1) * PASS, u * NH : (u + 1) * NH]
+            rows = wg[b * GROUP : (b + 1) * GROUP, u * NH : (u + 1) * NH]
             nc.sync.dma_start(wg_raw[b, u][:], rows.rearrange("(p t) n -> p t n", t=PACK))
 
-        nc.vector.memset(wvs[:], 0)
-        load_words(words2[1], tab2_words[1])
-        rw_t = late.tile([P, SP, PACK], F32, name="rw_t", align_bytes=64, offset=base + 3 * quarter + SP * 3 * N + 64)
-        nc.sync.dma_start(rw_t[:], rw.rearrange("(b p t) -> p b t", b=SP, t=PACK))
-        rw_h = keep.tile([P, SP, PACK], F32, name="rw_h")
-        nc.scalar.activation(rw_h[:], rw_t[:], ACT.Copy, scale=0.5)
+        nc.vector.memset(wv_rows[:], 0)
         load_wg(0, 0)
+        nc.sync.dma_start(rw_col[:], rw.rearrange("(b p t) -> p b t", b=IG, t=PACK))
         load_wg(1, 0)
-        nc.sync.dma_start(wvw[:].bitcast(I32), wv_words.rearrange("b p n -> p b n").bitcast(I32))
+        nc.sync.dma_start(wv_codes[:].bitcast(I32), wv_words.rearrange("b p n -> p b n").bitcast(I32))
         for r in range(4):
-            nc.sync.dma_start(wvs[r:P:32, :, :], wv_scales[:, r:16:4, :].rearrange("b q n -> q b n").bitcast(I32))
-        with nc.allow_non_contiguous_dma(reason="one value a partition"):
-            nc.sync.dma_start(bg_t[:], bg.rearrange("(c p) -> p c", p=P))
+            rows = wv_scales[:, r:BLOCKS:4, :].rearrange("b q n -> q b n")
+            nc.sync.dma_start(wv_rows[r:P:QUAD, :, :], rows.bitcast(I32))
+        with nc.allow_non_contiguous_dma(reason="the bias lies one value a partition"):
+            nc.sync.dma_start(bg_raw[:], bg.rearrange("(c p) -> p c", p=P))
         load_wg(0, 1)
         load_wg(1, 1)
-        bg_h = keep.tile([P, NT], F32, name="bg_h")
-        nc.gpsimd.tensor_scalar(bg_h[:], bg_t[:], 0.5, 0.0, ALU.mult, ALU.add)
-        gather_tab(1)
-        gather_tab2(0, 0)
-        permute_tab(1, 0)
-        gather_tab2(1, 0)
-        permute_tab(0, 1)
-        permute_tab(1, 1)
-        gather_tab2(0, 1)
-        gather_tab2(1, 1)
+        bg_half = keep.tile([P, N // P], F32, name="bg_half")
+        nc.gpsimd.tensor_scalar(bg_half[:], bg_raw[:], 0.5, 0.0, ALU.mult, ALU.add)
 
-        def score(b, c):
-            for a in range(KP):
-                score_pass(a, b, c)
+        for b in range(IG):
+            gather_v(1, b)
+        for h in range(2):
+            for a in range(KG):
+                gather_v2(a, h)
 
-        for b in range(SP):
-            for c in range(2):
-                score(b, c)
+        order = [(b, 2 * h + e) for h in range(2) for b in range(IG) for e in range(2)]
+        score_bank = {}
 
-        h16 = [keep.tile([P, S2, PACK], BF16, name=f"h16{b}", align_bytes=64) for b in range(SP)]
-        hq = [keep.tile([P, S2], U32, name=f"hq{b}", align_bytes=64) for b in range(SP)]
-        hs = [keep.tile([P, S2], U8, name=f"hs{b}", align_bytes=64) for b in range(SP)]
-        slots = {(0, 0): "wg16", (1, 0): "gw11", (0, 1): "gw211", (1, 1): "gw01"}
-        wg16 = {
-            key: keep.tile([P, NH, PACK], BF16, name=f"wg16{key[0]}{key[1]}", tag=slot, align_bytes=64)
-            for key, slot in slots.items()
+        def score(step):
+            b, c = order[step]
+            bank = psum.tile([P, PACK, JQ], F32, name=f"score{step}", tag=f"bank{step % SCORE_BANKS}")
+            score_bank[step] = bank
+            for a in range(KG):
+                scale_bytes = scales[a][:].bitcast(U8)
+                for t in range(PACK):
+                    column = b * GROUP + t * P
+                    nc.tensor.matmul_mx(
+                        out=bank[:, t, :],
+                        lhsT=v_codes[a][b][:, t * P : (t + 1) * P].bitcast(FP8X4),
+                        lhsT_scale=scale_bytes[4 * a : P, column : column + P],
+                        rhs=v2_codes[a][c // 2][:, (c % 2) * JQ : (c % 2 + 1) * JQ].bitcast(FP8X4),
+                        rhs_scale=scale_bytes[4 * a : P, S + c * JQ : S + (c + 1) * JQ],
+                        start=(a == 0 and t == 0),
+                        stop=(a == KG - 1 and t == PACK - 1),
+                    )
+
+        for step in range(SCORE_BANKS):
+            score(step)
+
+        h_bf16 = [keep.tile([P, S2, PACK], BF16, name=f"h_bf16{b}", align_bytes=ALIGN) for b in range(IG)]
+        h_codes = [keep.tile([P, S2], U32, name=f"h_codes{b}", align_bytes=ALIGN) for b in range(IG)]
+        h_scales = [keep.tile([P, S2], U8, name=f"h_scales{b}", align_bytes=ALIGN) for b in range(IG)]
+        slots = {(0, 0): "wg_bf16", (1, 0): "v_codes11", (0, 1): "v2_codes11", (1, 1): "v_codes01"}
+        wg_bf16 = {
+            (b, u): keep.tile([P, NH, PACK], BF16, name=f"wg_bf16{b}{u}", tag=slot, align_bytes=ALIGN)
+            for (b, u), slot in slots.items()
         }
-        wq = [keep.tile([P, N], U32, name=f"wq{b}", align_bytes=64) for b in range(SP)]
-        ws = [keep.tile([P, N], U8, name=f"ws{b}", align_bytes=64) for b in range(SP)]
+        wg_codes = [keep.tile([P, N], U32, name=f"wg_codes{b}", align_bytes=ALIGN) for b in range(IG)]
+        wg_scales = [keep.tile([P, N], U8, name=f"wg_scales{b}", align_bytes=ALIGN) for b in range(IG)]
 
-        def bound(b, c):
-            th = ring.tile([P, JC, PACK], F32, name="th")
-            nc.scalar.activation(th[:], banks[b, c][:].rearrange("p t j -> p j t"), ACT.Tanh)
-            nc.vector.tensor_tensor(
-                h16[b][:, c * JC : (c + 1) * JC, :],
-                th[:],
-                rw_h[:, b, :].unsqueeze(1).to_broadcast([P, JC, PACK]),
+        def bound(step):
+            b, c = order[step]
+            tanh_a = ring.tile([P, JQ, PACK], F32, name="tanh_a")
+            nc.scalar.activation(tanh_a[:], score_bank[step][:].rearrange("p t j -> p j t"), ACT.Tanh)
+            nc.vector.scalar_tensor_tensor(
+                h_bf16[b][:, c * JQ : (c + 1) * JQ, :],
+                tanh_a[:],
+                0.5,
+                rw_col[:, b, :].unsqueeze(1).to_broadcast([P, JQ, PACK]),
+                ALU.mult,
                 ALU.mult,
             )
 
-        JH = S2 // 2
+        def quantize(codes, scale_bytes, values):
+            nc.vector.quantize_mx(out=codes.bitcast(FP8X4), scales=scale_bytes, in_=values.rearrange("p n t -> p (n t)"))
 
-        def quant(codes, scales, src, lo, hi):
-            nc.vector.quantize_mx(
-                out=codes[:, lo:hi].bitcast(FP8X4),
-                scales=scales[:, lo:hi],
-                in_=src.rearrange("p n t -> p (n t)"),
-            )
+        def quantize_h(b, h):
+            sites = slice(h * JH, (h + 1) * JH)
+            quantize(h_codes[b][:, sites], h_scales[b][:, sites], h_bf16[b][:, sites, :])
 
-        def quant_h(b, h):
-            quant(hq[b], hs[b], h16[b][:, h * JH : (h + 1) * JH, :], h * JH, (h + 1) * JH)
+        def quantize_wg(b, u):
+            features = slice(u * NH, (u + 1) * NH)
+            quantize(wg_codes[b][:, features], wg_scales[b][:, features], wg_bf16[b, u][:])
 
-        def quant_wg(b, u):
-            quant(wq[b], ws[b], wg16[b, u][:], u * NH, (u + 1) * NH)
-
-        def wg_views(b, u, lo=0, hi=NH):
-            return (
-                wg16[b, u][:, lo:hi, :].rearrange("p (c i) t -> p c t i", i=4),
+        def cast_wg(copy, b, u, lo, hi):
+            copy(
+                wg_bf16[b, u][:, lo:hi, :].rearrange("p (c i) t -> p c t i", i=4),
                 wg_raw[b, u][:, :, lo:hi].rearrange("p t (c i) -> p c t i", i=4),
             )
 
-        wvs8 = wvs[:].bitcast(U8)
+        wv_scale_bytes = wv_rows[:].bitcast(U8)
         feat = {}
         gate = {}
 
@@ -221,82 +231,79 @@ def tile_list_residue_pocket_gate_kernel(
                 feat[h, u] = psum.tile([P, 2, JH], F32, name=f"feat{h}{u}", tag=f"bank{4 * (1 - h) + u}")
             for e in range(2):
                 n = 2 * u + e
-                for q in range(2):
-                    cols = slice(h * JH + q * JC, h * JH + (q + 1) * JC)
+                for q in range(JH // JQ):
+                    sites = slice(h * JH + q * JQ, h * JH + (q + 1) * JQ)
                     nc.tensor.matmul_mx(
-                        out=feat[h, u][:, e, q * JC : (q + 1) * JC],
-                        lhsT=wvw[:, b, 2 * P * n : 2 * P * (n + 1)].bitcast(FP4X4),
-                        lhsT_scale=wvs8[:, b, P * n : P * (n + 1)],
-                        rhs=hq[b][:, cols].bitcast(FP8X4),
-                        rhs_scale=hs[b][:, cols],
+                        out=feat[h, u][:, e, q * JQ : (q + 1) * JQ],
+                        lhsT=wv_codes[:, b, 2 * P * n : 2 * P * (n + 1)].bitcast(FP4X4),
+                        lhsT_scale=wv_scale_bytes[:, b, P * n : P * (n + 1)],
+                        rhs=h_codes[b][:, sites].bitcast(FP8X4),
+                        rhs_scale=h_scales[b][:, sites],
                         start=(b == 0 and e == 0 and q == 0),
-                        stop=(b == SP - 1 and e == 1 and q == 1),
+                        stop=(b == IG - 1 and e == 1 and q == JH // JQ - 1),
                     )
 
         def gate_pass(b, h, u):
             if b == 0:
                 gate[h, u] = psum.tile([P, 2, JH], F32, name=f"gate{h}{u}", tag=f"bank{4 * (1 - h) + 2 + u}")
-            cols = slice(h * JH, (h + 1) * JH)
+            sites = slice(h * JH, (h + 1) * JH)
             for e in range(2):
                 n = 2 * u + e
                 nc.tensor.matmul_mx(
                     out=gate[h, u][:, e, :],
-                    lhsT=wq[b][:, P * n : P * (n + 1)].bitcast(FP8X4),
-                    lhsT_scale=ws[b][:, P * n : P * (n + 1)],
-                    rhs=hq[b][:, cols].bitcast(FP8X4),
-                    rhs_scale=hs[b][:, cols],
+                    lhsT=wg_codes[b][:, P * n : P * (n + 1)].bitcast(FP8X4),
+                    lhsT_scale=wg_scales[b][:, P * n : P * (n + 1)],
+                    rhs=h_codes[b][:, sites].bitcast(FP8X4),
+                    rhs_scale=h_scales[b][:, sites],
                     start=(b == 0 and e == 0),
-                    stop=(b == SP - 1 and e == 1),
+                    stop=(b == IG - 1 and e == 1),
                 )
 
         def finish(h, u, parts):
-            th2 = ring.tile([P, 2, JH], F32, name="th2", bufs=4)
-            res = ring.tile([P, 2, JH], F32, name="res", bufs=4)
+            tanh_g = ring.tile([P, 2, JH], F32, name="tanh_g", bufs=4)
+            result = ring.tile([P, 2, JH], F32, name="result", bufs=4)
             rows = out[u * NH : (u + 1) * NH, h * JH : (h + 1) * JH].rearrange("(e p) j -> p e j", p=P)
             for e in range(2):
                 n = 2 * u + e
-                nc.scalar.activation(th2[:, e, :], gate[h, u][:, e, :], ACT.Tanh, bias=bg_h[:, n : n + 1])
+                nc.scalar.activation(tanh_g[:, e, :], gate[h, u][:, e, :], ACT.Tanh, bias=bg_half[:, n : n + 1])
             for part in parts:
-                nc.vector.scalar_tensor_tensor(res[:, part, :], th2[:, part, :], 1.0, feat[h, u][:, part, :], ALU.add, ALU.mult)
-                nc.sync.dma_start(rows[:, part, :], res[:, part, :])
+                nc.vector.scalar_tensor_tensor(
+                    result[:, part, :], tanh_g[:, part, :], 1.0, feat[h, u][:, part, :], ALU.add, ALU.mult
+                )
+                nc.sync.dma_start(rows[:, part, :], result[:, part, :])
+
+        cast_wg(nc.vector.tensor_copy, 0, 0, 0, NH)
+        for step in range(len(order)):
+            bound(step)
+            if step + SCORE_BANKS < len(order):
+                score(step + SCORE_BANKS)
+            if step == 0:
+                quantize_wg(0, 0)
+            elif step % 2 == 0:
+                b, c = order[step - 1]
+                quantize_h(b, c // 2)
+
+        cast_wg(nc.scalar.copy, 1, 0, 0, NH)
+        cast_wg(nc.scalar.copy, 0, 1, 0, NH)
+        cast_wg(nc.scalar.copy, 1, 1, 0, NH - P)
+        quantize_wg(1, 0)
+        quantize_h(1, 1)
+        cast_wg(nc.vector.tensor_copy, 1, 1, NH - P, NH)
+        quantize_wg(0, 1)
+        quantize_wg(1, 1)
 
         whole = [slice(0, 2)]
         halves = [slice(0, 1), slice(1, 2)]
-        nc.scalar.copy(*wg_views(0, 0))
-        bound(0, 0)
-        score(0, 2)
-        quant_wg(0, 0)
-        bound(0, 1)
-        score(0, 3)
-        bound(1, 0)
-        score(1, 2)
-        quant_h(0, 0)
-        bound(1, 1)
-        score(1, 3)
-        bound(0, 2)
-        quant_h(1, 0)
-        bound(0, 3)
-        bound(1, 2)
-        quant_h(0, 1)
-        bound(1, 3)
-        nc.scalar.copy(*wg_views(1, 0))
-        nc.scalar.copy(*wg_views(0, 1))
-        nc.scalar.copy(*wg_views(1, 1, 0, P))
-        quant_wg(1, 0)
-        quant_h(1, 1)
-        nc.vector.tensor_copy(*wg_views(1, 1, P, NH))
-        quant_wg(0, 1)
-        quant_wg(1, 1)
-        for b in range(SP):
+        for b in range(IG):
             for u in range(2):
                 feat_pass(b, 0, u)
-        for b in range(SP):
+        for b in range(IG):
             gate_pass(b, 0, 0)
         finish(0, 0, whole)
         for u in range(2):
             feat_pass(0, 1, u)
-        gate_pass(0, 1, 0)
-        gate_pass(1, 1, 0)
+        for b in range(IG):
+            gate_pass(b, 1, 0)
         feat_pass(1, 1, 0)
         finish(1, 0, whole)
         feat_pass(1, 1, 1)

@@ -27,19 +27,22 @@ LIST = 16
 JQ = 128
 JH = S2 // 2
 NH = N // 2
-ROWS_AT = P - KG * BLOCKS
-SCORE_BANKS = 3
+ROWS = KG * BLOCKS
+ROWS_AT = 64
+FEAT_BANK = (4, 5, 6, 7)
+GATE_BANK = (0, 1, 2, 3)
 ALIGN = 64
 
 WG_BYTES = 4 * PACK * NH
-V_WORDS_AT = 0
-WG_AT = {(0, 0): 0, (1, 0): WG_BYTES, (0, 1): 2 * WG_BYTES, (1, 1): 4 * T - ALIGN}
+V0_AT = WG_BYTES - ALIGN
+WG_AT = {(0, 0): 0, (1, 0): WG_BYTES, (0, 1): 2 * WG_BYTES, (1, 1): V0_AT + 4 * T - ALIGN}
 WV_WORDS_AT = 3 * WG_BYTES
 WV_SCALES_AT = WV_WORDS_AT + IG * 2 * N
 BG_AT = WV_SCALES_AT + IG * N
 RW_AT = BG_AT + ALIGN
-V2_WORDS_AT = [4 * T + WG_BYTES + a * 4 * T2 for a in range(KG)]
+V2_WORDS_AT = [WG_AT[1, 1] + WG_BYTES + a * 4 * T2 for a in range(KG)]
 V_PICKED_SCALES_AT = V2_WORDS_AT[1] - S // 2
+SCORE_BANKS = 4
 
 
 def tile_list_residue_pocket_gate_kernel(
@@ -56,30 +59,30 @@ def tile_list_residue_pocket_gate_kernel(
         idx2 = keep.tile([P, S2 // LIST], U16, name="idx2")
         v_rows = keep.tile([P, T // 4], I32, name="v_rows", align_bytes=ALIGN)
         v2_rows = keep.tile([P, T2 // 4], I32, name="v2_rows", align_bytes=ALIGN)
-        scales = [keep.tile([P, (S + S2) // 4], I32, name=f"scales{a}", align_bytes=ALIGN) for a in range(KG)]
+        scales = keep.tile([P, (S + S2) // 4], I32, name="scales", align_bytes=ALIGN)
         v_words = [
-            shared.tile([P, T], I32, name="v_words0", align_bytes=ALIGN, offset=V_WORDS_AT),
+            shared.tile([P, T], I32, name="v_words0", align_bytes=ALIGN, offset=V0_AT),
             keep.tile([P, T], I32, name="v_words1", align_bytes=ALIGN),
         ]
         v2_words = [
             shared.tile([P, T2], I32, name=f"v2_words{a}", align_bytes=ALIGN, offset=V2_WORDS_AT[a]) for a in range(KG)
         ]
 
-        nc.vector.memset(v2_rows[0:ROWS_AT, :], 0)
-        nc.gpsimd.memset(v_rows[0:ROWS_AT, :], 0)
-        for a in range(KG):
-            nc.gpsimd.memset(scales[a][:], 0)
+        for others in (slice(0, ROWS_AT), slice(ROWS_AT + ROWS, P)):
+            nc.vector.memset(v2_rows[others, :], 0)
+            nc.gpsimd.memset(v_rows[others, :], 0)
 
-        nc.sync.dma_start(v2_rows[ROWS_AT:P, :], tab2_scales.rearrange("a q t -> (a q) t").bitcast(I32))
+        loaded = slice(ROWS_AT, ROWS_AT + ROWS)
+        nc.sync.dma_start(v2_rows[loaded, :], tab2_scales.rearrange("a q t -> q a t").bitcast(I32))
         nc.sync.dma_start(idx2[:], offs2)
-        nc.sync.dma_start(v_rows[ROWS_AT:P, :], tab_scales.rearrange("a q t -> (a q) t").bitcast(I32))
+        nc.sync.dma_start(v_rows[loaded, :], tab_scales.rearrange("a q t -> q a t").bitcast(I32))
         nc.sync.dma_start(idx[:], offs)
 
         def load_words(tile, source):
             nc.sync.dma_start(tile[:], source.rearrange("p n t -> p (n t)").bitcast(I32))
 
-        for a in range(KG):
-            load_words(v_words[a], tab_words[a])
+        load_words(v_words[0], tab_words[0])
+        load_words(v_words[1], tab_words[1])
 
         v_picked = shared.tile([P, S], U8, name="v_picked", align_bytes=ALIGN, offset=V_PICKED_SCALES_AT)
         v2_picked = keep.tile([P, S2], U8, name="v2_picked", align_bytes=ALIGN)
@@ -92,10 +95,10 @@ def tile_list_residue_pocket_gate_kernel(
             staged[:, 0:S].rearrange("p (b t m) -> p b t m", b=IG, t=PACK),
             v_picked[:].rearrange("p (b m t) -> p b t m", b=IG, t=PACK),
         )
+        for r in range(4):
+            first = ROWS_AT + KG * r
+            nc.sync.dma_start(scales[r:P:4, :], staged32[first : first + ROWS, :])
         for a in range(KG):
-            first = ROWS_AT + BLOCKS * a
-            for r in range(4):
-                nc.sync.dma_start(scales[a][4 * a + r : P : QUAD, :], staged32[first + r : first + BLOCKS : 4, :])
             load_words(v2_words[a], tab2_words[a])
 
         v_codes = [
@@ -137,8 +140,8 @@ def tile_list_residue_pocket_gate_kernel(
             nc.sync.dma_start(wg_raw[b, u][:], rows.rearrange("(p t) n -> p t n", t=PACK))
 
         nc.vector.memset(wv_rows[:], 0)
-        load_wg(0, 0)
         nc.sync.dma_start(rw_col[:], rw.rearrange("(b p t) -> p b t", b=IG, t=PACK))
+        load_wg(0, 0)
         load_wg(1, 0)
         nc.sync.dma_start(wv_codes[:].bitcast(I32), wv_words.rearrange("b p n -> p b n").bitcast(I32))
         for r in range(4):
@@ -153,38 +156,50 @@ def tile_list_residue_pocket_gate_kernel(
 
         for b in range(IG):
             gather_v(1, b)
-        for h in range(2):
-            for a in range(KG):
+        for a in range(KG):
+            for h in range(2):
                 gather_v2(a, h)
 
-        order = [(b, 2 * h + e) for h in range(2) for b in range(IG) for e in range(2)]
+        warm = psum.tile([P, GROUP], F32, name="warm", tag="bank7")
+        for step in range(3):
+            nc.tensor.matmul_mx(
+                out=warm[:],
+                lhsT=v_codes[0][0][:, 0:P].bitcast(FP8X4),
+                lhsT_scale=staged[:, 0:P],
+                rhs=v_codes[1][0][:].bitcast(FP8X4),
+                rhs_scale=staged[:, 0:GROUP],
+                start=True,
+                stop=True,
+            )
+
+        order = [(b, c) for b in range(IG) for c in range(S2 // JQ)]
         score_bank = {}
 
-        def score(step):
+        def score(step, a):
             b, c = order[step]
-            bank = psum.tile([P, PACK, JQ], F32, name=f"score{step}", tag=f"bank{step % SCORE_BANKS}")
-            score_bank[step] = bank
-            for a in range(KG):
-                scale_bytes = scales[a][:].bitcast(U8)
-                for t in range(PACK):
-                    column = b * GROUP + t * P
-                    nc.tensor.matmul_mx(
-                        out=bank[:, t, :],
-                        lhsT=v_codes[a][b][:, t * P : (t + 1) * P].bitcast(FP8X4),
-                        lhsT_scale=scale_bytes[4 * a : P, column : column + P],
-                        rhs=v2_codes[a][c // 2][:, (c % 2) * JQ : (c % 2 + 1) * JQ].bitcast(FP8X4),
-                        rhs_scale=scale_bytes[4 * a : P, S + c * JQ : S + (c + 1) * JQ],
-                        start=(a == 0 and t == 0),
-                        stop=(a == KG - 1 and t == PACK - 1),
-                    )
+            if a == 0:
+                score_bank[step] = psum.tile([P, PACK, JQ], F32, name=f"score{step}", tag=f"bank{step % SCORE_BANKS}")
+            scale_bytes = scales[:].bitcast(U8)
+            for t in range(PACK):
+                column = b * GROUP + t * P
+                nc.tensor.matmul_mx(
+                    out=score_bank[step][:, t, :],
+                    lhsT=v_codes[a][b][:, t * P : (t + 1) * P].bitcast(FP8X4),
+                    lhsT_scale=scale_bytes[4 * a : P, column : column + P],
+                    rhs=v2_codes[a][c // 2][:, (c % 2) * JQ : (c % 2 + 1) * JQ].bitcast(FP8X4),
+                    rhs_scale=scale_bytes[4 * a : P, S + c * JQ : S + (c + 1) * JQ],
+                    start=(a == 0 and t == 0),
+                    stop=(a == KG - 1 and t == PACK - 1),
+                )
 
-        for step in range(SCORE_BANKS):
-            score(step)
+        for a in range(KG):
+            for step in range(SCORE_BANKS):
+                score(step, a)
 
         h_bf16 = [keep.tile([P, S2, PACK], BF16, name=f"h_bf16{b}", align_bytes=ALIGN) for b in range(IG)]
         h_codes = [keep.tile([P, S2], U32, name=f"h_codes{b}", align_bytes=ALIGN) for b in range(IG)]
         h_scales = [keep.tile([P, S2], U8, name=f"h_scales{b}", align_bytes=ALIGN) for b in range(IG)]
-        slots = {(0, 0): "wg_bf16", (1, 0): "v_codes11", (0, 1): "v2_codes11", (1, 1): "v_codes01"}
+        slots = {(0, 0): "wg_bf16", (1, 0): "v_codes11", (0, 1): "v2_codes11", (1, 1): "v_codes10"}
         wg_bf16 = {
             (b, u): keep.tile([P, NH, PACK], BF16, name=f"wg_bf16{b}{u}", tag=slot, align_bytes=ALIGN)
             for (b, u), slot in slots.items()
@@ -226,90 +241,80 @@ def tile_list_residue_pocket_gate_kernel(
         feat = {}
         gate = {}
 
-        def feat_pass(b, h, u):
+        def feat_pass(b, n, lo, hi):
             if b == 0:
-                feat[h, u] = psum.tile([P, 2, JH], F32, name=f"feat{h}{u}", tag=f"bank{4 * (1 - h) + u}")
-            for e in range(2):
-                n = 2 * u + e
-                for q in range(JH // JQ):
-                    sites = slice(h * JH + q * JQ, h * JH + (q + 1) * JQ)
-                    nc.tensor.matmul_mx(
-                        out=feat[h, u][:, e, q * JQ : (q + 1) * JQ],
-                        lhsT=wv_codes[:, b, 2 * P * n : 2 * P * (n + 1)].bitcast(FP4X4),
-                        lhsT_scale=wv_scale_bytes[:, b, P * n : P * (n + 1)],
-                        rhs=h_codes[b][:, sites].bitcast(FP8X4),
-                        rhs_scale=h_scales[b][:, sites],
-                        start=(b == 0 and e == 0 and q == 0),
-                        stop=(b == IG - 1 and e == 1 and q == JH // JQ - 1),
-                    )
+                feat[n] = psum.tile([P, S2], F32, name=f"feat{n}", tag=f"bank{FEAT_BANK[n]}")
+            nc.tensor.matmul_mx(
+                out=feat[n][:, lo:hi],
+                lhsT=wv_codes[:, b, 2 * P * n : 2 * P * (n + 1)].bitcast(FP4X4),
+                lhsT_scale=wv_scale_bytes[:, b, P * n : P * (n + 1)],
+                rhs=h_codes[b][:, lo:hi].bitcast(FP8X4),
+                rhs_scale=h_scales[b][:, lo:hi],
+                start=(b == 0),
+                stop=(b == IG - 1 and hi == S2),
+            )
 
-        def gate_pass(b, h, u):
+        def gate_pass(b, n, lo, hi):
             if b == 0:
-                gate[h, u] = psum.tile([P, 2, JH], F32, name=f"gate{h}{u}", tag=f"bank{4 * (1 - h) + 2 + u}")
-            sites = slice(h * JH, (h + 1) * JH)
-            for e in range(2):
-                n = 2 * u + e
-                nc.tensor.matmul_mx(
-                    out=gate[h, u][:, e, :],
-                    lhsT=wg_codes[b][:, P * n : P * (n + 1)].bitcast(FP8X4),
-                    lhsT_scale=wg_scales[b][:, P * n : P * (n + 1)],
-                    rhs=h_codes[b][:, sites].bitcast(FP8X4),
-                    rhs_scale=h_scales[b][:, sites],
-                    start=(b == 0 and e == 0),
-                    stop=(b == IG - 1 and e == 1),
-                )
+                gate[n] = psum.tile([P, S2], F32, name=f"gate{n}", tag=f"bank{GATE_BANK[n]}")
+            nc.tensor.matmul_mx(
+                out=gate[n][:, lo:hi],
+                lhsT=wg_codes[b][:, P * n : P * (n + 1)].bitcast(FP8X4),
+                lhsT_scale=wg_scales[b][:, P * n : P * (n + 1)],
+                rhs=h_codes[b][:, lo:hi].bitcast(FP8X4),
+                rhs_scale=h_scales[b][:, lo:hi],
+                start=(b == 0),
+                stop=(b == IG - 1 and hi == S2),
+            )
 
-        def finish(h, u, parts):
-            tanh_g = ring.tile([P, 2, JH], F32, name="tanh_g", bufs=4)
-            result = ring.tile([P, 2, JH], F32, name="result", bufs=4)
-            rows = out[u * NH : (u + 1) * NH, h * JH : (h + 1) * JH].rearrange("(e p) j -> p e j", p=P)
-            for e in range(2):
-                n = 2 * u + e
-                nc.scalar.activation(tanh_g[:, e, :], gate[h, u][:, e, :], ACT.Tanh, bias=bg_half[:, n : n + 1])
+        def finish(n, parts):
+            tanh_g = ring.tile([P, S2], F32, name="tanh_g", bufs=4)
+            result = ring.tile([P, S2], F32, name="result", bufs=4)
+            for part in parts:
+                nc.scalar.activation(tanh_g[:, part], gate[n][:, part], ACT.Tanh, bias=bg_half[:, n : n + 1])
             for part in parts:
                 nc.vector.scalar_tensor_tensor(
-                    result[:, part, :], tanh_g[:, part, :], 1.0, feat[h, u][:, part, :], ALU.add, ALU.mult
+                    result[:, part], tanh_g[:, part], 1.0, feat[n][:, part], ALU.add, ALU.mult
                 )
-                nc.sync.dma_start(rows[:, part, :], result[:, part, :])
+                nc.sync.dma_start(out[n * P : (n + 1) * P, part], result[:, part])
 
         cast_wg(nc.vector.tensor_copy, 0, 0, 0, NH)
+        quantize_wg(0, 0)
         for step in range(len(order)):
             bound(step)
             if step + SCORE_BANKS < len(order):
-                score(step + SCORE_BANKS)
-            if step == 0:
-                quantize_wg(0, 0)
-            elif step % 2 == 0:
+                for a in range(KG):
+                    score(step + SCORE_BANKS, a)
+            if step > 0 and step % 2 == 0:
                 b, c = order[step - 1]
                 quantize_h(b, c // 2)
 
         cast_wg(nc.scalar.copy, 1, 0, 0, NH)
         cast_wg(nc.scalar.copy, 0, 1, 0, NH)
-        cast_wg(nc.scalar.copy, 1, 1, 0, NH - P)
         quantize_wg(1, 0)
         quantize_h(1, 1)
-        cast_wg(nc.vector.tensor_copy, 1, 1, NH - P, NH)
+        cast_wg(nc.vector.tensor_copy, 1, 1, 0, NH)
         quantize_wg(0, 1)
         quantize_wg(1, 1)
 
-        whole = [slice(0, 2)]
-        halves = [slice(0, 1), slice(1, 2)]
+        for n in range(N // P):
+            feat_pass(0, n, 0, S2)
+        for n in range(2):
+            gate_pass(0, n, 0, S2)
+        for n in range(N // P):
+            for lo in range(0, JH, JQ):
+                feat_pass(1, n, lo, lo + JQ)
+        for n in range(2):
+            gate_pass(1, n, 0, JH)
+        whole = [slice(0, S2)]
+        halves = [slice(0, JH), slice(JH, S2)]
+        for n in range(2):
+            gate_pass(1, n, JH, S2)
+        for n in range(N // P):
+            for lo in range(JH, S2, JQ):
+                feat_pass(1, n, lo, lo + JQ)
         for b in range(IG):
-            for u in range(2):
-                feat_pass(b, 0, u)
-        for b in range(IG):
-            gate_pass(b, 0, 0)
-        finish(0, 0, whole)
-        for u in range(2):
-            feat_pass(0, 1, u)
-        for b in range(IG):
-            gate_pass(b, 1, 0)
-        feat_pass(1, 1, 0)
-        finish(1, 0, whole)
-        feat_pass(1, 1, 1)
-        for h in range(2):
-            gate_pass(0, h, 1)
-        gate_pass(1, 0, 1)
-        finish(0, 1, whole)
-        gate_pass(1, 1, 1)
-        finish(1, 1, halves)
+            for n in range(2, N // P):
+                gate_pass(b, n, 0, S2)
+        for n in range(N // P):
+            finish(n, halves if n == N // P - 1 else whole)

@@ -147,10 +147,10 @@ def tile_list_residue_pocket_gate_kernel(
         for r in range(4):
             rows = wv_scales[:, r:BLOCKS:4, :].rearrange("b q n -> q b n")
             nc.sync.dma_start(wv_rows[r:P:QUAD, :, :], rows.bitcast(I32))
-        with nc.allow_non_contiguous_dma(reason="the bias lies one value a partition"):
-            nc.sync.dma_start(bg_raw[:], bg.rearrange("(c p) -> p c", p=P))
         load_wg(0, 1)
         load_wg(1, 1)
+        with nc.allow_non_contiguous_dma(reason="the bias lies one value a partition"):
+            nc.sync.dma_start(bg_raw[:], bg.rearrange("(c p) -> p c", p=P))
         bg_half = keep.tile([P, N // P], F32, name="bg_half")
         nc.gpsimd.tensor_scalar(bg_half[:], bg_raw[:], 0.5, 0.0, ALU.mult, ALU.add)
 
@@ -159,18 +159,6 @@ def tile_list_residue_pocket_gate_kernel(
         for a in range(KG):
             for h in range(2):
                 gather_v2(a, h)
-
-        warm = psum.tile([P, GROUP], F32, name="warm", tag="bank7")
-        for step in range(3):
-            nc.tensor.matmul_mx(
-                out=warm[:],
-                lhsT=v_codes[0][0][:, 0:P].bitcast(FP8X4),
-                lhsT_scale=staged[:, 0:P],
-                rhs=v_codes[1][0][:].bitcast(FP8X4),
-                rhs_scale=staged[:, 0:GROUP],
-                start=True,
-                stop=True,
-            )
 
         order = [(b, c) for b in range(IG) for c in range(S2 // JQ)]
         score_bank = {}
@@ -291,9 +279,10 @@ def tile_list_residue_pocket_gate_kernel(
 
         cast_wg(nc.scalar.copy, 1, 0, 0, NH)
         cast_wg(nc.scalar.copy, 0, 1, 0, NH)
+        cast_wg(nc.scalar.copy, 1, 1, 0, P)
         quantize_wg(1, 0)
         quantize_h(1, 1)
-        cast_wg(nc.vector.tensor_copy, 1, 1, 0, NH)
+        cast_wg(nc.vector.tensor_copy, 1, 1, P, NH)
         quantize_wg(0, 1)
         quantize_wg(1, 1)
 

@@ -70,7 +70,7 @@ def tile_list_residue_pocket_gate_kernel(
 
         for others in (slice(0, ROWS_AT), slice(ROWS_AT + ROWS, P)):
             nc.vector.memset(v2_rows[others, :], 0)
-            nc.gpsimd.memset(v_rows[others, :], 0)
+            nc.vector.memset(v_rows[others, :], 0)
 
         loaded = slice(ROWS_AT, ROWS_AT + ROWS)
         nc.sync.dma_start(v2_rows[loaded, :], tab2_scales.rearrange("a q t -> q a t").bitcast(I32))
@@ -143,12 +143,12 @@ def tile_list_residue_pocket_gate_kernel(
         nc.sync.dma_start(rw_col[:], rw.rearrange("(b p t) -> p b t", b=IG, t=PACK))
         load_wg(0, 0)
         load_wg(1, 0)
+        load_wg(0, 1)
+        load_wg(1, 1)
         nc.sync.dma_start(wv_codes[:].bitcast(I32), wv_words.rearrange("b p n -> p b n").bitcast(I32))
         for r in range(4):
             rows = wv_scales[:, r:BLOCKS:4, :].rearrange("b q n -> q b n")
             nc.sync.dma_start(wv_rows[r:P:QUAD, :, :], rows.bitcast(I32))
-        load_wg(0, 1)
-        load_wg(1, 1)
         with nc.allow_non_contiguous_dma(reason="the bias lies one value a partition"):
             nc.sync.dma_start(bg_raw[:], bg.rearrange("(c p) -> p c", p=P))
         bg_half = keep.tile([P, N // P], F32, name="bg_half")
@@ -267,9 +267,10 @@ def tile_list_residue_pocket_gate_kernel(
                 nc.sync.dma_start(out[n * P : (n + 1) * P, part], result[:, part])
 
         cast_wg(nc.vector.tensor_copy, 0, 0, 0, NH)
-        quantize_wg(0, 0)
         for step in range(len(order)):
             bound(step)
+            if step == 0:
+                quantize_wg(0, 0)
             if step + SCORE_BANKS < len(order):
                 for a in range(KG):
                     score(step + SCORE_BANKS, a)

@@ -27,8 +27,7 @@ LIST = 16
 JQ = 128
 JH = S2 // 2
 NH = N // 2
-ROWS = KG * BLOCKS
-ROWS_AT = 64
+ROWS_AT = P - KG * BLOCKS
 FEAT_BANK = (4, 5, 6, 7)
 GATE_BANK = (0, 1, 2, 3)
 ALIGN = 64
@@ -43,6 +42,7 @@ RW_AT = BG_AT + ALIGN
 V2_WORDS_AT = [WG_AT[1, 1] + WG_BYTES + a * 4 * T2 for a in range(KG)]
 V_PICKED_SCALES_AT = V2_WORDS_AT[1] - S // 2
 SCORE_BANKS = 4
+CAST_SPLIT = 128
 
 
 def tile_list_residue_pocket_gate_kernel(
@@ -59,7 +59,7 @@ def tile_list_residue_pocket_gate_kernel(
         idx2 = keep.tile([P, S2 // LIST], U16, name="idx2")
         v_rows = keep.tile([P, T // 4], I32, name="v_rows", align_bytes=ALIGN)
         v2_rows = keep.tile([P, T2 // 4], I32, name="v2_rows", align_bytes=ALIGN)
-        scales = keep.tile([P, (S + S2) // 4], I32, name="scales", align_bytes=ALIGN)
+        scales = [keep.tile([P, (S + S2) // 4], I32, name=f"scales{a}", align_bytes=ALIGN) for a in range(KG)]
         v_words = [
             shared.tile([P, T], I32, name="v_words0", align_bytes=ALIGN, offset=V0_AT),
             keep.tile([P, T], I32, name="v_words1", align_bytes=ALIGN),
@@ -68,14 +68,14 @@ def tile_list_residue_pocket_gate_kernel(
             shared.tile([P, T2], I32, name=f"v2_words{a}", align_bytes=ALIGN, offset=V2_WORDS_AT[a]) for a in range(KG)
         ]
 
-        for others in (slice(0, ROWS_AT), slice(ROWS_AT + ROWS, P)):
-            nc.vector.memset(v2_rows[others, :], 0)
-            nc.vector.memset(v_rows[others, :], 0)
+        nc.vector.memset(v2_rows[0:ROWS_AT, :], 0)
+        nc.vector.memset(v_rows[0:ROWS_AT, :], 0)
+        for a in range(KG):
+            nc.gpsimd.memset(scales[a][:], 0)
 
-        loaded = slice(ROWS_AT, ROWS_AT + ROWS)
-        nc.sync.dma_start(v2_rows[loaded, :], tab2_scales.rearrange("a q t -> q a t").bitcast(I32))
+        nc.sync.dma_start(v2_rows[ROWS_AT:P, :], tab2_scales.rearrange("a q t -> (a q) t").bitcast(I32))
         nc.sync.dma_start(idx2[:], offs2)
-        nc.sync.dma_start(v_rows[loaded, :], tab_scales.rearrange("a q t -> q a t").bitcast(I32))
+        nc.sync.dma_start(v_rows[ROWS_AT:P, :], tab_scales.rearrange("a q t -> (a q) t").bitcast(I32))
         nc.sync.dma_start(idx[:], offs)
 
         def load_words(tile, source):
@@ -95,11 +95,15 @@ def tile_list_residue_pocket_gate_kernel(
             staged[:, 0:S].rearrange("p (b t m) -> p b t m", b=IG, t=PACK),
             v_picked[:].rearrange("p (b m t) -> p b t m", b=IG, t=PACK),
         )
-        for r in range(4):
-            first = ROWS_AT + KG * r
-            nc.sync.dma_start(scales[r:P:4, :], staged32[first : first + ROWS, :])
+        def move_scales(a):
+            first = ROWS_AT + BLOCKS * a
+            for r in range(4):
+                nc.sync.dma_start(scales[a][4 * a + r : P : QUAD, :], staged32[first + r : first + BLOCKS : 4, :])
+
+        move_scales(0)
         for a in range(KG):
             load_words(v2_words[a], tab2_words[a])
+        move_scales(1)
 
         v_codes = [
             [keep.tile([P, GROUP], U32, name=f"v_codes{a}{b}", tag=f"v_codes{a}{b}", align_bytes=ALIGN) for b in range(IG)]
@@ -143,12 +147,12 @@ def tile_list_residue_pocket_gate_kernel(
         nc.sync.dma_start(rw_col[:], rw.rearrange("(b p t) -> p b t", b=IG, t=PACK))
         load_wg(0, 0)
         load_wg(1, 0)
-        load_wg(0, 1)
-        load_wg(1, 1)
         nc.sync.dma_start(wv_codes[:].bitcast(I32), wv_words.rearrange("b p n -> p b n").bitcast(I32))
         for r in range(4):
             rows = wv_scales[:, r:BLOCKS:4, :].rearrange("b q n -> q b n")
             nc.sync.dma_start(wv_rows[r:P:QUAD, :, :], rows.bitcast(I32))
+        load_wg(0, 1)
+        load_wg(1, 1)
         with nc.allow_non_contiguous_dma(reason="the bias lies one value a partition"):
             nc.sync.dma_start(bg_raw[:], bg.rearrange("(c p) -> p c", p=P))
         bg_half = keep.tile([P, N // P], F32, name="bg_half")
@@ -167,7 +171,7 @@ def tile_list_residue_pocket_gate_kernel(
             b, c = order[step]
             if a == 0:
                 score_bank[step] = psum.tile([P, PACK, JQ], F32, name=f"score{step}", tag=f"bank{step % SCORE_BANKS}")
-            scale_bytes = scales[:].bitcast(U8)
+            scale_bytes = scales[a][:].bitcast(U8)
             for t in range(PACK):
                 column = b * GROUP + t * P
                 nc.tensor.matmul_mx(
@@ -211,13 +215,13 @@ def tile_list_residue_pocket_gate_kernel(
         def quantize(codes, scale_bytes, values):
             nc.vector.quantize_mx(out=codes.bitcast(FP8X4), scales=scale_bytes, in_=values.rearrange("p n t -> p (n t)"))
 
-        def quantize_h(b, h):
-            sites = slice(h * JH, (h + 1) * JH)
+        def quantize_h(b, lo, hi):
+            sites = slice(lo, hi)
             quantize(h_codes[b][:, sites], h_scales[b][:, sites], h_bf16[b][:, sites, :])
 
-        def quantize_wg(b, u):
-            features = slice(u * NH, (u + 1) * NH)
-            quantize(wg_codes[b][:, features], wg_scales[b][:, features], wg_bf16[b, u][:])
+        def quantize_wg(b, u, lo, hi):
+            features = slice(u * NH + lo, u * NH + hi)
+            quantize(wg_codes[b][:, features], wg_scales[b][:, features], wg_bf16[b, u][:, lo:hi, :])
 
         def cast_wg(copy, b, u, lo, hi):
             copy(
@@ -255,7 +259,7 @@ def tile_list_residue_pocket_gate_kernel(
                 stop=(b == IG - 1 and hi == S2),
             )
 
-        def finish(n, parts):
+        def finish(n, parts, stores):
             tanh_g = ring.tile([P, S2], F32, name="tanh_g", bufs=4)
             result = ring.tile([P, S2], F32, name="result", bufs=4)
             for part in parts:
@@ -264,28 +268,31 @@ def tile_list_residue_pocket_gate_kernel(
                 nc.vector.scalar_tensor_tensor(
                     result[:, part], tanh_g[:, part], 1.0, feat[n][:, part], ALU.add, ALU.mult
                 )
+            for part in stores:
                 nc.sync.dma_start(out[n * P : (n + 1) * P, part], result[:, part])
 
         cast_wg(nc.vector.tensor_copy, 0, 0, 0, NH)
         for step in range(len(order)):
             bound(step)
             if step == 0:
-                quantize_wg(0, 0)
+                quantize_wg(0, 0, 0, NH)
             if step + SCORE_BANKS < len(order):
                 for a in range(KG):
                     score(step + SCORE_BANKS, a)
-            if step > 0 and step % 2 == 0:
-                b, c = order[step - 1]
-                quantize_h(b, c // 2)
+            if order[step] == (1, 0):
+                quantize_h(0, 0, S2)
+            if order[step] == (1, 2):
+                quantize_h(1, 0, JH)
 
         cast_wg(nc.scalar.copy, 1, 0, 0, NH)
         cast_wg(nc.scalar.copy, 0, 1, 0, NH)
-        cast_wg(nc.scalar.copy, 1, 1, 0, P)
-        quantize_wg(1, 0)
-        quantize_h(1, 1)
-        cast_wg(nc.vector.tensor_copy, 1, 1, P, NH)
-        quantize_wg(0, 1)
-        quantize_wg(1, 1)
+        cast_wg(nc.scalar.copy, 1, 1, 0, CAST_SPLIT)
+        quantize_wg(1, 0, 0, NH)
+        quantize_h(1, JH, S2)
+        cast_wg(nc.vector.tensor_copy, 1, 1, CAST_SPLIT, NH)
+        quantize_wg(0, 1, 0, NH)
+        quantize_wg(1, 1, 0, P)
+        quantize_wg(1, 1, P, NH)
 
         for n in range(N // P):
             feat_pass(0, n, 0, S2)
@@ -301,10 +308,12 @@ def tile_list_residue_pocket_gate_kernel(
         for n in range(2):
             gate_pass(1, n, JH, S2)
         for n in range(N // P):
+            if n >= 2:
+                for b in range(IG):
+                    gate_pass(b, n, 0, S2)
             for lo in range(JH, S2, JQ):
                 feat_pass(1, n, lo, lo + JQ)
-        for b in range(IG):
-            for n in range(2, N // P):
-                gate_pass(b, n, 0, S2)
-        for n in range(N // P):
-            finish(n, halves if n == N // P - 1 else whole)
+        finish(0, halves, whole)
+        finish(1, whole, whole)
+        finish(2, whole, whole)
+        finish(3, halves, halves)

@@ -144,8 +144,8 @@ def tile_list_residue_pocket_gate_kernel(
             nc.sync.dma_start(wg_raw[b, u][:], rows.rearrange("(p t) n -> p t n", t=PACK))
 
         nc.vector.memset(wv_rows[:], 0)
-        nc.sync.dma_start(rw_col[:], rw.rearrange("(b p t) -> p b t", b=IG, t=PACK))
         load_wg(0, 0)
+        nc.sync.dma_start(rw_col[:], rw.rearrange("(b p t) -> p b t", b=IG, t=PACK))
         load_wg(1, 0)
         nc.sync.dma_start(wv_codes[:].bitcast(I32), wv_words.rearrange("b p n -> p b n").bitcast(I32))
         for r in range(4):
@@ -189,19 +189,19 @@ def tile_list_residue_pocket_gate_kernel(
                 score(step, a)
 
         h_bf16 = [keep.tile([P, S2, PACK], BF16, name=f"h_bf16{b}", align_bytes=ALIGN) for b in range(IG)]
-        h_codes = [keep.tile([P, S2], U32, name=f"h_codes{b}", align_bytes=ALIGN) for b in range(IG)]
+        h_codes = {1: keep.tile([P, S2], U32, name="h_codes1", align_bytes=ALIGN)}
         h_scales = [keep.tile([P, S2], U8, name=f"h_scales{b}", align_bytes=ALIGN) for b in range(IG)]
         slots = {(0, 0): "wg_bf16", (1, 0): "v_codes11", (0, 1): "v2_codes11", (1, 1): "v_codes10"}
         wg_bf16 = {
             (b, u): keep.tile([P, NH, PACK], BF16, name=f"wg_bf16{b}{u}", tag=slot, align_bytes=ALIGN)
             for (b, u), slot in slots.items()
         }
-        wg_codes = [keep.tile([P, N], U32, name=f"wg_codes{b}", align_bytes=ALIGN) for b in range(IG)]
+        wg_codes = {1: keep.tile([P, N], U32, name="wg_codes1", align_bytes=ALIGN)}
         wg_scales = [keep.tile([P, N], U8, name=f"wg_scales{b}", align_bytes=ALIGN) for b in range(IG)]
 
         def bound(step):
             b, c = order[step]
-            tanh_a = ring.tile([P, JQ, PACK], F32, name="tanh_a")
+            tanh_a = keep.tile([P, JQ, PACK], F32, name=f"tanh_a{step}", tag=f"tanh_a{step}", align_bytes=ALIGN)
             nc.scalar.activation(tanh_a[:], score_bank[step][:].rearrange("p t j -> p j t"), ACT.Tanh)
             nc.vector.scalar_tensor_tensor(
                 h_bf16[b][:, c * JQ : (c + 1) * JQ, :],
@@ -234,7 +234,7 @@ def tile_list_residue_pocket_gate_kernel(
         gate = {}
 
         def feat_pass(b, n, lo, hi):
-            if b == 0:
+            if n not in feat:
                 feat[n] = psum.tile([P, S2], F32, name=f"feat{n}", tag=f"bank{FEAT_BANK[n]}")
             nc.tensor.matmul_mx(
                 out=feat[n][:, lo:hi],
@@ -242,12 +242,12 @@ def tile_list_residue_pocket_gate_kernel(
                 lhsT_scale=wv_scale_bytes[:, b, P * n : P * (n + 1)],
                 rhs=h_codes[b][:, lo:hi].bitcast(FP8X4),
                 rhs_scale=h_scales[b][:, lo:hi],
-                start=(b == 0),
+                start=(b == 0 and lo == 0),
                 stop=(b == IG - 1 and hi == S2),
             )
 
         def gate_pass(b, n, lo, hi):
-            if b == 0:
+            if n not in gate:
                 gate[n] = psum.tile([P, S2], F32, name=f"gate{n}", tag=f"bank{GATE_BANK[n]}")
             nc.tensor.matmul_mx(
                 out=gate[n][:, lo:hi],
@@ -255,7 +255,7 @@ def tile_list_residue_pocket_gate_kernel(
                 lhsT_scale=wg_scales[b][:, P * n : P * (n + 1)],
                 rhs=h_codes[b][:, lo:hi].bitcast(FP8X4),
                 rhs_scale=h_scales[b][:, lo:hi],
-                start=(b == 0),
+                start=(b == 0 and lo == 0),
                 stop=(b == IG - 1 and hi == S2),
             )
 
@@ -275,12 +275,16 @@ def tile_list_residue_pocket_gate_kernel(
         for step in range(len(order)):
             bound(step)
             if step == 0:
+                wg_codes[0] = keep.tile([P, N], U32, name="wg_codes0", tag=f"tanh_a{step}", align_bytes=ALIGN)
                 quantize_wg(0, 0, 0, NH)
             if step + SCORE_BANKS < len(order):
                 for a in range(KG):
                     score(step + SCORE_BANKS, a)
+            if order[step] == (0, 2):
+                h_codes[0] = keep.tile([P, S2], U32, name="h_codes0", tag=f"tanh_a{step}", align_bytes=ALIGN)
+                quantize_h(0, 0, JH)
             if order[step] == (1, 0):
-                quantize_h(0, 0, S2)
+                quantize_h(0, JH, S2)
             if order[step] == (1, 2):
                 quantize_h(1, 0, JH)
 
@@ -294,10 +298,12 @@ def tile_list_residue_pocket_gate_kernel(
         quantize_wg(1, 1, 0, P)
         quantize_wg(1, 1, P, NH)
 
-        for n in range(N // P):
-            feat_pass(0, n, 0, S2)
-        for n in range(2):
-            gate_pass(0, n, 0, S2)
+        for half in range(0, S2, JH):
+            for n in range(2):
+                gate_pass(0, n, half, half + JH)
+            for n in range(N // P):
+                for lo in range(half, half + JH, JQ):
+                    feat_pass(0, n, lo, lo + JQ)
         for n in range(N // P):
             for lo in range(0, JH, JQ):
                 feat_pass(1, n, lo, lo + JQ)

@@ -42,6 +42,7 @@ RW_AT = BG_AT + ALIGN
 V2_WORDS_AT = [WG_AT[1, 1] + WG_BYTES + a * 4 * T2 for a in range(KG)]
 V_PICKED_SCALES_AT = V2_WORDS_AT[1] - S // 2
 SCORE_BANKS = 4
+EARLY = 2
 CAST_SPLIT = 128
 
 
@@ -169,7 +170,8 @@ def tile_list_residue_pocket_gate_kernel(
 
         def score(step, a):
             b, c = order[step]
-            if a == 0:
+            first = 1 if EARLY <= step < SCORE_BANKS else 0
+            if a == first:
                 score_bank[step] = psum.tile([P, PACK, JQ], F32, name=f"score{step}", tag=f"bank{step % SCORE_BANKS}")
             scale_bytes = scales[a][:].bitcast(U8)
             for t in range(PACK):
@@ -180,12 +182,15 @@ def tile_list_residue_pocket_gate_kernel(
                     lhsT_scale=scale_bytes[4 * a : P, column : column + P],
                     rhs=v2_codes[a][c // 2][:, (c % 2) * JQ : (c % 2 + 1) * JQ].bitcast(FP8X4),
                     rhs_scale=scale_bytes[4 * a : P, S + c * JQ : S + (c + 1) * JQ],
-                    start=(a == 0 and t == 0),
-                    stop=(a == KG - 1 and t == PACK - 1),
+                    start=(a == first and t == 0),
+                    stop=(a != first and t == PACK - 1),
                 )
 
         for a in range(KG):
-            for step in range(SCORE_BANKS):
+            for step in range(EARLY):
+                score(step, a)
+        for step in range(EARLY, SCORE_BANKS):
+            for a in reversed(range(KG)):
                 score(step, a)
 
         h_bf16 = [keep.tile([P, S2, PACK], BF16, name=f"h_bf16{b}", align_bytes=ALIGN) for b in range(IG)]

@@ -39,6 +39,7 @@ WV_WORDS_AT = 3 * WG_BYTES
 WV_SCALES_AT = WV_WORDS_AT + IG * 2 * N
 BG_AT = WV_SCALES_AT + IG * N
 RW_AT = BG_AT + ALIGN
+WG_FIRST_AT = [RW_AT + ALIGN + q * WG_BYTES // 2 for q in range(2)]
 V2_WORDS_AT = [WG_AT[1, 1] + WG_BYTES + a * 4 * T2 for a in range(KG)]
 V_PICKED_SCALES_AT = V2_WORDS_AT[1] - S // 2
 SCORE_BANKS = 4
@@ -134,7 +135,12 @@ def tile_list_residue_pocket_gate_kernel(
         wg_raw = {
             (b, u): shared.tile([P, PACK, NH], F32, name=f"wg_raw{b}{u}", align_bytes=ALIGN, offset=place)
             for (b, u), place in WG_AT.items()
+            if (b, u) != (0, 0)
         }
+        wg_first = [
+            shared.tile([P, PACK, P], F32, name=f"wg_first{q}", align_bytes=ALIGN, offset=place)
+            for q, place in enumerate(WG_FIRST_AT)
+        ]
         wv_codes = shared.tile([P, IG, 2 * N], U8, name="wv_codes", align_bytes=ALIGN, offset=WV_WORDS_AT)
         wv_rows = shared.tile([P, IG, N // 4], I32, name="wv_rows", align_bytes=ALIGN, offset=WV_SCALES_AT)
         bg_raw = shared.tile([P, N // P], F32, name="bg_raw", align_bytes=ALIGN, offset=BG_AT)
@@ -145,8 +151,11 @@ def tile_list_residue_pocket_gate_kernel(
             nc.sync.dma_start(wg_raw[b, u][:], rows.rearrange("(p t) n -> p t n", t=PACK))
 
         nc.vector.memset(wv_rows[:], 0)
-        load_wg(0, 0)
-        nc.sync.dma_start(rw_col[:], rw.rearrange("(b p t) -> p b t", b=IG, t=PACK))
+        for q in range(2):
+            rows = wg[0:GROUP, q * P : (q + 1) * P]
+            nc.sync.dma_start(wg_first[q][:], rows.rearrange("(p t) n -> p t n", t=PACK))
+            if q == 0:
+                nc.sync.dma_start(rw_col[:], rw.rearrange("(b p t) -> p b t", b=IG, t=PACK))
         load_wg(1, 0)
         nc.sync.dma_start(wv_codes[:].bitcast(I32), wv_words.rearrange("b p n -> p b n").bitcast(I32))
         for r in range(4):
@@ -276,12 +285,21 @@ def tile_list_residue_pocket_gate_kernel(
             for part in stores:
                 nc.sync.dma_start(out[n * P : (n + 1) * P, part], result[:, part])
 
-        cast_wg(nc.vector.tensor_copy, 0, 0, 0, NH)
+        def cast_first(q):
+            nc.vector.tensor_copy(
+                wg_bf16[0, 0][:, q * P : (q + 1) * P, :].rearrange("p (c i) t -> p c t i", i=4),
+                wg_first[q][:].rearrange("p t (c i) -> p c t i", i=4),
+            )
+
+        cast_first(0)
+        wg_codes[0] = keep.tile([P, N], U32, name="wg_codes0", align_bytes=ALIGN)
+        quantize_wg(0, 0, 0, P)
         for step in range(len(order)):
             bound(step)
             if step == 0:
-                wg_codes[0] = keep.tile([P, N], U32, name="wg_codes0", tag=f"tanh_a{step}", align_bytes=ALIGN)
-                quantize_wg(0, 0, 0, NH)
+                cast_first(1)
+            if step == 1:
+                quantize_wg(0, 0, P, NH)
             if step + SCORE_BANKS < len(order):
                 for a in range(KG):
                     score(step + SCORE_BANKS, a)

@@ -28,23 +28,21 @@ JQ = 128
 JH = S2 // 2
 NH = N // 2
 ROWS_AT = P - KG * BLOCKS
-FEAT_BANK = (4, 5, 6, 7)
-GATE_BANK = (0, 1, 2, 3)
 ALIGN = 64
+LINE = 4
+SCORE_BANKS = 4
+EARLY = 2
+CAST_SPLIT = 128
 
 WG_BYTES = 4 * PACK * NH
-V0_AT = WG_BYTES - ALIGN
-WG_AT = {(0, 0): 0, (1, 0): WG_BYTES, (0, 1): 2 * WG_BYTES, (1, 1): V0_AT + 4 * T - ALIGN}
-WV_WORDS_AT = 3 * WG_BYTES
+WG_AT = {(1, 0): 0, (0, 1): WG_BYTES, (1, 1): 4 * T - ALIGN}
+WV_WORDS_AT = 2 * WG_BYTES
 WV_SCALES_AT = WV_WORDS_AT + IG * 2 * N
 BG_AT = WV_SCALES_AT + IG * N
 RW_AT = BG_AT + ALIGN
 WG_FIRST_AT = [RW_AT + ALIGN + q * WG_BYTES // 2 for q in range(2)]
 V2_WORDS_AT = [WG_AT[1, 1] + WG_BYTES + a * 4 * T2 for a in range(KG)]
 V_PICKED_SCALES_AT = V2_WORDS_AT[1] - S // 2
-SCORE_BANKS = 4
-EARLY = 2
-CAST_SPLIT = 128
 
 
 def tile_list_residue_pocket_gate_kernel(
@@ -53,7 +51,7 @@ def tile_list_residue_pocket_gate_kernel(
     nc = tc.nc
     with ExitStack() as ctx:
         keep = ctx.enter_context(tc.tile_pool(name="keep", bufs=1))
-        ring = ctx.enter_context(tc.tile_pool(name="ring", bufs=8))
+        ring = ctx.enter_context(tc.tile_pool(name="ring", bufs=N // P))
         psum = ctx.enter_context(tc.psum_pool(name="psum", bufs=1))
         shared = ctx.enter_context(tc.tile_pool(name="shared", bufs=1))
 
@@ -63,7 +61,7 @@ def tile_list_residue_pocket_gate_kernel(
         v2_rows = keep.tile([P, T2 // 4], I32, name="v2_rows", align_bytes=ALIGN)
         scales = [keep.tile([P, (S + S2) // 4], I32, name=f"scales{a}", align_bytes=ALIGN) for a in range(KG)]
         v_words = [
-            shared.tile([P, T], I32, name="v_words0", align_bytes=ALIGN, offset=V0_AT),
+            shared.tile([P, T], I32, name="v_words0", align_bytes=ALIGN, offset=0),
             keep.tile([P, T], I32, name="v_words1", align_bytes=ALIGN),
         ]
         v2_words = [
@@ -97,6 +95,7 @@ def tile_list_residue_pocket_gate_kernel(
             staged[:, 0:S].rearrange("p (b t m) -> p b t m", b=IG, t=PACK),
             v_picked[:].rearrange("p (b m t) -> p b t m", b=IG, t=PACK),
         )
+
         def move_scales(a):
             first = ROWS_AT + BLOCKS * a
             for r in range(4):
@@ -135,7 +134,6 @@ def tile_list_residue_pocket_gate_kernel(
         wg_raw = {
             (b, u): shared.tile([P, PACK, NH], F32, name=f"wg_raw{b}{u}", align_bytes=ALIGN, offset=place)
             for (b, u), place in WG_AT.items()
-            if (b, u) != (0, 0)
         }
         wg_first = [
             shared.tile([P, PACK, P], F32, name=f"wg_first{q}", align_bytes=ALIGN, offset=place)
@@ -237,11 +235,14 @@ def tile_list_residue_pocket_gate_kernel(
             features = slice(u * NH + lo, u * NH + hi)
             quantize(wg_codes[b][:, features], wg_scales[b][:, features], wg_bf16[b, u][:, lo:hi, :])
 
+        def cast(copy, values, raw):
+            copy(values.rearrange("p (c i) t -> p c t i", i=LINE), raw.rearrange("p t (c i) -> p c t i", i=LINE))
+
         def cast_wg(copy, b, u, lo, hi):
-            copy(
-                wg_bf16[b, u][:, lo:hi, :].rearrange("p (c i) t -> p c t i", i=4),
-                wg_raw[b, u][:, :, lo:hi].rearrange("p t (c i) -> p c t i", i=4),
-            )
+            cast(copy, wg_bf16[b, u][:, lo:hi, :], wg_raw[b, u][:, :, lo:hi])
+
+        def cast_first(q):
+            cast(nc.vector.tensor_copy, wg_bf16[0, 0][:, q * P : (q + 1) * P, :], wg_first[q][:])
 
         wv_scale_bytes = wv_rows[:].bitcast(U8)
         feat = {}
@@ -249,7 +250,7 @@ def tile_list_residue_pocket_gate_kernel(
 
         def feat_pass(b, n, lo, hi):
             if n not in feat:
-                feat[n] = psum.tile([P, S2], F32, name=f"feat{n}", tag=f"bank{FEAT_BANK[n]}")
+                feat[n] = psum.tile([P, S2], F32, name=f"feat{n}", tag=f"bank{SCORE_BANKS + n}")
             nc.tensor.matmul_mx(
                 out=feat[n][:, lo:hi],
                 lhsT=wv_codes[:, b, 2 * P * n : 2 * P * (n + 1)].bitcast(FP4X4),
@@ -262,7 +263,7 @@ def tile_list_residue_pocket_gate_kernel(
 
         def gate_pass(b, n, lo, hi):
             if n not in gate:
-                gate[n] = psum.tile([P, S2], F32, name=f"gate{n}", tag=f"bank{GATE_BANK[n]}")
+                gate[n] = psum.tile([P, S2], F32, name=f"gate{n}", tag=f"bank{n}")
             nc.tensor.matmul_mx(
                 out=gate[n][:, lo:hi],
                 lhsT=wg_codes[b][:, P * n : P * (n + 1)].bitcast(FP8X4),
@@ -273,23 +274,16 @@ def tile_list_residue_pocket_gate_kernel(
                 stop=(b == IG - 1 and hi == S2),
             )
 
-        def finish(n, parts, stores):
-            tanh_g = ring.tile([P, S2], F32, name="tanh_g", bufs=4)
-            result = ring.tile([P, S2], F32, name="result", bufs=4)
+        def finish(n, parts):
+            tanh_g = ring.tile([P, S2], F32, name="tanh_g")
+            result = ring.tile([P, S2], F32, name="result")
             for part in parts:
                 nc.scalar.activation(tanh_g[:, part], gate[n][:, part], ACT.Tanh, bias=bg_half[:, n : n + 1])
             for part in parts:
                 nc.vector.scalar_tensor_tensor(
                     result[:, part], tanh_g[:, part], 1.0, feat[n][:, part], ALU.add, ALU.mult
                 )
-            for part in stores:
-                nc.sync.dma_start(out[n * P : (n + 1) * P, part], result[:, part])
-
-        def cast_first(q):
-            nc.vector.tensor_copy(
-                wg_bf16[0, 0][:, q * P : (q + 1) * P, :].rearrange("p (c i) t -> p c t i", i=4),
-                wg_first[q][:].rearrange("p t (c i) -> p c t i", i=4),
-            )
+            nc.sync.dma_start(out[n * P : (n + 1) * P, :], result[:])
 
         cast_first(0)
         wg_codes[0] = keep.tile([P, N], U32, name="wg_codes0", align_bytes=ALIGN)
@@ -321,8 +315,9 @@ def tile_list_residue_pocket_gate_kernel(
         quantize_wg(1, 1, 0, P)
         quantize_wg(1, 1, P, NH)
 
+        early_gates = range(NH // P)
         for half in range(0, S2, JH):
-            for n in range(2):
+            for n in early_gates:
                 gate_pass(0, n, half, half + JH)
             for n in range(N // P):
                 for lo in range(half, half + JH, JQ):
@@ -330,19 +325,16 @@ def tile_list_residue_pocket_gate_kernel(
         for n in range(N // P):
             for lo in range(0, JH, JQ):
                 feat_pass(1, n, lo, lo + JQ)
-        for n in range(2):
-            gate_pass(1, n, 0, JH)
-        whole = [slice(0, S2)]
-        halves = [slice(0, JH), slice(JH, S2)]
-        for n in range(2):
-            gate_pass(1, n, JH, S2)
+        for half in range(0, S2, JH):
+            for n in early_gates:
+                gate_pass(1, n, half, half + JH)
         for n in range(N // P):
-            if n >= 2:
+            if n not in early_gates:
                 for b in range(IG):
                     gate_pass(b, n, 0, S2)
             for lo in range(JH, S2, JQ):
                 feat_pass(1, n, lo, lo + JQ)
-        finish(0, halves, whole)
-        finish(1, whole, whole)
-        finish(2, whole, whole)
-        finish(3, halves, halves)
+
+        for n in range(N // P):
+            width = JH if n in (0, N // P - 1) else S2
+            finish(n, [slice(lo, lo + width) for lo in range(0, S2, width)])

@@ -1,6 +1,7 @@
 from contextlib import ExitStack
 
 import concourse.mybir as mybir
+from concourse.masks import make_identity
 
 K, T, S, T2, S2, N = 1024, 4096, 1024, 2048, 512, 512
 FLOPS = 2 * K * S * S2 + 4 * S * N * S2
@@ -43,6 +44,7 @@ RW_AT = BG_AT + ALIGN
 WG_FIRST_AT = [RW_AT + ALIGN + q * WG_BYTES // 2 for q in range(2)]
 V2_WORDS_AT = [WG_AT[1, 1] + WG_BYTES + a * 4 * T2 for a in range(KG)]
 V_PICKED_SCALES_AT = V2_WORDS_AT[1] - S // 2
+H_FIRST_AT = V2_WORDS_AT[1] + 4 * T2
 
 
 def tile_list_residue_pocket_gate_kernel(
@@ -58,7 +60,7 @@ def tile_list_residue_pocket_gate_kernel(
         idx = keep.tile([P, S // LIST], U16, name="idx")
         idx2 = keep.tile([P, S2 // LIST], U16, name="idx2")
         v_rows = keep.tile([P, T // 4], I32, name="v_rows", align_bytes=ALIGN)
-        v2_rows = keep.tile([P, T2 // 4], I32, name="v2_rows", align_bytes=ALIGN)
+        v2_rows = keep.tile([P, T2 // 4], I32, name="v2_rows", tag="v2_rows", align_bytes=ALIGN)
         scales = [keep.tile([P, (S + S2) // 4], I32, name=f"scales{a}", align_bytes=ALIGN) for a in range(KG)]
         v_words = [
             shared.tile([P, T], I32, name="v_words0", align_bytes=ALIGN, offset=0),
@@ -85,7 +87,7 @@ def tile_list_residue_pocket_gate_kernel(
         load_words(v_words[1], tab_words[1])
 
         v_picked = shared.tile([P, S], U8, name="v_picked", align_bytes=ALIGN, offset=V_PICKED_SCALES_AT)
-        v2_picked = keep.tile([P, S2], U8, name="v2_picked", align_bytes=ALIGN)
+        v2_picked = keep.tile([P, S2], U8, name="v2_picked", tag="v2_picked", align_bytes=ALIGN)
         staged = keep.tile([P, S + S2], U8, name="staged", align_bytes=ALIGN)
         staged32 = staged[:].bitcast(I32)
         nc.vector.tensor_copy(v2_picked[:], v2_rows[:].bitcast(U8).indirect(idx2[:]))
@@ -95,6 +97,15 @@ def tile_list_residue_pocket_gate_kernel(
             staged[:, 0:S].rearrange("p (b t m) -> p b t m", b=IG, t=PACK),
             v_picked[:].rearrange("p (b m t) -> p b t m", b=IG, t=PACK),
         )
+
+        rw_rows = keep.tile([P, GROUP], F32, name="rw_rows", tag="v2_rows", align_bytes=ALIGN)
+        identity = keep.tile([P, P], F32, name="identity", tag="v2_picked", align_bytes=ALIGN)
+        nc.gpsimd.memset(rw_rows[:], 0.0)
+        make_identity(nc, identity[:])
+        nc.sync.dma_start(rw_rows[0:IG, :], rw.rearrange("(b i) -> b i", b=IG))
+        rw_bank = psum.tile([P, PACK, P], F32, name="rw_bank", tag="bank7")
+        for t in range(PACK):
+            nc.tensor.transpose(rw_bank[:, t, :], rw_rows[:, t:GROUP:PACK], identity[:])
 
         def move_scales(a):
             first = ROWS_AT + BLOCKS * a
@@ -142,7 +153,6 @@ def tile_list_residue_pocket_gate_kernel(
         wv_codes = shared.tile([P, IG, 2 * N], U8, name="wv_codes", align_bytes=ALIGN, offset=WV_WORDS_AT)
         wv_rows = shared.tile([P, IG, N // 4], I32, name="wv_rows", align_bytes=ALIGN, offset=WV_SCALES_AT)
         bg_raw = shared.tile([P, N // P], F32, name="bg_raw", align_bytes=ALIGN, offset=BG_AT)
-        rw_col = shared.tile([P, IG, PACK], F32, name="rw_col", align_bytes=ALIGN, offset=RW_AT)
 
         def load_wg(b, u):
             rows = wg[b * GROUP : (b + 1) * GROUP, u * NH : (u + 1) * NH]
@@ -152,8 +162,6 @@ def tile_list_residue_pocket_gate_kernel(
         for q in range(2):
             rows = wg[0:GROUP, q * P : (q + 1) * P]
             nc.sync.dma_start(wg_first[q][:], rows.rearrange("(p t) n -> p t n", t=PACK))
-            if q == 0:
-                nc.sync.dma_start(rw_col[:], rw.rearrange("(b p t) -> p b t", b=IG, t=PACK))
         load_wg(1, 0)
         nc.sync.dma_start(wv_codes[:].bitcast(I32), wv_words.rearrange("b p n -> p b n").bitcast(I32))
         for r in range(4):
@@ -163,8 +171,7 @@ def tile_list_residue_pocket_gate_kernel(
         load_wg(1, 1)
         with nc.allow_non_contiguous_dma(reason="the bias lies one value a partition"):
             nc.sync.dma_start(bg_raw[:], bg.rearrange("(c p) -> p c", p=P))
-        bg_half = keep.tile([P, N // P], F32, name="bg_half")
-        nc.gpsimd.tensor_scalar(bg_half[:], bg_raw[:], 0.5, 0.0, ALU.mult, ALU.add)
+        bg_half = shared.tile([P, N // P], F32, name="bg_half", align_bytes=ALIGN, offset=WG_AT[0, 1])
 
         for b in range(IG):
             gather_v(1, b)
@@ -177,9 +184,9 @@ def tile_list_residue_pocket_gate_kernel(
 
         def score(step, a):
             b, c = order[step]
-            first = 1 if EARLY <= step < SCORE_BANKS else 0
+            first = 1 if EARLY <= step else 0
             if a == first:
-                score_bank[step] = psum.tile([P, PACK, JQ], F32, name=f"score{step}", tag=f"bank{step % SCORE_BANKS}")
+                score_bank[step] = psum.tile([P, PACK, JQ], F32, name=f"score{step}", tag=f"bank{step % 7}")
             scale_bytes = scales[a][:].bitcast(U8)
             for t in range(PACK):
                 column = b * GROUP + t * P
@@ -196,30 +203,39 @@ def tile_list_residue_pocket_gate_kernel(
         for a in range(KG):
             for step in range(EARLY):
                 score(step, a)
-        for step in range(EARLY, SCORE_BANKS):
+        for step in range(EARLY, 7):
             for a in reversed(range(KG)):
                 score(step, a)
 
-        h_bf16 = [keep.tile([P, S2, PACK], BF16, name=f"h_bf16{b}", align_bytes=ALIGN) for b in range(IG)]
+        h_bf16 = [
+            shared.tile([P, S2, PACK], BF16, name="h_bf160", align_bytes=ALIGN, offset=H_FIRST_AT),
+            keep.tile([P, S2, PACK], BF16, name="h_bf161", align_bytes=ALIGN),
+        ]
         h_codes = {1: keep.tile([P, S2], U32, name="h_codes1", align_bytes=ALIGN)}
         h_scales = [keep.tile([P, S2], U8, name=f"h_scales{b}", align_bytes=ALIGN) for b in range(IG)]
-        slots = {(0, 0): "wg_bf16", (1, 0): "v_codes11", (0, 1): "v2_codes11", (1, 1): "v_codes10"}
+        slots = {(0, 0): "wg_bf16", (0, 1): "v_codes11", (1, 1): "v2_codes11"}
         wg_bf16 = {
             (b, u): keep.tile([P, NH, PACK], BF16, name=f"wg_bf16{b}{u}", tag=slot, align_bytes=ALIGN)
             for (b, u), slot in slots.items()
         }
+        wg_bf16[1, 0] = shared.tile(
+            [P, NH, PACK], BF16, name="wg_bf1610", align_bytes=ALIGN, offset=H_FIRST_AT + 2 * PACK * JQ
+        )
         wg_codes = {1: keep.tile([P, N], U32, name="wg_codes1", align_bytes=ALIGN)}
         wg_scales = [keep.tile([P, N], U8, name=f"wg_scales{b}", align_bytes=ALIGN) for b in range(IG)]
+
+        tanh_tiles = {}
 
         def bound(step):
             b, c = order[step]
             tanh_a = keep.tile([P, JQ, PACK], F32, name=f"tanh_a{step}", tag=f"tanh_a{step}", align_bytes=ALIGN)
+            tanh_tiles[step] = tanh_a
             nc.scalar.activation(tanh_a[:], score_bank[step][:].rearrange("p t j -> p j t"), ACT.Tanh)
             nc.vector.scalar_tensor_tensor(
                 h_bf16[b][:, c * JQ : (c + 1) * JQ, :],
                 tanh_a[:],
                 0.5,
-                rw_col[:, b, :].unsqueeze(1).to_broadcast([P, JQ, PACK]),
+                rw_bank[:, :, b].unsqueeze(1).to_broadcast([P, JQ, PACK]),
                 ALU.mult,
                 ALU.mult,
             )
@@ -241,6 +257,10 @@ def tile_list_residue_pocket_gate_kernel(
         def cast_wg(copy, b, u, lo, hi):
             cast(copy, wg_bf16[b, u][:, lo:hi, :], wg_raw[b, u][:, :, lo:hi])
 
+        def cast_pool(lo, hi):
+            raw = wg_raw[1, 0][:, :, lo:hi].rearrange("p t n -> p n t")
+            nc.gpsimd.tensor_scalar(wg_bf16[1, 0][:, lo:hi, :], raw, 1.0, 0.0, ALU.mult, ALU.add)
+
         def cast_first(q):
             cast(nc.vector.tensor_copy, wg_bf16[0, 0][:, q * P : (q + 1) * P, :], wg_first[q][:])
 
@@ -250,7 +270,7 @@ def tile_list_residue_pocket_gate_kernel(
 
         def feat_pass(b, n, lo, hi):
             if n not in feat:
-                feat[n] = psum.tile([P, S2], F32, name=f"feat{n}", tag=f"bank{SCORE_BANKS + n}")
+                feat[n] = psum.tile([P, S2], F32, name=f"feat{n}", tag=f"bank{3 + n}")
             nc.tensor.matmul_mx(
                 out=feat[n][:, lo:hi],
                 lhsT=wv_codes[:, b, 2 * P * n : 2 * P * (n + 1)].bitcast(FP4X4),
@@ -263,7 +283,7 @@ def tile_list_residue_pocket_gate_kernel(
 
         def gate_pass(b, n, lo, hi):
             if n not in gate:
-                gate[n] = psum.tile([P, S2], F32, name=f"gate{n}", tag=f"bank{n}")
+                gate[n] = psum.tile([P, S2], F32, name=f"gate{n}", tag=f"bank{(1, 2, 0, 7)[n]}")
             nc.tensor.matmul_mx(
                 out=gate[n][:, lo:hi],
                 lhsT=wg_codes[b][:, P * n : P * (n + 1)].bitcast(FP8X4),
@@ -294,23 +314,24 @@ def tile_list_residue_pocket_gate_kernel(
                 cast_first(1)
             if step == 1:
                 quantize_wg(0, 0, P, NH)
-            if step + SCORE_BANKS < len(order):
-                for a in range(KG):
-                    score(step + SCORE_BANKS, a)
+            if step == 0:
+                for a in reversed(range(KG)):
+                    score(7, a)
             if order[step] == (0, 2):
                 h_codes[0] = keep.tile([P, S2], U32, name="h_codes0", tag=f"tanh_a{step}", align_bytes=ALIGN)
                 quantize_h(0, 0, JH)
+                cast_pool(0, P)
             if order[step] == (1, 0):
                 quantize_h(0, JH, S2)
+                cast_pool(P, NH)
             if order[step] == (1, 2):
                 quantize_h(1, 0, JH)
 
-        cast_wg(nc.scalar.copy, 1, 0, 0, NH)
         cast_wg(nc.scalar.copy, 0, 1, 0, NH)
-        cast_wg(nc.scalar.copy, 1, 1, 0, CAST_SPLIT)
+        nc.scalar.mul(bg_half[:], bg_raw[:], 0.5)
+        cast_wg(nc.scalar.copy, 1, 1, 0, NH)
         quantize_wg(1, 0, 0, NH)
         quantize_h(1, JH, S2)
-        cast_wg(nc.vector.tensor_copy, 1, 1, CAST_SPLIT, NH)
         quantize_wg(0, 1, 0, NH)
         quantize_wg(1, 1, 0, P)
         quantize_wg(1, 1, P, NH)

@@ -32,7 +32,7 @@ ROWS_AT = P - KG * BLOCKS
 ALIGN = 64
 LINE = 4
 SCORE_BANKS = 4
-EARLY = 2
+EARLY = 3
 CAST_SPLIT = 128
 
 WG_BYTES = 4 * PACK * NH
@@ -44,7 +44,6 @@ RW_AT = BG_AT + ALIGN
 WG_FIRST_AT = [RW_AT + ALIGN + q * WG_BYTES // 2 for q in range(2)]
 V2_WORDS_AT = [WG_AT[1, 1] + WG_BYTES + a * 4 * T2 for a in range(KG)]
 V_PICKED_SCALES_AT = V2_WORDS_AT[1] - S // 2
-H_FIRST_AT = V2_WORDS_AT[1] + 4 * T2
 
 
 def tile_list_residue_pocket_gate_kernel(
@@ -207,10 +206,11 @@ def tile_list_residue_pocket_gate_kernel(
             for a in reversed(range(KG)):
                 score(step, a)
 
-        h_bf16 = [
-            shared.tile([P, S2, PACK], BF16, name="h_bf160", align_bytes=ALIGN, offset=H_FIRST_AT),
-            keep.tile([P, S2, PACK], BF16, name="h_bf161", align_bytes=ALIGN),
-        ]
+        h_bf16 = {
+            (b, u): keep.tile([P, JH, PACK], BF16, name=f"h_bf16{b}{u}", tag=f"h_bf16{b}{u}", align_bytes=ALIGN)
+            for b in range(IG)
+            for u in range(2)
+        }
         h_codes = {1: keep.tile([P, S2], U32, name="h_codes1", align_bytes=ALIGN)}
         h_scales = [keep.tile([P, S2], U8, name=f"h_scales{b}", align_bytes=ALIGN) for b in range(IG)]
         slots = {(0, 0): "wg_bf16", (0, 1): "v_codes11", (1, 1): "v2_codes11"}
@@ -218,10 +218,7 @@ def tile_list_residue_pocket_gate_kernel(
             (b, u): keep.tile([P, NH, PACK], BF16, name=f"wg_bf16{b}{u}", tag=slot, align_bytes=ALIGN)
             for (b, u), slot in slots.items()
         }
-        wg_bf16[1, 0] = shared.tile(
-            [P, NH, PACK], BF16, name="wg_bf1610", align_bytes=ALIGN, offset=H_FIRST_AT + 2 * PACK * JQ
-        )
-        wg_codes = {1: keep.tile([P, N], U32, name="wg_codes1", align_bytes=ALIGN)}
+        wg_codes = {}
         wg_scales = [keep.tile([P, N], U8, name=f"wg_scales{b}", align_bytes=ALIGN) for b in range(IG)]
 
         tanh_tiles = {}
@@ -232,7 +229,7 @@ def tile_list_residue_pocket_gate_kernel(
             tanh_tiles[step] = tanh_a
             nc.scalar.activation(tanh_a[:], score_bank[step][:].rearrange("p t j -> p j t"), ACT.Tanh)
             nc.vector.scalar_tensor_tensor(
-                h_bf16[b][:, c * JQ : (c + 1) * JQ, :],
+                h_bf16[b, c // 2][:, (c % 2) * JQ : (c % 2 + 1) * JQ, :],
                 tanh_a[:],
                 0.5,
                 rw_bank[:, :, b].unsqueeze(1).to_broadcast([P, JQ, PACK]),
@@ -245,7 +242,7 @@ def tile_list_residue_pocket_gate_kernel(
 
         def quantize_h(b, lo, hi):
             sites = slice(lo, hi)
-            quantize(h_codes[b][:, sites], h_scales[b][:, sites], h_bf16[b][:, sites, :])
+            quantize(h_codes[b][:, sites], h_scales[b][:, sites], h_bf16[b, lo // JH][:])
 
         def quantize_wg(b, u, lo, hi):
             features = slice(u * NH + lo, u * NH + hi)
@@ -268,40 +265,51 @@ def tile_list_residue_pocket_gate_kernel(
         feat = {}
         gate = {}
 
+        def place(n, site):
+            if n < 2:
+                return site // JH, n * JH + site % JH
+            return n, site
+
+        def view(banks, n, lo, hi):
+            key, column = place(n, lo)
+            return banks[key][:, column : column + hi - lo]
+
         def feat_pass(b, n, lo, hi):
-            if n not in feat:
-                feat[n] = psum.tile([P, S2], F32, name=f"feat{n}", tag=f"bank{3 + n}")
+            key = place(n, lo)[0]
+            if key not in feat:
+                feat[key] = psum.tile([P, S2], F32, name=f"feat{key}", tag=f"bank{(2, 6, 3, 4)[key]}")
             nc.tensor.matmul_mx(
-                out=feat[n][:, lo:hi],
+                out=view(feat, n, lo, hi),
                 lhsT=wv_codes[:, b, 2 * P * n : 2 * P * (n + 1)].bitcast(FP4X4),
                 lhsT_scale=wv_scale_bytes[:, b, P * n : P * (n + 1)],
                 rhs=h_codes[b][:, lo:hi].bitcast(FP8X4),
                 rhs_scale=h_scales[b][:, lo:hi],
-                start=(b == 0 and lo == 0),
-                stop=(b == IG - 1 and hi == S2),
+                start=(b == 0 and place(n, lo)[1] == 0),
+                stop=(b == IG - 1 and place(n, hi - 1)[1] == S2 - 1),
             )
 
         def gate_pass(b, n, lo, hi):
-            if n not in gate:
-                gate[n] = psum.tile([P, S2], F32, name=f"gate{n}", tag=f"bank{(1, 2, 0, 7)[n]}")
+            key = place(n, lo)[0]
+            if key not in gate:
+                gate[key] = psum.tile([P, S2], F32, name=f"gate{key}", tag=f"bank{(1, 5, 0, 7)[key]}")
             nc.tensor.matmul_mx(
-                out=gate[n][:, lo:hi],
+                out=view(gate, n, lo, hi),
                 lhsT=wg_codes[b][:, P * n : P * (n + 1)].bitcast(FP8X4),
                 lhsT_scale=wg_scales[b][:, P * n : P * (n + 1)],
                 rhs=h_codes[b][:, lo:hi].bitcast(FP8X4),
                 rhs_scale=h_scales[b][:, lo:hi],
-                start=(b == 0 and lo == 0),
-                stop=(b == IG - 1 and hi == S2),
+                start=(b == 0 and place(n, lo)[1] == 0),
+                stop=(b == IG - 1 and place(n, hi - 1)[1] == S2 - 1),
             )
 
         def finish(n, parts):
             tanh_g = ring.tile([P, S2], F32, name="tanh_g")
             result = ring.tile([P, S2], F32, name="result")
             for part in parts:
-                nc.scalar.activation(tanh_g[:, part], gate[n][:, part], ACT.Tanh, bias=bg_half[:, n : n + 1])
+                nc.scalar.activation(tanh_g[:, part], view(gate, n, part.start, part.stop), ACT.Tanh, bias=bg_half[:, n : n + 1])
             for part in parts:
                 nc.vector.scalar_tensor_tensor(
-                    result[:, part], tanh_g[:, part], 1.0, feat[n][:, part], ALU.add, ALU.mult
+                    result[:, part], tanh_g[:, part], 1.0, view(feat, n, part.start, part.stop), ALU.add, ALU.mult
                 )
             nc.sync.dma_start(out[n * P : (n + 1) * P, :], result[:])
 
@@ -312,24 +320,25 @@ def tile_list_residue_pocket_gate_kernel(
             bound(step)
             if step == 0:
                 cast_first(1)
-            if step == 1:
+            if step == 0:
                 quantize_wg(0, 0, P, NH)
+                wg_bf16[1, 0] = keep.tile([P, NH, PACK], BF16, name="wg_bf1610", tag="wg_bf16", align_bytes=ALIGN)
+                cast_pool(0, NH)
             if step == 0:
                 for a in reversed(range(KG)):
                     score(7, a)
             if order[step] == (0, 2):
                 h_codes[0] = keep.tile([P, S2], U32, name="h_codes0", tag=f"tanh_a{step}", align_bytes=ALIGN)
                 quantize_h(0, 0, JH)
-                cast_pool(0, P)
             if order[step] == (1, 0):
                 quantize_h(0, JH, S2)
-                cast_pool(P, NH)
             if order[step] == (1, 2):
                 quantize_h(1, 0, JH)
 
         cast_wg(nc.scalar.copy, 0, 1, 0, NH)
         nc.scalar.mul(bg_half[:], bg_raw[:], 0.5)
         cast_wg(nc.scalar.copy, 1, 1, 0, NH)
+        wg_codes[1] = keep.tile([P, N], U32, name="wg_codes1", tag="h_bf1610", align_bytes=ALIGN)
         quantize_wg(1, 0, 0, NH)
         quantize_h(1, JH, S2)
         quantize_wg(0, 1, 0, NH)
@@ -357,5 +366,5 @@ def tile_list_residue_pocket_gate_kernel(
                 feat_pass(1, n, lo, lo + JQ)
 
         for n in range(N // P):
-            width = JH if n in (0, N // P - 1) else S2
+            width = S2 if n == 2 else JH
             finish(n, [slice(lo, lo + width) for lo in range(0, S2, width)])

@@ -31,17 +31,18 @@ NH = N // 2
 ROWS_AT = P - KG * BLOCKS
 ALIGN = 64
 LINE = 4
-SCORE_BANKS = 4
+SCORE_BANKS = 7
+RW_BANK = 7
+GATE_BANK = (1, 5, 0, RW_BANK)
+FEAT_BANK = (2, 6, 3, 4)
 EARLY = 3
-CAST_SPLIT = 128
 
 WG_BYTES = 4 * PACK * NH
 WG_AT = {(1, 0): 0, (0, 1): WG_BYTES, (1, 1): 4 * T - ALIGN}
 WV_WORDS_AT = 2 * WG_BYTES
 WV_SCALES_AT = WV_WORDS_AT + IG * 2 * N
 BG_AT = WV_SCALES_AT + IG * N
-RW_AT = BG_AT + ALIGN
-WG_FIRST_AT = [RW_AT + ALIGN + q * WG_BYTES // 2 for q in range(2)]
+WG_FIRST_AT = [BG_AT + ALIGN + q * WG_BYTES // 2 for q in range(2)]
 V2_WORDS_AT = [WG_AT[1, 1] + WG_BYTES + a * 4 * T2 for a in range(KG)]
 V_PICKED_SCALES_AT = V2_WORDS_AT[1] - S // 2
 
@@ -102,9 +103,12 @@ def tile_list_residue_pocket_gate_kernel(
         nc.gpsimd.memset(rw_rows[:], 0.0)
         make_identity(nc, identity[:])
         nc.sync.dma_start(rw_rows[0:IG, :], rw.rearrange("(b i) -> b i", b=IG))
-        rw_bank = psum.tile([P, PACK, P], F32, name="rw_bank", tag="bank7")
+        rw_bank = psum.tile([P, PACK, P], F32, name="rw_bank", tag=f"bank{RW_BANK}")
         for t in range(PACK):
             nc.tensor.transpose(rw_bank[:, t, :], rw_rows[:, t:GROUP:PACK], identity[:])
+        rw_second = keep.tile([P, PACK], F32, name="rw_second")
+        nc.vector.tensor_copy(rw_second[:], rw_bank[:, :, 1])
+        rw_of_group = [rw_bank[:, :, 0], rw_second[:]]
 
         def move_scales(a):
             first = ROWS_AT + BLOCKS * a
@@ -170,7 +174,7 @@ def tile_list_residue_pocket_gate_kernel(
         load_wg(1, 1)
         with nc.allow_non_contiguous_dma(reason="the bias lies one value a partition"):
             nc.sync.dma_start(bg_raw[:], bg.rearrange("(c p) -> p c", p=P))
-        bg_half = shared.tile([P, N // P], F32, name="bg_half", align_bytes=ALIGN, offset=WG_AT[0, 1])
+        bg_half = shared.tile([P, N // P], F32, name="bg_half", align_bytes=ALIGN, offset=WG_AT[1, 1])
 
         for b in range(IG):
             gather_v(1, b)
@@ -185,7 +189,8 @@ def tile_list_residue_pocket_gate_kernel(
             b, c = order[step]
             first = 1 if EARLY <= step else 0
             if a == first:
-                score_bank[step] = psum.tile([P, PACK, JQ], F32, name=f"score{step}", tag=f"bank{step % 7}")
+                bank = f"bank{step % SCORE_BANKS}"
+                score_bank[step] = psum.tile([P, PACK, JQ], F32, name=f"score{step}", tag=bank)
             scale_bytes = scales[a][:].bitcast(U8)
             for t in range(PACK):
                 column = b * GROUP + t * P
@@ -202,14 +207,14 @@ def tile_list_residue_pocket_gate_kernel(
         for a in range(KG):
             for step in range(EARLY):
                 score(step, a)
-        for step in range(EARLY, 7):
+        for step in range(EARLY, SCORE_BANKS):
             for a in reversed(range(KG)):
                 score(step, a)
 
         h_bf16 = {
-            (b, u): keep.tile([P, JH, PACK], BF16, name=f"h_bf16{b}{u}", tag=f"h_bf16{b}{u}", align_bytes=ALIGN)
+            (b, h): keep.tile([P, JH, PACK], BF16, name=f"h_bf16{b}{h}", tag=f"h_bf16{b}{h}", align_bytes=ALIGN)
             for b in range(IG)
-            for u in range(2)
+            for h in range(2)
         }
         h_codes = {1: keep.tile([P, S2], U32, name="h_codes1", align_bytes=ALIGN)}
         h_scales = [keep.tile([P, S2], U8, name=f"h_scales{b}", align_bytes=ALIGN) for b in range(IG)]
@@ -221,18 +226,15 @@ def tile_list_residue_pocket_gate_kernel(
         wg_codes = {}
         wg_scales = [keep.tile([P, N], U8, name=f"wg_scales{b}", align_bytes=ALIGN) for b in range(IG)]
 
-        tanh_tiles = {}
-
         def bound(step):
             b, c = order[step]
             tanh_a = keep.tile([P, JQ, PACK], F32, name=f"tanh_a{step}", tag=f"tanh_a{step}", align_bytes=ALIGN)
-            tanh_tiles[step] = tanh_a
             nc.scalar.activation(tanh_a[:], score_bank[step][:].rearrange("p t j -> p j t"), ACT.Tanh)
             nc.vector.scalar_tensor_tensor(
                 h_bf16[b, c // 2][:, (c % 2) * JQ : (c % 2 + 1) * JQ, :],
                 tanh_a[:],
                 0.5,
-                rw_bank[:, :, b].unsqueeze(1).to_broadcast([P, JQ, PACK]),
+                rw_of_group[b].unsqueeze(1).to_broadcast([P, JQ, PACK]),
                 ALU.mult,
                 ALU.mult,
             )
@@ -251,12 +253,8 @@ def tile_list_residue_pocket_gate_kernel(
         def cast(copy, values, raw):
             copy(values.rearrange("p (c i) t -> p c t i", i=LINE), raw.rearrange("p t (c i) -> p c t i", i=LINE))
 
-        def cast_wg(copy, b, u, lo, hi):
-            cast(copy, wg_bf16[b, u][:, lo:hi, :], wg_raw[b, u][:, :, lo:hi])
-
-        def cast_pool(lo, hi):
-            raw = wg_raw[1, 0][:, :, lo:hi].rearrange("p t n -> p n t")
-            nc.gpsimd.tensor_scalar(wg_bf16[1, 0][:, lo:hi, :], raw, 1.0, 0.0, ALU.mult, ALU.add)
+        def cast_wg(b, u, lo, hi):
+            cast(nc.scalar.copy, wg_bf16[b, u][:, lo:hi, :], wg_raw[b, u][:, :, lo:hi])
 
         def cast_first(q):
             cast(nc.vector.tensor_copy, wg_bf16[0, 0][:, q * P : (q + 1) * P, :], wg_first[q][:])
@@ -266,7 +264,7 @@ def tile_list_residue_pocket_gate_kernel(
         gate = {}
 
         def place(n, site):
-            if n < 2:
+            if n < NH // P:
                 return site // JH, n * JH + site % JH
             return n, site
 
@@ -277,7 +275,7 @@ def tile_list_residue_pocket_gate_kernel(
         def feat_pass(b, n, lo, hi):
             key = place(n, lo)[0]
             if key not in feat:
-                feat[key] = psum.tile([P, S2], F32, name=f"feat{key}", tag=f"bank{(2, 6, 3, 4)[key]}")
+                feat[key] = psum.tile([P, S2], F32, name=f"feat{key}", tag=f"bank{FEAT_BANK[key]}")
             nc.tensor.matmul_mx(
                 out=view(feat, n, lo, hi),
                 lhsT=wv_codes[:, b, 2 * P * n : 2 * P * (n + 1)].bitcast(FP4X4),
@@ -291,7 +289,7 @@ def tile_list_residue_pocket_gate_kernel(
         def gate_pass(b, n, lo, hi):
             key = place(n, lo)[0]
             if key not in gate:
-                gate[key] = psum.tile([P, S2], F32, name=f"gate{key}", tag=f"bank{(1, 5, 0, 7)[key]}")
+                gate[key] = psum.tile([P, S2], F32, name=f"gate{key}", tag=f"bank{GATE_BANK[key]}")
             nc.tensor.matmul_mx(
                 out=view(gate, n, lo, hi),
                 lhsT=wg_codes[b][:, P * n : P * (n + 1)].bitcast(FP8X4),
@@ -306,7 +304,8 @@ def tile_list_residue_pocket_gate_kernel(
             tanh_g = ring.tile([P, S2], F32, name="tanh_g")
             result = ring.tile([P, S2], F32, name="result")
             for part in parts:
-                nc.scalar.activation(tanh_g[:, part], view(gate, n, part.start, part.stop), ACT.Tanh, bias=bg_half[:, n : n + 1])
+                logits = view(gate, n, part.start, part.stop)
+                nc.scalar.activation(tanh_g[:, part], logits, ACT.Tanh, bias=bg_half[:, n : n + 1])
             for part in parts:
                 nc.vector.scalar_tensor_tensor(
                     result[:, part], tanh_g[:, part], 1.0, view(feat, n, part.start, part.stop), ALU.add, ALU.mult
@@ -320,13 +319,12 @@ def tile_list_residue_pocket_gate_kernel(
             bound(step)
             if step == 0:
                 cast_first(1)
-            if step == 0:
                 quantize_wg(0, 0, P, NH)
                 wg_bf16[1, 0] = keep.tile([P, NH, PACK], BF16, name="wg_bf1610", tag="wg_bf16", align_bytes=ALIGN)
-                cast_pool(0, NH)
-            if step == 0:
+                raw = wg_raw[1, 0][:].rearrange("p t n -> p n t")
+                nc.gpsimd.tensor_scalar(wg_bf16[1, 0][:], raw, 1.0, 0.0, ALU.mult, ALU.add)
                 for a in reversed(range(KG)):
-                    score(7, a)
+                    score(SCORE_BANKS, a)
             if order[step] == (0, 2):
                 h_codes[0] = keep.tile([P, S2], U32, name="h_codes0", tag=f"tanh_a{step}", align_bytes=ALIGN)
                 quantize_h(0, 0, JH)
@@ -335,9 +333,10 @@ def tile_list_residue_pocket_gate_kernel(
             if order[step] == (1, 2):
                 quantize_h(1, 0, JH)
 
-        cast_wg(nc.scalar.copy, 0, 1, 0, NH)
+        cast_wg(0, 1, 0, NH)
+        cast_wg(1, 1, 0, P)
+        cast_wg(1, 1, P, NH)
         nc.scalar.mul(bg_half[:], bg_raw[:], 0.5)
-        cast_wg(nc.scalar.copy, 1, 1, 0, NH)
         wg_codes[1] = keep.tile([P, N], U32, name="wg_codes1", tag="h_bf1610", align_bytes=ALIGN)
         quantize_wg(1, 0, 0, NH)
         quantize_h(1, JH, S2)
@@ -366,5 +365,5 @@ def tile_list_residue_pocket_gate_kernel(
                 feat_pass(1, n, lo, lo + JQ)
 
         for n in range(N // P):
-            width = S2 if n == 2 else JH
+            width = JH if n in early_gates or n == N // P - 1 else S2
             finish(n, [slice(lo, lo + width) for lo in range(0, S2, width)])

@@ -38,11 +38,10 @@ FEAT_BANK = (2, 6, 3, 4)
 EARLY = 3
 
 WG_BYTES = 4 * PACK * NH
-WG_AT = {(1, 0): 0, (0, 1): WG_BYTES, (1, 1): 4 * T - ALIGN}
 WV_WORDS_AT = 2 * WG_BYTES
 WV_SCALES_AT = WV_WORDS_AT + IG * 2 * N
 BG_AT = WV_SCALES_AT + IG * N
-WG_FIRST_AT = [BG_AT + ALIGN + q * WG_BYTES // 2 for q in range(2)]
+WG_AT = {(1, 0): 0, (0, 1): WG_BYTES, (1, 1): 4 * T - ALIGN, (0, 0): BG_AT + ALIGN}
 V2_WORDS_AT = [WG_AT[1, 1] + WG_BYTES + a * 4 * T2 for a in range(KG)]
 V_PICKED_SCALES_AT = V2_WORDS_AT[1] - S // 2
 
@@ -106,9 +105,6 @@ def tile_list_residue_pocket_gate_kernel(
         rw_bank = psum.tile([P, PACK, P], F32, name="rw_bank", tag=f"bank{RW_BANK}")
         for t in range(PACK):
             nc.tensor.transpose(rw_bank[:, t, :], rw_rows[:, t:GROUP:PACK], identity[:])
-        rw_second = keep.tile([P, PACK], F32, name="rw_second")
-        nc.vector.tensor_copy(rw_second[:], rw_bank[:, :, 1])
-        rw_of_group = [rw_bank[:, :, 0], rw_second[:]]
 
         def move_scales(a):
             first = ROWS_AT + BLOCKS * a
@@ -149,10 +145,6 @@ def tile_list_residue_pocket_gate_kernel(
             (b, u): shared.tile([P, PACK, NH], F32, name=f"wg_raw{b}{u}", align_bytes=ALIGN, offset=place)
             for (b, u), place in WG_AT.items()
         }
-        wg_first = [
-            shared.tile([P, PACK, P], F32, name=f"wg_first{q}", align_bytes=ALIGN, offset=place)
-            for q, place in enumerate(WG_FIRST_AT)
-        ]
         wv_codes = shared.tile([P, IG, 2 * N], U8, name="wv_codes", align_bytes=ALIGN, offset=WV_WORDS_AT)
         wv_rows = shared.tile([P, IG, N // 4], I32, name="wv_rows", align_bytes=ALIGN, offset=WV_SCALES_AT)
         bg_raw = shared.tile([P, N // P], F32, name="bg_raw", align_bytes=ALIGN, offset=BG_AT)
@@ -162,9 +154,7 @@ def tile_list_residue_pocket_gate_kernel(
             nc.sync.dma_start(wg_raw[b, u][:], rows.rearrange("(p t) n -> p t n", t=PACK))
 
         nc.vector.memset(wv_rows[:], 0)
-        for q in range(2):
-            rows = wg[0:GROUP, q * P : (q + 1) * P]
-            nc.sync.dma_start(wg_first[q][:], rows.rearrange("(p t) n -> p t n", t=PACK))
+        load_wg(0, 0)
         load_wg(1, 0)
         nc.sync.dma_start(wv_codes[:].bitcast(I32), wv_words.rearrange("b p n -> p b n").bitcast(I32))
         for r in range(4):
@@ -234,7 +224,7 @@ def tile_list_residue_pocket_gate_kernel(
                 h_bf16[b, c // 2][:, (c % 2) * JQ : (c % 2 + 1) * JQ, :],
                 tanh_a[:],
                 0.5,
-                rw_of_group[b].unsqueeze(1).to_broadcast([P, JQ, PACK]),
+                rw_bank[:, :, b].unsqueeze(1).to_broadcast([P, JQ, PACK]),
                 ALU.mult,
                 ALU.mult,
             )
@@ -250,14 +240,9 @@ def tile_list_residue_pocket_gate_kernel(
             features = slice(u * NH + lo, u * NH + hi)
             quantize(wg_codes[b][:, features], wg_scales[b][:, features], wg_bf16[b, u][:, lo:hi, :])
 
-        def cast(copy, values, raw):
-            copy(values.rearrange("p (c i) t -> p c t i", i=LINE), raw.rearrange("p t (c i) -> p c t i", i=LINE))
-
-        def cast_wg(b, u, lo, hi):
-            cast(nc.scalar.copy, wg_bf16[b, u][:, lo:hi, :], wg_raw[b, u][:, :, lo:hi])
-
-        def cast_first(q):
-            cast(nc.vector.tensor_copy, wg_bf16[0, 0][:, q * P : (q + 1) * P, :], wg_first[q][:])
+        def cast_wg(copy, b, u, lo, hi):
+            values = wg_bf16[b, u][:, lo:hi, :].rearrange("p (c i) t -> p c t i", i=LINE)
+            copy(values, wg_raw[b, u][:, :, lo:hi].rearrange("p t (c i) -> p c t i", i=LINE))
 
         wv_scale_bytes = wv_rows[:].bitcast(U8)
         feat = {}
@@ -310,16 +295,18 @@ def tile_list_residue_pocket_gate_kernel(
                 nc.vector.scalar_tensor_tensor(
                     result[:, part], tanh_g[:, part], 1.0, view(feat, n, part.start, part.stop), ALU.add, ALU.mult
                 )
-            nc.sync.dma_start(out[n * P : (n + 1) * P, :], result[:])
+            for part in parts if n == N // P - 1 else [slice(0, S2)]:
+                nc.sync.dma_start(out[n * P : (n + 1) * P, part], result[:, part])
 
-        cast_first(0)
+        cast_wg(nc.vector.tensor_copy, 0, 0, 0, P)
+        cast_wg(nc.vector.tensor_copy, 0, 0, P, NH)
         wg_codes[0] = keep.tile([P, N], U32, name="wg_codes0", align_bytes=ALIGN)
         quantize_wg(0, 0, 0, P)
+        quantize_wg(0, 0, P, NH)
+
         for step in range(len(order)):
             bound(step)
             if step == 0:
-                cast_first(1)
-                quantize_wg(0, 0, P, NH)
                 wg_bf16[1, 0] = keep.tile([P, NH, PACK], BF16, name="wg_bf1610", tag="wg_bf16", align_bytes=ALIGN)
                 raw = wg_raw[1, 0][:].rearrange("p t n -> p n t")
                 nc.gpsimd.tensor_scalar(wg_bf16[1, 0][:], raw, 1.0, 0.0, ALU.mult, ALU.add)
@@ -333,9 +320,9 @@ def tile_list_residue_pocket_gate_kernel(
             if order[step] == (1, 2):
                 quantize_h(1, 0, JH)
 
-        cast_wg(0, 1, 0, NH)
-        cast_wg(1, 1, 0, P)
-        cast_wg(1, 1, P, NH)
+        cast_wg(nc.scalar.copy, 0, 1, 0, NH)
+        cast_wg(nc.scalar.copy, 1, 1, 0, P)
+        cast_wg(nc.scalar.copy, 1, 1, P, NH)
         nc.scalar.mul(bg_half[:], bg_raw[:], 0.5)
         wg_codes[1] = keep.tile([P, N], U32, name="wg_codes1", tag="h_bf1610", align_bytes=ALIGN)
         quantize_wg(1, 0, 0, NH)

@@ -29,7 +29,7 @@ JQ = 128
 JH = S2 // 2
 NH = N // 2
 ROWS_AT = P - KG * BLOCKS
-ALIGN = 64
+ALIGN = 256
 LINE = 4
 SCORE_BANKS = 7
 RW_BANK = 7
@@ -286,8 +286,8 @@ def tile_list_residue_pocket_gate_kernel(
             )
 
         def finish(n, parts):
-            tanh_g = ring.tile([P, S2], F32, name="tanh_g")
-            result = ring.tile([P, S2], F32, name="result")
+            tanh_g = ring.tile([P, S2], F32, name="tanh_g", align_bytes=ALIGN)
+            result = ring.tile([P, S2], F32, name="result", align_bytes=ALIGN)
             for part in parts:
                 logits = view(gate, n, part.start, part.stop)
                 nc.scalar.activation(tanh_g[:, part], logits, ACT.Tanh, bias=bg_half[:, n : n + 1])

@@ -30,6 +30,7 @@ JH = S2 // 2
 NH = N // 2
 ROWS_AT = P - KG * BLOCKS
 ALIGN = 256
+PAGE = 4096
 LINE = 4
 SCORE_BANKS = 7
 RW_BANK = 7
@@ -38,12 +39,12 @@ FEAT_BANK = (2, 6, 3, 4)
 EARLY = 3
 
 WG_BYTES = 4 * PACK * NH
-WV_WORDS_AT = 2 * WG_BYTES
+WV_WORDS_AT = 3 * WG_BYTES
 WV_SCALES_AT = WV_WORDS_AT + IG * 2 * N
-BG_AT = WV_SCALES_AT + IG * N
-WG_AT = {(1, 0): 0, (0, 1): WG_BYTES, (1, 1): 4 * T - ALIGN, (0, 0): BG_AT + ALIGN}
-V2_WORDS_AT = [WG_AT[1, 1] + WG_BYTES + a * 4 * T2 for a in range(KG)]
+WG_AT = {(1, 0): 0, (0, 1): WG_BYTES, (0, 0): 2 * WG_BYTES, (1, 1): WV_SCALES_AT + IG * N}
+V2_WORDS_AT = [4 * T + PAGE + a * 4 * T2 for a in range(KG)]
 V_PICKED_SCALES_AT = V2_WORDS_AT[1] - S // 2
+V1_WORDS_AT = V2_WORDS_AT[1] + 4 * T2
 
 
 def tile_list_residue_pocket_gate_kernel(
@@ -56,14 +57,14 @@ def tile_list_residue_pocket_gate_kernel(
         psum = ctx.enter_context(tc.psum_pool(name="psum", bufs=1))
         shared = ctx.enter_context(tc.tile_pool(name="shared", bufs=1))
 
-        idx = keep.tile([P, S // LIST], U16, name="idx")
-        idx2 = keep.tile([P, S2 // LIST], U16, name="idx2")
-        v_rows = keep.tile([P, T // 4], I32, name="v_rows", align_bytes=ALIGN)
-        v2_rows = keep.tile([P, T2 // 4], I32, name="v2_rows", tag="v2_rows", align_bytes=ALIGN)
-        scales = [keep.tile([P, (S + S2) // 4], I32, name=f"scales{a}", align_bytes=ALIGN) for a in range(KG)]
+        idx = keep.tile([P, S // LIST], U16, name="idx", align_bytes=ALIGN)
+        idx2 = keep.tile([P, S2 // LIST], U16, name="idx2", align_bytes=ALIGN)
+        v_rows = keep.tile([P, T // 4], I32, name="v_rows", align_bytes=PAGE)
+        v2_rows = keep.tile([P, T2 // 4], I32, name="v2_rows", tag="v2_rows", align_bytes=PAGE // 2)
+        scales = [keep.tile([P, (S + S2) // 4], I32, name=f"scales{a}", align_bytes=PAGE // 2) for a in range(KG)]
         v_words = [
-            shared.tile([P, T], I32, name="v_words0", align_bytes=ALIGN, offset=0),
-            keep.tile([P, T], I32, name="v_words1", align_bytes=ALIGN),
+            shared.tile([P, T], I32, name="v_words0", align_bytes=PAGE, offset=0),
+            shared.tile([P, T], I32, name="v_words1", align_bytes=PAGE, offset=V1_WORDS_AT),
         ]
         v2_words = [
             shared.tile([P, T2], I32, name=f"v2_words{a}", align_bytes=ALIGN, offset=V2_WORDS_AT[a]) for a in range(KG)
@@ -87,7 +88,7 @@ def tile_list_residue_pocket_gate_kernel(
 
         v_picked = shared.tile([P, S], U8, name="v_picked", align_bytes=ALIGN, offset=V_PICKED_SCALES_AT)
         v2_picked = keep.tile([P, S2], U8, name="v2_picked", tag="v2_picked", align_bytes=ALIGN)
-        staged = keep.tile([P, S + S2], U8, name="staged", align_bytes=ALIGN)
+        staged = keep.tile([P, S + S2], U8, name="staged", align_bytes=PAGE // 2)
         staged32 = staged[:].bitcast(I32)
         nc.vector.tensor_copy(v2_picked[:], v2_rows[:].bitcast(U8).indirect(idx2[:]))
         nc.vector.tensor_copy(v_picked[:], v_rows[:].bitcast(U8).indirect(idx[:]))
@@ -97,7 +98,7 @@ def tile_list_residue_pocket_gate_kernel(
             v_picked[:].rearrange("p (b m t) -> p b t m", b=IG, t=PACK),
         )
 
-        rw_rows = keep.tile([P, GROUP], F32, name="rw_rows", tag="v2_rows", align_bytes=ALIGN)
+        rw_rows = keep.tile([P, GROUP], F32, name="rw_rows", tag="v2_rows", align_bytes=PAGE // 2)
         identity = keep.tile([P, P], F32, name="identity", tag="v2_picked", align_bytes=ALIGN)
         nc.gpsimd.memset(rw_rows[:], 0.0)
         make_identity(nc, identity[:])
@@ -147,7 +148,7 @@ def tile_list_residue_pocket_gate_kernel(
         }
         wv_codes = shared.tile([P, IG, 2 * N], U8, name="wv_codes", align_bytes=ALIGN, offset=WV_WORDS_AT)
         wv_rows = shared.tile([P, IG, N // 4], I32, name="wv_rows", align_bytes=ALIGN, offset=WV_SCALES_AT)
-        bg_raw = shared.tile([P, N // P], F32, name="bg_raw", align_bytes=ALIGN, offset=BG_AT)
+        bg_raw = shared.tile([P, N // P], F32, name="bg_raw", align_bytes=ALIGN, offset=V1_WORDS_AT)
 
         def load_wg(b, u):
             rows = wg[b * GROUP : (b + 1) * GROUP, u * NH : (u + 1) * NH]
@@ -287,7 +288,7 @@ def tile_list_residue_pocket_gate_kernel(
 
         def finish(n, parts):
             tanh_g = ring.tile([P, S2], F32, name="tanh_g", align_bytes=ALIGN)
-            result = ring.tile([P, S2], F32, name="result", align_bytes=ALIGN)
+            result = ring.tile([P, S2], F32, name="result", align_bytes=PAGE // 2)
             for part in parts:
                 logits = view(gate, n, part.start, part.stop)
                 nc.scalar.activation(tanh_g[:, part], logits, ACT.Tanh, bias=bg_half[:, n : n + 1])

@@ -37,6 +37,7 @@ RW_BANK = 7
 GATE_BANK = (1, 5, 0, RW_BANK)
 FEAT_BANK = (2, 6, 3, 4)
 EARLY = 3
+V2_PIECES = [((0, JH), (JH, S2)), ((0, JQ), (JQ, JH), (JH, S2))]
 
 WG_BYTES = 4 * PACK * NH
 WV_WORDS_AT = 3 * WG_BYTES
@@ -117,30 +118,28 @@ def tile_list_residue_pocket_gate_kernel(
             load_words(v2_words[a], tab2_words[a])
         move_scales(1)
 
-        v_codes = [
-            [keep.tile([P, GROUP], U32, name=f"v_codes{a}{b}", tag=f"v_codes{a}{b}", align_bytes=ALIGN) for b in range(IG)]
+        v_codes = [keep.tile([P, S], U32, name=f"v_codes{a}", tag=f"v_codes{a}", align_bytes=ALIGN) for a in range(KG)]
+        v2_codes = {
+            (a, lo): keep.tile([P, hi - lo], U32, name=f"v2_codes{a}_{lo}", tag=f"v2_codes{a}_{lo}", align_bytes=ALIGN)
             for a in range(KG)
-        ]
-        v2_codes = [
-            [keep.tile([P, JH], U32, name=f"v2_codes{a}{h}", tag=f"v2_codes{a}{h}", align_bytes=ALIGN) for h in range(2)]
-            for a in range(KG)
-        ]
+            for lo, hi in V2_PIECES[a]
+        }
 
-        def gather_v(a, b):
-            columns = GROUP // LIST
+        def gather_v(a):
             nc.vector.tensor_copy(
-                v_codes[a][b][:].rearrange("p (t m) -> p m t", t=PACK),
-                v_words[a][:].bitcast(U32).indirect(idx[:, columns * b : columns * (b + 1)]),
+                v_codes[a][:].rearrange("p (b t m) -> p b m t", b=IG, t=PACK),
+                v_words[a][:].bitcast(U32).indirect(idx[:]),
             )
 
-        def gather_v2(a, h):
-            columns = JH // LIST
-            nc.vector.tensor_copy(
-                v2_codes[a][h][:], v2_words[a][:].bitcast(U32).indirect(idx2[:, columns * h : columns * (h + 1)])
-            )
+        def gather_v2(a, lo, hi):
+            window = v2_words[a][:].bitcast(U32)
+            nc.vector.tensor_copy(v2_codes[a, lo][:], window.indirect(idx2[:, lo // LIST : hi // LIST]))
 
-        for b in range(IG):
-            gather_v(0, b)
+        def site_codes(a, c):
+            lo = max(lo for lo, hi in V2_PIECES[a] if lo <= c * JQ)
+            return v2_codes[a, lo][:, c * JQ - lo : (c + 1) * JQ - lo]
+
+        gather_v(0)
 
         wg_raw = {
             (b, u): shared.tile([P, PACK, NH], F32, name=f"wg_raw{b}{u}", align_bytes=ALIGN, offset=place)
@@ -167,11 +166,10 @@ def tile_list_residue_pocket_gate_kernel(
             nc.sync.dma_start(bg_raw[:], bg.rearrange("(c p) -> p c", p=P))
         bg_half = shared.tile([P, N // P], F32, name="bg_half", align_bytes=ALIGN, offset=WG_AT[1, 1])
 
-        for b in range(IG):
-            gather_v(1, b)
+        gather_v(1)
         for a in range(KG):
-            for h in range(2):
-                gather_v2(a, h)
+            for lo, hi in V2_PIECES[a]:
+                gather_v2(a, lo, hi)
 
         order = [(b, c) for b in range(IG) for c in range(S2 // JQ)]
         score_bank = {}
@@ -187,9 +185,9 @@ def tile_list_residue_pocket_gate_kernel(
                 column = b * GROUP + t * P
                 nc.tensor.matmul_mx(
                     out=score_bank[step][:, t, :],
-                    lhsT=v_codes[a][b][:, t * P : (t + 1) * P].bitcast(FP8X4),
+                    lhsT=v_codes[a][:, column : column + P].bitcast(FP8X4),
                     lhsT_scale=scale_bytes[4 * a : P, column : column + P],
-                    rhs=v2_codes[a][c // 2][:, (c % 2) * JQ : (c % 2 + 1) * JQ].bitcast(FP8X4),
+                    rhs=site_codes(a, c).bitcast(FP8X4),
                     rhs_scale=scale_bytes[4 * a : P, S + c * JQ : S + (c + 1) * JQ],
                     start=(a == first and t == 0),
                     stop=(a != first and t == PACK - 1),
@@ -209,7 +207,7 @@ def tile_list_residue_pocket_gate_kernel(
         }
         h_codes = {1: keep.tile([P, S2], U32, name="h_codes1", align_bytes=ALIGN)}
         h_scales = [keep.tile([P, S2], U8, name=f"h_scales{b}", align_bytes=ALIGN) for b in range(IG)]
-        slots = {(0, 0): "wg_bf16", (0, 1): "v_codes11", (1, 1): "v2_codes11"}
+        slots = {(0, 0): "wg_bf16", (0, 1): "v_codes1", (1, 1): f"v2_codes1_{JH}"}
         wg_bf16 = {
             (b, u): keep.tile([P, NH, PACK], BF16, name=f"wg_bf16{b}{u}", tag=slot, align_bytes=ALIGN)
             for (b, u), slot in slots.items()
@@ -337,11 +335,9 @@ def tile_list_residue_pocket_gate_kernel(
             for n in early_gates:
                 gate_pass(0, n, half, half + JH)
             for n in range(N // P):
-                for lo in range(half, half + JH, JQ):
-                    feat_pass(0, n, lo, lo + JQ)
+                feat_pass(0, n, half, half + JH)
         for n in range(N // P):
-            for lo in range(0, JH, JQ):
-                feat_pass(1, n, lo, lo + JQ)
+            feat_pass(1, n, 0, JH)
         for half in range(0, S2, JH):
             for n in early_gates:
                 gate_pass(1, n, half, half + JH)
@@ -349,8 +345,7 @@ def tile_list_residue_pocket_gate_kernel(
             if n not in early_gates:
                 for b in range(IG):
                     gate_pass(b, n, 0, S2)
-            for lo in range(JH, S2, JQ):
-                feat_pass(1, n, lo, lo + JQ)
+            feat_pass(1, n, JH, S2)
 
         for n in range(N // P):
             width = JH if n in early_gates or n == N // P - 1 else S2

@@ -348,5 +348,4 @@ def tile_list_residue_pocket_gate_kernel(
             feat_pass(1, n, JH, S2)
 
         for n in range(N // P):
-            width = JH if n in early_gates or n == N // P - 1 else S2
-            finish(n, [slice(lo, lo + width) for lo in range(0, S2, width)])
+            finish(n, [slice(lo, lo + JH) for lo in range(0, S2, JH)])

@@ -29,6 +29,7 @@ JQ = 128
 JH = S2 // 2
 NH = N // 2
 ROWS_AT = P - KG * BLOCKS
+PLANE = (12, 4)
 ALIGN = 256
 PAGE = 4096
 LINE = 4
@@ -73,8 +74,7 @@ def tile_list_residue_pocket_gate_kernel(
 
         nc.vector.memset(v2_rows[0:ROWS_AT, :], 0)
         nc.vector.memset(v_rows[0:ROWS_AT, :], 0)
-        for a in range(KG):
-            nc.gpsimd.memset(scales[a][:], 0)
+        nc.gpsimd.memset(scales[1][:], 0)
 
         nc.sync.dma_start(v2_rows[ROWS_AT:P, :], tab2_scales.rearrange("a q t -> (a q) t").bitcast(I32))
         nc.sync.dma_start(idx2[:], offs2)
@@ -89,8 +89,8 @@ def tile_list_residue_pocket_gate_kernel(
 
         v_picked = shared.tile([P, S], U8, name="v_picked", align_bytes=ALIGN, offset=V_PICKED_SCALES_AT)
         v2_picked = keep.tile([P, S2], U8, name="v2_picked", tag="v2_picked", align_bytes=ALIGN)
-        staged = keep.tile([P, S + S2], U8, name="staged", align_bytes=PAGE // 2)
-        staged32 = staged[:].bitcast(I32)
+        staged32 = scales[0][:]
+        staged = staged32.bitcast(U8)
         nc.vector.tensor_copy(v2_picked[:], v2_rows[:].bitcast(U8).indirect(idx2[:]))
         nc.vector.tensor_copy(v_picked[:], v_rows[:].bitcast(U8).indirect(idx[:]))
         nc.vector.tensor_copy(staged32[:, S // 4 : (S + S2) // 4], v2_picked[:].bitcast(I32))
@@ -108,15 +108,14 @@ def tile_list_residue_pocket_gate_kernel(
         for t in range(PACK):
             nc.tensor.transpose(rw_bank[:, t, :], rw_rows[:, t:GROUP:PACK], identity[:])
 
-        def move_scales(a):
-            first = ROWS_AT + BLOCKS * a
-            for r in range(4):
-                nc.sync.dma_start(scales[a][4 * a + r : P : QUAD, :], staged32[first + r : first + BLOCKS : 4, :])
-
-        move_scales(0)
+        for q in range(P // QUAD - 1):
+            rows = staged32[ROWS_AT + 4 * q : ROWS_AT + 4 * q + 4, :]
+            nc.sync.dma_start(staged32[QUAD * q + PLANE[0] : QUAD * q + PLANE[0] + 4, :], rows)
         for a in range(KG):
             load_words(v2_words[a], tab2_words[a])
-        move_scales(1)
+        for r in range(4):
+            rows = staged32[ROWS_AT + BLOCKS + r : P : 4, :]
+            nc.sync.dma_start(scales[1][PLANE[1] + r : P : QUAD, :], rows)
 
         v_codes = [keep.tile([P, S], U32, name=f"v_codes{a}", tag=f"v_codes{a}", align_bytes=ALIGN) for a in range(KG)]
         v2_codes = {
@@ -186,9 +185,9 @@ def tile_list_residue_pocket_gate_kernel(
                 nc.tensor.matmul_mx(
                     out=score_bank[step][:, t, :],
                     lhsT=v_codes[a][:, column : column + P].bitcast(FP8X4),
-                    lhsT_scale=scale_bytes[4 * a : P, column : column + P],
+                    lhsT_scale=scale_bytes[PLANE[a] : P, column : column + P],
                     rhs=site_codes(a, c).bitcast(FP8X4),
-                    rhs_scale=scale_bytes[4 * a : P, S + c * JQ : S + (c + 1) * JQ],
+                    rhs_scale=scale_bytes[PLANE[a] : P, S + c * JQ : S + (c + 1) * JQ],
                     start=(a == first and t == 0),
                     stop=(a != first and t == PACK - 1),
                 )
@@ -294,7 +293,7 @@ def tile_list_residue_pocket_gate_kernel(
                 nc.vector.scalar_tensor_tensor(
                     result[:, part], tanh_g[:, part], 1.0, view(feat, n, part.start, part.stop), ALU.add, ALU.mult
                 )
-            for part in parts if n == N // P - 1 else [slice(0, S2)]:
+            for part in parts if n >= NH // P else [slice(0, S2)]:
                 nc.sync.dma_start(out[n * P : (n + 1) * P, part], result[:, part])
 
         cast_wg(nc.vector.tensor_copy, 0, 0, 0, P)

@@ -74,7 +74,9 @@ def tile_list_residue_pocket_gate_kernel(
 
         nc.vector.memset(v2_rows[0:ROWS_AT, :], 0)
         nc.vector.memset(v_rows[0:ROWS_AT, :], 0)
-        nc.gpsimd.memset(scales[1][:], 0)
+        nc.vector.memset(scales[1][:], 0)
+        rw_rows = keep.tile([P, GROUP], F32, name="rw_rows", align_bytes=PAGE // 2)
+        nc.vector.memset(rw_rows[:], 0.0)
 
         nc.sync.dma_start(v2_rows[ROWS_AT:P, :], tab2_scales.rearrange("a q t -> (a q) t").bitcast(I32))
         nc.sync.dma_start(idx2[:], offs2)
@@ -99,9 +101,7 @@ def tile_list_residue_pocket_gate_kernel(
             v_picked[:].rearrange("p (b m t) -> p b t m", b=IG, t=PACK),
         )
 
-        rw_rows = keep.tile([P, GROUP], F32, name="rw_rows", tag="v2_rows", align_bytes=PAGE // 2)
-        identity = keep.tile([P, P], F32, name="identity", tag="v2_picked", align_bytes=ALIGN)
-        nc.gpsimd.memset(rw_rows[:], 0.0)
+        identity = keep.tile([P, P], F32, name="identity", align_bytes=ALIGN)
         make_identity(nc, identity[:])
         nc.sync.dma_start(rw_rows[0:IG, :], rw.rearrange("(b i) -> b i", b=IG))
         rw_bank = psum.tile([P, PACK, P], F32, name="rw_bank", tag=f"bank{RW_BANK}")

@@ -108,14 +108,16 @@ def tile_list_residue_pocket_gate_kernel(
         for t in range(PACK):
             nc.tensor.transpose(rw_bank[:, t, :], rw_rows[:, t:GROUP:PACK], identity[:])
 
-        for q in range(P // QUAD - 1):
-            rows = staged32[ROWS_AT + 4 * q : ROWS_AT + 4 * q + 4, :]
-            nc.sync.dma_start(staged32[QUAD * q + PLANE[0] : QUAD * q + PLANE[0] + 4, :], rows)
+        def move_scales(a, quadrants):
+            for q in quadrants:
+                first = ROWS_AT + BLOCKS * a + 4 * q
+                place = QUAD * q + PLANE[a]
+                nc.sync.dma_start(scales[a][place : place + 4, :], staged32[first : first + 4, :])
+
+        move_scales(0, (0, 2, 1))
         for a in range(KG):
             load_words(v2_words[a], tab2_words[a])
-        for r in range(4):
-            rows = staged32[ROWS_AT + BLOCKS + r : P : 4, :]
-            nc.sync.dma_start(scales[1][PLANE[1] + r : P : QUAD, :], rows)
+        move_scales(1, (0, 2, 1, 3))
 
         v_codes = [keep.tile([P, S], U32, name=f"v_codes{a}", tag=f"v_codes{a}", align_bytes=ALIGN) for a in range(KG)]
         v2_codes = {

from contextlib import ExitStack

import concourse.mybir as mybir
from concourse.masks import make_identity

K, T, S, T2, S2, N = 1024, 4096, 1024, 2048, 512, 512
FLOPS = 2 * K * S * S2 + 4 * S * N * S2

F32 = mybir.dt.float32
BF16 = mybir.dt.bfloat16
I32 = mybir.dt.int32
U32 = mybir.dt.uint32
U16 = mybir.dt.uint16
U8 = mybir.dt.uint8
FP8X4 = mybir.dt.float8_e4m3fn_x4
FP4X4 = mybir.dt.float4_e2m1fn_x4
ACT = mybir.ActivationFunctionType
ALU = mybir.AluOpType

P = 128
PACK = 4
GROUP = P * PACK
KG = K // GROUP
IG = S // GROUP
BLOCKS = 16
QUAD = 32
LIST = 16
JQ = 128
JH = S2 // 2
NH = N // 2
ROWS_AT = P - KG * BLOCKS
PLANE = (12, 4)
ALIGN = 256
PAGE = 4096
LINE = 4
SCORE_BANKS = 7
RW_BANK = 7
GATE_BANK = (1, 5, 0, RW_BANK)
FEAT_BANK = (2, 6, 3, 4)
EARLY = 3
V2_PIECES = [((0, JH), (JH, S2)), ((0, JQ), (JQ, JH), (JH, S2))]

WG_BYTES = 4 * PACK * NH
WV_WORDS_AT = 3 * WG_BYTES
WV_SCALES_AT = WV_WORDS_AT + IG * 2 * N
WG_AT = {(1, 0): 0, (0, 1): WG_BYTES, (0, 0): 2 * WG_BYTES, (1, 1): WV_SCALES_AT + IG * N}
V2_WORDS_AT = [4 * T + PAGE + a * 4 * T2 for a in range(KG)]
V_PICKED_SCALES_AT = V2_WORDS_AT[1] - S // 2
V1_WORDS_AT = V2_WORDS_AT[1] + 4 * T2


def tile_list_residue_pocket_gate_kernel(
    tc, tab_words, tab_scales, offs, tab2_words, tab2_scales, offs2, rw, wv_words, wv_scales, wg, bg, out
):
    nc = tc.nc
    with ExitStack() as ctx:
        keep = ctx.enter_context(tc.tile_pool(name="keep", bufs=1))
        ring = ctx.enter_context(tc.tile_pool(name="ring", bufs=N // P))
        psum = ctx.enter_context(tc.psum_pool(name="psum", bufs=1))
        shared = ctx.enter_context(tc.tile_pool(name="shared", bufs=1))

        idx = keep.tile([P, S // LIST], U16, name="idx", align_bytes=ALIGN)
        idx2 = keep.tile([P, S2 // LIST], U16, name="idx2", align_bytes=ALIGN)
        v_rows = keep.tile([P, T // 4], I32, name="v_rows", align_bytes=PAGE)
        v2_rows = keep.tile([P, T2 // 4], I32, name="v2_rows", tag="v2_rows", align_bytes=PAGE // 2)
        scales = [keep.tile([P, (S + S2) // 4], I32, name=f"scales{a}", align_bytes=PAGE // 2) for a in range(KG)]
        v_words = [
            shared.tile([P, T], I32, name="v_words0", align_bytes=PAGE, offset=0),
            shared.tile([P, T], I32, name="v_words1", align_bytes=PAGE, offset=V1_WORDS_AT),
        ]
        v2_words = [
            shared.tile([P, T2], I32, name=f"v2_words{a}", align_bytes=ALIGN, offset=V2_WORDS_AT[a]) for a in range(KG)
        ]

        nc.vector.memset(v2_rows[0:ROWS_AT, :], 0)
        nc.vector.memset(v_rows[0:ROWS_AT, :], 0)
        nc.vector.memset(scales[1][:], 0)
        rw_rows = keep.tile([P, GROUP], F32, name="rw_rows", align_bytes=PAGE // 2)
        nc.vector.memset(rw_rows[:], 0.0)

        nc.sync.dma_start(v2_rows[ROWS_AT:P, :], tab2_scales.rearrange("a q t -> (a q) t").bitcast(I32))
        nc.sync.dma_start(idx2[:], offs2)
        nc.sync.dma_start(v_rows[ROWS_AT:P, :], tab_scales.rearrange("a q t -> (a q) t").bitcast(I32))
        nc.sync.dma_start(idx[:], offs)

        def load_words(tile, source):
            nc.sync.dma_start(tile[:], source.rearrange("p n t -> p (n t)").bitcast(I32))

        load_words(v_words[0], tab_words[0])
        load_words(v_words[1], tab_words[1])

        v_picked = shared.tile([P, S], U8, name="v_picked", align_bytes=ALIGN, offset=V_PICKED_SCALES_AT)
        v2_picked = keep.tile([P, S2], U8, name="v2_picked", tag="v2_picked", align_bytes=ALIGN)
        staged32 = scales[0][:]
        staged = staged32.bitcast(U8)
        nc.vector.tensor_copy(v2_picked[:], v2_rows[:].bitcast(U8).indirect(idx2[:]))
        nc.vector.tensor_copy(v_picked[:], v_rows[:].bitcast(U8).indirect(idx[:]))
        nc.vector.tensor_copy(staged32[:, S // 4 : (S + S2) // 4], v2_picked[:].bitcast(I32))
        nc.vector.tensor_copy(
            staged[:, 0:S].rearrange("p (b t m) -> p b t m", b=IG, t=PACK),
            v_picked[:].rearrange("p (b m t) -> p b t m", b=IG, t=PACK),
        )

        identity = keep.tile([P, P], F32, name="identity", align_bytes=ALIGN)
        make_identity(nc, identity[:])
        nc.sync.dma_start(rw_rows[0:IG, :], rw.rearrange("(b i) -> b i", b=IG))
        rw_bank = psum.tile([P, PACK, P], F32, name="rw_bank", tag=f"bank{RW_BANK}")
        for t in range(PACK):
            nc.tensor.transpose(rw_bank[:, t, :], rw_rows[:, t:GROUP:PACK], identity[:])

        def move_scales(a, quadrants):
            for q in quadrants:
                first = ROWS_AT + BLOCKS * a + 4 * q
                place = QUAD * q + PLANE[a]
                nc.sync.dma_start(scales[a][place : place + 4, :], staged32[first : first + 4, :])

        move_scales(0, (0, 2, 1))
        for a in range(KG):
            load_words(v2_words[a], tab2_words[a])
        move_scales(1, (0, 2, 1, 3))

        v_codes = [keep.tile([P, S], U32, name=f"v_codes{a}", tag=f"v_codes{a}", align_bytes=ALIGN) for a in range(KG)]
        v2_codes = {
            (a, lo): keep.tile([P, hi - lo], U32, name=f"v2_codes{a}_{lo}", tag=f"v2_codes{a}_{lo}", align_bytes=ALIGN)
            for a in range(KG)
            for lo, hi in V2_PIECES[a]
        }

        def gather_v(a):
            nc.vector.tensor_copy(
                v_codes[a][:].rearrange("p (b t m) -> p b m t", b=IG, t=PACK),
                v_words[a][:].bitcast(U32).indirect(idx[:]),
            )

        def gather_v2(a, lo, hi):
            window = v2_words[a][:].bitcast(U32)
            nc.vector.tensor_copy(v2_codes[a, lo][:], window.indirect(idx2[:, lo // LIST : hi // LIST]))

        def site_codes(a, c):
            lo = max(lo for lo, hi in V2_PIECES[a] if lo <= c * JQ)
            return v2_codes[a, lo][:, c * JQ - lo : (c + 1) * JQ - lo]

        gather_v(0)

        wg_raw = {
            (b, u): shared.tile([P, PACK, NH], F32, name=f"wg_raw{b}{u}", align_bytes=ALIGN, offset=place)
            for (b, u), place in WG_AT.items()
        }
        wv_codes = shared.tile([P, IG, 2 * N], U8, name="wv_codes", align_bytes=ALIGN, offset=WV_WORDS_AT)
        wv_rows = shared.tile([P, IG, N // 4], I32, name="wv_rows", align_bytes=ALIGN, offset=WV_SCALES_AT)
        bg_raw = shared.tile([P, N // P], F32, name="bg_raw", align_bytes=ALIGN, offset=V1_WORDS_AT)

        def load_wg(b, u):
            rows = wg[b * GROUP : (b + 1) * GROUP, u * NH : (u + 1) * NH]
            nc.sync.dma_start(wg_raw[b, u][:], rows.rearrange("(p t) n -> p t n", t=PACK))

        nc.vector.memset(wv_rows[:], 0)
        load_wg(0, 0)
        load_wg(1, 0)
        nc.sync.dma_start(wv_codes[:].bitcast(I32), wv_words.rearrange("b p n -> p b n").bitcast(I32))
        for r in range(4):
            rows = wv_scales[:, r:BLOCKS:4, :].rearrange("b q n -> q b n")
            nc.sync.dma_start(wv_rows[r:P:QUAD, :, :], rows.bitcast(I32))
        load_wg(0, 1)
        load_wg(1, 1)
        with nc.allow_non_contiguous_dma(reason="the bias lies one value a partition"):
            nc.sync.dma_start(bg_raw[:], bg.rearrange("(c p) -> p c", p=P))
        bg_half = shared.tile([P, N // P], F32, name="bg_half", align_bytes=ALIGN, offset=WG_AT[1, 1])

        gather_v(1)
        for a in range(KG):
            for lo, hi in V2_PIECES[a]:
                gather_v2(a, lo, hi)

        order = [(b, c) for b in range(IG) for c in range(S2 // JQ)]
        score_bank = {}

        def score(step, a):
            b, c = order[step]
            first = 1 if EARLY <= step else 0
            if a == first:
                bank = f"bank{step % SCORE_BANKS}"
                score_bank[step] = psum.tile([P, PACK, JQ], F32, name=f"score{step}", tag=bank)
            scale_bytes = scales[a][:].bitcast(U8)
            for t in range(PACK):
                column = b * GROUP + t * P
                nc.tensor.matmul_mx(
                    out=score_bank[step][:, t, :],
                    lhsT=v_codes[a][:, column : column + P].bitcast(FP8X4),
                    lhsT_scale=scale_bytes[PLANE[a] : P, column : column + P],
                    rhs=site_codes(a, c).bitcast(FP8X4),
                    rhs_scale=scale_bytes[PLANE[a] : P, S + c * JQ : S + (c + 1) * JQ],
                    start=(a == first and t == 0),
                    stop=(a != first and t == PACK - 1),
                )

        for a in range(KG):
            for step in range(EARLY):
                score(step, a)
        for step in range(EARLY, SCORE_BANKS):
            for a in reversed(range(KG)):
                score(step, a)

        h_bf16 = {
            (b, h): keep.tile([P, JH, PACK], BF16, name=f"h_bf16{b}{h}", tag=f"h_bf16{b}{h}", align_bytes=ALIGN)
            for b in range(IG)
            for h in range(2)
        }
        h_codes = {1: keep.tile([P, S2], U32, name="h_codes1", align_bytes=ALIGN)}
        h_scales = [keep.tile([P, S2], U8, name=f"h_scales{b}", align_bytes=ALIGN) for b in range(IG)]
        slots = {(0, 0): "wg_bf16", (0, 1): "v_codes1", (1, 1): f"v2_codes1_{JH}"}
        wg_bf16 = {
            (b, u): keep.tile([P, NH, PACK], BF16, name=f"wg_bf16{b}{u}", tag=slot, align_bytes=ALIGN)
            for (b, u), slot in slots.items()
        }
        wg_codes = {}
        wg_scales = [keep.tile([P, N], U8, name=f"wg_scales{b}", align_bytes=ALIGN) for b in range(IG)]

        def bound(step):
            b, c = order[step]
            tanh_a = keep.tile([P, JQ, PACK], F32, name=f"tanh_a{step}", tag=f"tanh_a{step}", align_bytes=ALIGN)
            nc.scalar.activation(tanh_a[:], score_bank[step][:].rearrange("p t j -> p j t"), ACT.Tanh)
            nc.vector.scalar_tensor_tensor(
                h_bf16[b, c // 2][:, (c % 2) * JQ : (c % 2 + 1) * JQ, :],
                tanh_a[:],
                0.5,
                rw_bank[:, :, b].unsqueeze(1).to_broadcast([P, JQ, PACK]),
                ALU.mult,
                ALU.mult,
            )

        def quantize(codes, scale_bytes, values):
            nc.vector.quantize_mx(out=codes.bitcast(FP8X4), scales=scale_bytes, in_=values.rearrange("p n t -> p (n t)"))

        def quantize_h(b, lo, hi):
            sites = slice(lo, hi)
            quantize(h_codes[b][:, sites], h_scales[b][:, sites], h_bf16[b, lo // JH][:])

        def quantize_wg(b, u, lo, hi):
            features = slice(u * NH + lo, u * NH + hi)
            quantize(wg_codes[b][:, features], wg_scales[b][:, features], wg_bf16[b, u][:, lo:hi, :])

        def cast_wg(copy, b, u, lo, hi):
            values = wg_bf16[b, u][:, lo:hi, :].rearrange("p (c i) t -> p c t i", i=LINE)
            copy(values, wg_raw[b, u][:, :, lo:hi].rearrange("p t (c i) -> p c t i", i=LINE))

        wv_scale_bytes = wv_rows[:].bitcast(U8)
        feat = {}
        gate = {}

        def place(n, site):
            if n < NH // P:
                return site // JH, n * JH + site % JH
            return n, site

        def view(banks, n, lo, hi):
            key, column = place(n, lo)
            return banks[key][:, column : column + hi - lo]

        def feat_pass(b, n, lo, hi):
            key = place(n, lo)[0]
            if key not in feat:
                feat[key] = psum.tile([P, S2], F32, name=f"feat{key}", tag=f"bank{FEAT_BANK[key]}")
            nc.tensor.matmul_mx(
                out=view(feat, n, lo, hi),
                lhsT=wv_codes[:, b, 2 * P * n : 2 * P * (n + 1)].bitcast(FP4X4),
                lhsT_scale=wv_scale_bytes[:, b, P * n : P * (n + 1)],
                rhs=h_codes[b][:, lo:hi].bitcast(FP8X4),
                rhs_scale=h_scales[b][:, lo:hi],
                start=(b == 0 and place(n, lo)[1] == 0),
                stop=(b == IG - 1 and place(n, hi - 1)[1] == S2 - 1),
            )

        def gate_pass(b, n, lo, hi):
            key = place(n, lo)[0]
            if key not in gate:
                gate[key] = psum.tile([P, S2], F32, name=f"gate{key}", tag=f"bank{GATE_BANK[key]}")
            nc.tensor.matmul_mx(
                out=view(gate, n, lo, hi),
                lhsT=wg_codes[b][:, P * n : P * (n + 1)].bitcast(FP8X4),
                lhsT_scale=wg_scales[b][:, P * n : P * (n + 1)],
                rhs=h_codes[b][:, lo:hi].bitcast(FP8X4),
                rhs_scale=h_scales[b][:, lo:hi],
                start=(b == 0 and place(n, lo)[1] == 0),
                stop=(b == IG - 1 and place(n, hi - 1)[1] == S2 - 1),
            )

        def finish(n, parts):
            tanh_g = ring.tile([P, S2], F32, name="tanh_g", align_bytes=ALIGN)
            result = ring.tile([P, S2], F32, name="result", align_bytes=PAGE // 2)
            for part in parts:
                logits = view(gate, n, part.start, part.stop)
                nc.scalar.activation(tanh_g[:, part], logits, ACT.Tanh, bias=bg_half[:, n : n + 1])
            for part in parts:
                nc.vector.scalar_tensor_tensor(
                    result[:, part], tanh_g[:, part], 1.0, view(feat, n, part.start, part.stop), ALU.add, ALU.mult
                )
            for part in parts if n >= NH // P else [slice(0, S2)]:
                nc.sync.dma_start(out[n * P : (n + 1) * P, part], result[:, part])

        cast_wg(nc.vector.tensor_copy, 0, 0, 0, P)
        cast_wg(nc.vector.tensor_copy, 0, 0, P, NH)
        wg_codes[0] = keep.tile([P, N], U32, name="wg_codes0", align_bytes=ALIGN)
        quantize_wg(0, 0, 0, P)
        quantize_wg(0, 0, P, NH)

        for step in range(len(order)):
            bound(step)
            if step == 0:
                wg_bf16[1, 0] = keep.tile([P, NH, PACK], BF16, name="wg_bf1610", tag="wg_bf16", align_bytes=ALIGN)
                raw = wg_raw[1, 0][:].rearrange("p t n -> p n t")
                nc.gpsimd.tensor_scalar(wg_bf16[1, 0][:], raw, 1.0, 0.0, ALU.mult, ALU.add)
                for a in reversed(range(KG)):
                    score(SCORE_BANKS, a)
            if order[step] == (0, 2):
                h_codes[0] = keep.tile([P, S2], U32, name="h_codes0", tag=f"tanh_a{step}", align_bytes=ALIGN)
                quantize_h(0, 0, JH)
            if order[step] == (1, 0):
                quantize_h(0, JH, S2)
            if order[step] == (1, 2):
                quantize_h(1, 0, JH)

        cast_wg(nc.scalar.copy, 0, 1, 0, NH)
        cast_wg(nc.scalar.copy, 1, 1, 0, P)
        cast_wg(nc.scalar.copy, 1, 1, P, NH)
        nc.scalar.mul(bg_half[:], bg_raw[:], 0.5)
        wg_codes[1] = keep.tile([P, N], U32, name="wg_codes1", tag="h_bf1610", align_bytes=ALIGN)
        quantize_wg(1, 0, 0, NH)
        quantize_h(1, JH, S2)
        quantize_wg(0, 1, 0, NH)
        quantize_wg(1, 1, 0, P)
        quantize_wg(1, 1, P, NH)

        early_gates = range(NH // P)
        for half in range(0, S2, JH):
            for n in early_gates:
                gate_pass(0, n, half, half + JH)
            for n in range(N // P):
                feat_pass(0, n, half, half + JH)
        for n in range(N // P):
            feat_pass(1, n, 0, JH)
        for half in range(0, S2, JH):
            for n in early_gates:
                gate_pass(1, n, half, half + JH)
        for n in range(N // P):
            if n not in early_gates:
                for b in range(IG):
                    gate_pass(b, n, 0, S2)
            feat_pass(1, n, JH, S2)

        for n in range(N // P):
            finish(n, [slice(lo, lo + JH) for lo in range(0, S2, JH)])
